import numpy as np, ml_dtypes
CORES = [3,11,19,27,35,43,51,59]
N = 8
BF = ml_dtypes.bfloat16
NB, T0, P, Q, RO, CM = 3072, 1280, 192, 4, 3, 3456
H = 3 * P // 2
def tally(fork):
    far = np.arange(P) % Q < Q - 1
    return np.add.reduce(np.where(fork, np.where(far, 1, 1 - Q), 0), axis=(1, 2))
def lanes(lv):
    T = lv.shape[2]; o = (np.arange(T) + T - H) % T
    return o[np.argsort(1 - lv[:, :, o], axis=2, kind="stable")[:, :, :P]]
def at(a, ix):
    return np.take_along_axis(a, ix[:, :, None, :], 3)
def play(x, rg, lv, z, w, kap, th, cap, rounds):
    x, rg, lv, z, w, kap, th, cap = [np.asarray(a).astype(np.int32) for a in (x, rg, lv, z, w, kap, th, cap)]
    bal = np.zeros(N, np.int64); far = np.arange(P) % Q < Q - 1; best = None
    for t in range(rounds):
        T = T0 + P * t
        ring = at(rg, lanes(lv))
        xl = at(x, ring.transpose(0, 1, 3, 2).reshape(N, 8, P * 16)).reshape(N, 8, 16, P, 16)
        k = np.argmax(np.add.reduce(np.minimum(xl, z[..., None]), axis=2), axis=3)
        y0 = np.abs(np.take_along_axis(xl, k[:, :, None, :, None], 4)[..., 0] - z)
        y = np.array(y0)
        for c in range(Q - 1): y[..., c::Q] = np.roll(y0[..., c::Q], 1 + (t + c) % (N - 1), axis=0)
        u = np.add.reduce(w[..., None] * y, axis=2) & 4095
        h = ((u * u >> 5)[..., None] + kap[:, :, None, :] * u[..., None]) & 4095
        tau = h * T >> 12; age = h & 15
        b = np.take_along_axis(rg.reshape(N, 8, 16 * T), (age * T + tau).reshape(N, 8, P * 16), 2)
        xb = at(x, b).reshape(N, 8, 16, P, 16)
        far_off = np.add.reduce(np.abs(xb - y[..., None]), axis=2)
        m = np.argmin(far_off, axis=3)[..., None]
        best = np.take_along_axis(far_off, m, 3)[..., 0]; fork = best < th[:, :, None]
        tm = np.take_along_axis(tau, m, 3)[..., 0]; am = np.take_along_axis(age, m, 3)[..., 0]
        xm = np.take_along_axis(xb, m[:, :, None, :, :], 4)[..., 0]
        tail = np.take_along_axis(at(rg, tm), np.minimum(am[:, :, None, :] + np.arange(15)[:, None], 15), 2)
        tail = np.where(fork[:, :, None], tail, ring[:, :, :15])
        new = np.broadcast_to((NB + P * t + np.arange(P)).astype(np.int32), (N, 8, 1, P))
        xn = np.where(fork[:, :, None], (xm + y) >> 1, y)
        bal = bal + tally(fork)
        off = fork & np.where(far, bal[:, None, None] > cap[:, :, None], -bal[:, None, None] > cap[:, :, None])
        x = np.concatenate([x, xn.astype(np.int32)], axis=3); rg = np.concatenate([rg, np.concatenate([new, tail], axis=2).astype(np.int32)], axis=3)
        lv = np.concatenate([lv, np.where(off, 0, 1).astype(np.int32)], axis=2)
    return x, rg, lv, best, bal
def parts(rng):
    x = (rng.integers(24, 65, (N, 8, 1, NB)) * rng.random((N, 8, 16, NB))).astype(np.int64)
    rg = rng.integers(0, NB, (N, 8, 16, T0))
    lv = (np.argsort(rng.random((N, 8, T0)), axis=2) < rng.integers(T0 // 2, T0, (N, 8, 1))).astype(np.int64)
    z = (rng.permutation(np.linspace(16, 64, N))[:, None, None, None] * rng.random((N, 8, 16, P))).astype(np.int64)
    return x, rg, lv, z, rng.integers(0, 4096, (N, 8, 16)), rng.integers(0, 2048, (N, 8, 16))
def tune(rng, x, rg, lv, z, w, kap):
    one = np.ones((N, 8), np.int64); best = play(x, rg, lv, z, w, kap, one, one, 1)[3]
    th = np.take_along_axis(np.sort(best, axis=2), rng.integers(P // 4, 3 * P // 4, (N, 8, 1)), 2)[:, :, 0] + rng.integers(0, 2, (N, 8))
    return np.clip(th, 1, 1008), best
def caps(rng, th, best):
    return np.minimum((1.5 * (np.abs(tally(best < th[:, :, None]))[:, None] + 8) * rng.random((N, 8))).astype(np.int64), CM)
def close(th, best):
    b = np.abs(tally(best < th[:, :, None]))[:, None]; d = np.array([0, -1, 1, 0, -1, -CM, CM, -1])
    return np.clip(b + d[(np.arange(8)[None, :] + 3 * np.arange(N)[:, None]) % 8], 0, CM)
def pack(x, rg, lv, z, w, kap, th, cap):
    i = lambda a, s: np.ascontiguousarray(np.reshape(a, s)).astype(np.int32)
    return {"x0": np.reshape(x, (N, 128, NB)).astype(np.float32).astype(BF), "rings": i(rg, (N, 128, T0)), "live": i(lv, (N, 8, T0)), "z": np.reshape(z, (N, 128, P)).astype(np.float32).astype(BF),
            "w": i(w, (N, 128, 1)), "kap": i(kap, (N, 128, 1)), "th": i(th, (N, 8, 1)), "cap": i(cap, (N, 8, 1))}
def setup_inputs(rng):
    p = parts(rng); th, best = tune(rng, *p)
    return pack(*p, th, caps(rng, th, best))
def setup_inputs_spread(rng):
    x = (np.exp2(6 * rng.random((N, 8, 1, NB))) * rng.random((N, 8, 16, NB))).astype(np.int64)
    z = (np.exp2(6 * rng.random((N, 8, 1, P))) * rng.random((N, 8, 16, P))).astype(np.int64)
    rg = (NB * rng.random((N, 8, 16, T0)) ** rng.integers(1, 5, (N, 8, 1, 1))).astype(np.int64); rg = np.minimum(rg, NB - 1)
    lv = (np.argsort(rng.random((N, 8, T0)), axis=2) < (P * np.exp2(1.3 * rng.random((N, 8, 1)))).astype(np.int64)).astype(np.int64)
    w = np.exp2(12 * rng.random((N, 8, 16))).astype(np.int64); kap = np.exp2(11 * rng.random((N, 8, 16))).astype(np.int64)
    w = np.minimum(w, 4095); kap = np.minimum(kap, 2047); th, best = tune(rng, x, rg, lv, z, w, kap)
    return pack(x, rg, lv, z, w, kap, th, caps(rng, th, best))
def setup_inputs_ends(rng):
    hi = rng.integers(0, 2, (N, 8)); hi[:, 0] = 0; hi[:, 7] = 1; up = rng.permutation(N) % 2 == 0; o = rng.permutation(8); far = np.arange(P) % Q < Q - 1
    x = 63 * rng.integers(0, 2, (N, 8, 16, NB)); x[..., 0] = 63 * (1 - hi)[..., None]; x[..., NB - 1] = 63 * hi[..., None]
    one = (NB - 1) * hi; nil = NB - 1 - one
    rg = np.where(rng.random((N, 8, 16, T0)) < 0.5, one[:, :, None, None], nil[:, :, None, None]); rg[:, :, 0] = one[:, :, None]
    rg[:, :, 0, 0] = np.where(up[:, None], one, nil); rg[:, :, 1, 0] = one
    lv = rng.integers(0, 2, (N, 8, T0)); lv[:, :, T0 - H:] = 1
    z = np.array(np.broadcast_to(np.where(far, 0, 63), (N, 8, 16, P)))
    kap = 2047 * rng.integers(0, 2, (N, 8, 16)); w = 4095 * rng.integers(0, 2, (N, 8, 16)); cap = np.full((N, 8), CM)
    th = np.where(rng.integers(0, 2, (N, 8)) == 0, 1, 1008); th[:, o[0]] = 1; th[:, o[1]] = 1008
    for g in o[5:]:
        r = 63 * rng.integers(0, 2, (N, 16, P)); r[:, 1] = 63 - r[:, 0]
        z[:, g] = np.where(far, r, 63); th[:, g] = np.where(up, 1008, 1); cap[:, g] = 0
    good = []
    for n in range(1, 17):
        u = (4095 * 63 * n) & 4095; hs = [((u * u >> 5) + c * u) & 4095 for c in (0, 2047)]
        if all((h & 15) > 0 and (h * T0 >> 12) > 0 and (h * (T0 + P * (RO - 1)) >> 12) < T0 for h in hs): good.append((n, hs))
    for q in range(N):
        for g in o[:5]:
            n, hs = good[0] if g == o[0] else good[int(rng.integers(0, len(good)))]
            w[q, g] = 4095 * (rng.permutation(16) < n)
            for t in range(RO):
                for h in hs: rg[q, g, h & 15, h * (T0 + P * t) >> 12] = one[q, g] if up[q] else nil[q, g]
    return pack(x, rg, lv, z, w, kap, th, cap)
def setup_inputs_corners(rng):
    x, rg, lv, z, w, kap = parts(rng); v = np.arange(T0)
    for q in range(N):
        for g in range(8):
            lv[q, g] = (v < P, v >= T0 - P, v >= 0, (v < P - 1) | (v == T0 - 1), rng.permutation(T0) < P, (v >= T0 - H - P) & (v < T0 - H), rng.permutation(T0) < 2 * P, v != T0 - H)[(g + q) % 8]
    rg[:, 0] = np.where(rng.random((N, 16, T0)) < 0.5, 0, NB - 1); rg[:, 1] = rg[:, 1, :1]; rg[:, 2] = rng.integers(NB - 16, NB, (N, 16, T0))
    x[:, 3, :, 1::2] = x[:, 3, :, ::2]; x[:, 4, :, ::3] = 0; x[:, 4, :, 1::3] = 63
    w[:, 5:7] = 0; x[:, 5:7, 0] = 63
    w[:, 5, 0] = 65; z[:, 5, 0] = rng.choice(np.array([0, 62, 63]), (N, P)); kap[:, 5, 15] = 2047
    w[:, 6, 0] = 1; z[:, 6, 0] = rng.choice(np.array([60, 61, 63]), (N, P)); kap[:, 6] = np.where(rng.random((N, 16)) < 0.5, 1365, kap[:, 6])
    w[:, 7] = 4095; kap[:, 7] = 2047 * rng.integers(0, 2, (N, 16))
    th, best = tune(rng, x, rg, lv, z, w, kap); m = rng.integers(0, 5, (N, 8)); th = np.where(m == 0, 1, np.where(m == 1, 1008, th))
    return pack(x, rg, lv, z, w, kap, th, close(th, best))
def setup_inputs_crowd(rng):
    x, rg, lv, z, w, kap = parts(rng); lv[:, ::2] = 1
    for g in (0, 1, 4, 5): rg[:, g] = rg[:, g, :, :1]; z[:, g] = z[:, g, :, :1]
    z[:, 1, :, 0] = 63 - z[:, 1, :, 0]; z[:, 5, :, P - 1] = 63 - z[:, 5, :, P - 1]
    w[:, 2:4] = 0; w[:, 3, 7] = 3; x[:, 3, 7] = 63; z[:, 3, 7] = 63; z[:, 3, 7, 1] = 0
    kap[:, 6] = kap[:, 6, :1]; kap[:, 7] = 0; rg[:, 7] = np.where(rng.random((N, 16, T0)) < 0.5, 0, NB - 1)
    w[:, 7] = 4095; x[:, 7, :, 0] = 63; x[:, 7, :, NB - 1] = 63; z[:, 7, :, ::5] = 0
    th, best = tune(rng, x, rg, lv, z, w, kap); th[:, 0] = np.max(best[:, 0], axis=1) + 1; th[:, 4] = np.min(best[:, 4], axis=1); th[:, 1] = np.max(best[:, 1], axis=1)
    th = np.clip(th, 1, 1008)
    return pack(x, rg, lv, z, w, kap, th, close(th, best))
def setup_inputs_balance(rng):
    x, rg, lv, z, w, kap = parts(rng); far = np.arange(P) % Q < Q - 1; own = np.flatnonzero(~far); own = own[own >= P // 2]
    o = rng.permutation(N); m = int(o[2]); j = int(np.flatnonzero(o == (m - 3) % N)[0]); o[j] = o[1]; o[1] = (m - 3) % N
    tall = np.isin(np.arange(N), np.concatenate([o[:1], o[3::2]]))
    up = np.repeat(tall[:, None], 8, axis=1); up[m] = rng.permutation(8) < 4
    k = int(rng.choice(np.flatnonzero(up[m]))); dn = np.flatnonzero(~up[m]); dn = np.concatenate([dn[dn == (k - 1) % 8], dn[dn != (k - 1) % 8]])
    one = rng.integers(0, NB, (N, 8)); nil = (one + 1) % NB; near = (one + 2) % NB; dim = (one + 3) % NB
    n = rng.integers(1, 4, N); n[o[:3]] = 0; n[o[3]] = 1
    th = np.where(rng.integers(0, 2, (N, 8)) == 0, 1, 1008); th[:, k] = np.where(tall, 1008, 1); th[o[1], k - 1] = 1008; th[o[1], dn[2]] = 1; th[m, dn[2]] = 1008
    d = np.array([0, -1, 1, 0, -1, 0, -1, CM])
    cap = np.clip((CM - (Q - 1) * n)[:, None] + d[(np.arange(8)[None, :] + 3 * np.arange(N)[:, None]) % 8], 0, CM)
    cap[m] = rng.choice(np.array([0, 1, 2, CM]), 8); cap[m, dn[:2]] = 0; cap[m, dn[2]] = 1; cap[m, k] = 0
    lv[:, :, T0 - H:] = 1; lv[:, :, 0] = 0; lv[m, dn[:2]] = np.arange(T0) >= T0 - P
    z = np.array(np.broadcast_to(np.where(far, 0, 63), (N, 8, 16, P)))
    a = rng.integers(1, 4096, (N, 8, 8)); w[..., ::2] = a; w[..., 1::2] = 4096 - a; w[..., 14:] = 0
    for q in range(N):
        c = rng.permutation(own)
        for g in range(8):
            x[q, g, :, one[q, g]] = 63; x[q, g, :, nil[q, g]] = 0; x[q, g, :, near[q, g]] = 63; x[q, g, 15, near[q, g]] = 62
            x[q, g, :, dim[q, g]] = 0; x[q, g, 15, dim[q, g]] = 1
            rg[q, g, 0] = one[q, g]; rg[q, g, 1, 0] = one[q, g]; rg[q, g, 0, 0] = one[q, g] if up[q, g] else nil[q, g]
            if not up[q, g] and th[q, g] == 1008: z[q, g, :, c[0]] = 0; z[q, g, 15, c[0]] = 1
        for v in c[1:1 + int(n[q])]: z[q, int(rng.integers(0, 8)), :, v] = 0
    s = (m - 1) % N; i = P // 2 + Q * int(rng.integers(0, P // 2 // Q))
    rg[s, k, 0, T0 - H + i] = near[s, k]
    s = (m - 5) % N; i = Q * int(rng.integers(0, P // 2 // Q))
    rg[s, dn[2], 0, T0 - P // 2 + i] = dim[s, dn[2]]
    return pack(x, rg, lv, z, w, kap, th, cap)
def check_inputs(d):
    bad = []
    for k, lo, hi in (("x0", 0, 63), ("rings", 0, NB - 1), ("live", 0, 1), ("z", 0, 63), ("w", 0, 4095), ("kap", 0, 2047), ("th", 1, 1008), ("cap", 0, CM)):
        a = np.asarray(d[k]).astype(np.float64)
        if not (np.min(a) >= lo and np.max(a) <= hi): bad.append("range of " + k)
        elif np.any(a != np.floor(a)): bad.append("whole numbers of " + k)
    if np.min(np.add.reduce(np.asarray(d["live"]).astype(np.int64), axis=2)) < P: bad.append("live timelines")
    return bad
def reference(x0, rings, live, z, w, kap, th, cap):
    x, rg, lv, best, bal = play(x0.astype(np.float32).reshape(N, 8, 16, NB), rings.reshape(N, 8, 16, T0), live.reshape(N, 8, T0), z.astype(np.float32).reshape(N, 8, 16, P),
                                w.reshape(N, 8, 16), kap.reshape(N, 8, 16), th.reshape(N, 8), cap.reshape(N, 8), RO)
    return {"yx": x[..., NB:].reshape(N, 128, P * RO).astype(np.float32).astype(BF), "yt": rg[..., T0:].reshape(N, 128, P * RO).astype(np.float32), "ya": lv[..., T0:].reshape(N, 8, P * RO).astype(np.float32)}

@@ -1,0 +1,788 @@
+import numpy as np
+from concourse.bass import DstId, RemoteDMATransfer
+from concourse.mybir import AluOpType as A, ActivationFunctionType as F, AxisListType
+
+N, NB, T0, P, RO = 8, 3072, 1280, 192, 3
+OFS = 1824
+PER = {1280: (1, 5), 1472: (4, 23), 1664: (2, 13)}
+
+
+def _sb(n, d):
+    return ("sbuf", [128, n], d)
+
+
+f32, bf, i32, u16, f16 = "float32", "bfloat16", "int32", "uint16", "float16"
+SCRATCH = {
+    "XW": _sb(3648, bf), "RI": _sb(1280, i32), "RG": _sb(1664, f16), "NL": _sb(4096, f32), "RT": _sb(4288, f32),
+    "XT0": _sb(4288, bf), "XT1": _sb(4288, bf), "TB0": _sb(256, u16), "TB1": _sb(256, u16),
+    "D2": _sb(3072, bf), "A2": _sb(3072, bf), "D5": _sb(3072, bf), "A5": _sb(3072, bf), "Z16": _sb(3072, bf),
+    "EM": _sb(6016, bf), "ID7": _sb(896, bf), "SH": _sb(2048, bf), "LVI": _sb(1280, i32), "LVB": _sb(1280, bf),
+    "ZN": _sb(192, bf), "ZI": _sb(192, bf), "WI": _sb(4, i32), "KI": _sb(4, i32), "TI": _sb(4, i32), "CI": _sb(4, i32),
+    "YR": _sb(2304, bf), "YS": _sb(576, bf), "YT": _sb(576, f32), "MK": _sb(48, f32),
+    "RR": _sb(192, u16), "RH": _sb(192, f16), "OFR": _sb(12, u16), "OY": _sb(12, u16), "HX": _sb(192, u16),
+    "IDX": _sb(12, u16), "OSC": _sb(80, u16), "LAU": _sb(12, u16), "EXO": _sb(12, u16), "OS": _sb(128, u16),
+    "WS2": _sb(144, bf), "WS5": _sb(144, bf), "WA": _sb(144, bf), "BO": _sb(128, bf), "TRI": _sb(128, bf), "UPP": _sb(128, bf),
+    "ONE": _sb(144, bf), "M3": _sb(128, bf), "WH": _sb(128, bf), "WL": _sb(128, bf), "REP": _sb(128, f32), "FW": _sb(32, bf),
+    "KA": _sb(96, bf), "KB": _sb(96, bf), "KH": _sb(96, bf), "KO": _sb(96, bf), "KX": _sb(96, f32), "M96": _sb(96, f32),
+    "DS": _sb(96, f32), "DL": _sb(96, f32), "col": _sb(32, f32), "ci": _sb(16, i32), "I144": _sb(144, f32),
+    "t1": _sb(128, f32), "t2": _sb(128, f32), "t3": _sb(128, f32), "t5": _sb(96, f32), "t6": _sb(96, f32),
+    "II": _sb(12, f32), "s1": _sb(12, f32), "s2": _sb(12, i32), "s3": _sb(12, f32),
+    "LAN": _sb(12, f32), "C6": _sb(12, f32), "K4": _sb(12, f32), "SG": _sb(12, f32), "DK": _sb(12, f32), "ST": _sb(12, f32),
+    "CS": _sb(4, f32), "NC": _sb(4, f32), "LJ": _sb(192, f32), "N0": _sb(192, f32), "NR": _sb(192, f32),
+    "SC": _sb(192, f32), "e1": _sb(12, i32), "e2": _sb(12, i32), "UL": _sb(192, f32), "u0": _sb(12, i32), "UD": _sb(16, i32),
+    "uu": _sb(12, i32), "QD": _sb(16, i32), "KU": _sb(192, f32), "HS": _sb(192, i32), "HA": _sb(192, i32),
+    "KEY": _sb(12, f32), "FK": _sb(12, bf), "k1": _sb(12, i32), "k2": _sb(12, i32), "k3": _sb(12, f32), "k4": _sb(12, i32),
+    "k5": _sb(12, i32), "k6": _sb(12, f32), "k7": _sb(12, f32), "k8": _sb(12, f32), "BB": _sb(48, f32), "OK": _sb(12, f32),
+    "JB": _sb(16, bf), "EE": _sb(12, f32), "J2": _sb(12, f32), "TO": _sb(12, f32), "o1": _sb(12, f32), "o2": _sb(12, f32),
+    "SX": _sb(192, bf), "SY": _sb(192, bf), "NLD": _sb(80, bf), "EI": _sb(80, bf), "KV": _sb(80, f32), "m1": _sb(80, f32),
+    "hb": _sb(2, bf), "TC": _sb(2, f32),
+}
+for _k in range(8):
+    SCRATCH["PS%d" % _k] = ("psum", [128, 512], f32)
+NDMA = 26
+SEMAPHORES = ["qv", "qs", "qp", "qg", "sent"] + ["d%d" % _k for _k in range(NDMA)] + ["arr%d" % _k for _k in range(6)]
+TWO = (bf, f16, u16)
+
+
+def R(name, a=0, b=None, st=1, p=(0, 128)):
+    if b is None:
+        b = SCRATCH[name][1][1]
+    m = 0
+    if st == 1:
+        m = ((1 << (b - a)) - 1) << a
+    else:
+        for c in range(a, b, st):
+            m |= 1 << c
+    return {"n": name, "a": a, "b": b, "st": st, "p": p, "m": m, "k": len(range(a, b, st)), "off": None}
+
+
+def C(name, c):
+    return R(name, c, c + 1)
+
+
+def IND(win, off):
+    d = dict(win)
+    d["off"] = off
+    d["k"] = 16 * off["k"]
+    return d
+
+
+def build(rank, cfg):
+    ops, ph = [], ["load"]
+
+    def add(q, fn, args, reads, writes, cost, lat=0.0, acc=False, sem=None):
+        rd = []
+        for r in reads:
+            if isinstance(r, dict):
+                rd.append(r)
+                if r["off"] is not None:
+                    rd.append(r["off"])
+        wr = []
+        for w in writes:
+            wr.append(w)
+            if w["off"] is not None:
+                rd.append(w["off"])
+        ops.append({"q": q, "fn": fn, "args": args, "r": rd, "w": wr, "c": cost, "lat": lat, "acc": acc, "sem": sem,
+                    "ph": ph[0], "after": []})
+
+    lab = {}
+
+    def name(k):
+        lab[k] = len(ops) - 1
+
+    def hint(a, b):
+        ops[lab[b]]["after"].append(lab[a])
+
+    def two(*v):
+        return all(SCRATCH[x["n"]][2] in TWO for x in v)
+
+    def vc(out, in0, f):
+        if in0 is not None and in0["off"] is not None:
+            return 0.05 + in0["k"] * cfg["g"] * 1e-3
+        if out["off"] is not None:
+            return 0.05 + out["k"] * cfg["sc"] * 1e-3
+        return max(64, out["k"] * f) * 1e-3
+
+    def cp(out, a):
+        add("v", "tensor_copy", (out, a), [a], [out], vc(out, a, 0.5 if two(out, a) else 1))
+
+    def tt(out, a, b, op):
+        ps = a["n"][:2] == "PS" or b["n"][:2] == "PS"
+        add("v", "tensor_tensor", (out, a, b, op), [a, b], [out], vc(out, a, 1 if ps else 2))
+
+    def ts(out, a, s1, op0, s2=None, op1=None):
+        args = (out, a, s1, s2, op0) if op1 is None else (out, a, s1, s2, op0, op1)
+        add("v", "tensor_scalar", args, [a, s1, s2], [out], vc(out, a, 0.5 if two(out, a) else 1))
+
+    def ms(out, v, q="g"):
+        if q == "g":
+            return iota(out, [[0, out["k"]]], int(v), 0)
+        add("v", "memset", (out, v), [], [out], vc(out, None, 0.5 if two(out) else 1))
+
+    def scan(out, d0, d1, init, op0, op1):
+        add("v", "tensor_tensor_scan", (out, d0, d1, init, op0, op1), [d0, d1, init], [out], vc(out, None, 1))
+
+    def red(out, a, op):
+        add("v", "tensor_reduce", (out, a, AxisListType.X, op), [a], [out], 0.064)
+
+    def act(out, a, func, bias=None, scale=None):
+        c = 0.065 + a["k"] * cfg["g"] * 1e-3 if a["off"] is not None else 0.03 + max(64, a["k"]) * 1e-3
+        add("s", "activation", (out, a, func, bias, scale), [a, bias, scale], [out], c)
+
+    def lin(out, a, scale, bias):
+        act(out, a, F.Identity, bias, scale)
+
+    def mm(out, l, r, start=True, stop=True):
+        c = max(64, r["k"]) * cfg["pe"] * (4 if SCRATCH[r["n"]][2] == f32 else 1) + 0.005
+        add("p", "matmul", (out, l, r, start, stop), [l, r], [out], c, acc=not start)
+
+    def iota(out, pat, base, cm):
+        add("g", "iota", (out, pat, base, cm), [], [out], 0.15 + out["k"] * 2e-3)
+
+    def sel(out, a, pat, op, base, cm):
+        add("g", "affine_select", (out, a, pat, op, 0.0, base, cm), [a], [out], 0.19 + out["k"] * 2e-3)
+
+    def copy(q, out, a):
+        if q == "v":
+            cp(out, a)
+        elif q == "s":
+            act(out, a, F.Copy)
+        else:
+            sel(out, a, [[0, a["k"]]], A.is_ge, 0, 0)
+
+    nd = [0]
+
+    def load(q, out, name, lat):
+        add(q, "load", (out, name), [], [out], 0.06, lat=lat, sem="d%d" % nd[0])
+        nd[0] += 1
+
+    def store(q, name, a, b, src):
+        add(q, "store", (name, a, b, src), [src], [], 0.06 if q != "g" else 1.0, lat=2.0, sem="d%d" % nd[0])
+        nd[0] += 1
+
+    load("y", R("LVI", p=(0, 8)), "live", 2.0)
+    load("y", R("RI"), "rings", 4.0)
+    load("y", R("XW", 0, NB), "x0", 6.5)
+    load("s", R("ZN"), "z", 2.4)
+    load("y", C("WI", 0), "w", 7.0)
+    load("y", C("KI", 0), "kap", 7.0)
+    load("y", R("TI", 0, 1, p=(0, 8)), "th", 7.0)
+    load("y", R("CI", 0, 1, p=(0, 8)), "cap", 7.0)
+
+    ph[0] = "c0"
+    pm, npm, pm1, pmm, pm16, mk0, mk1, c95, mlo, mhi = [C("col", k) for k in range(10)]
+    whi, wlo, kva, kvb, kvh, thr, cap, nn, n0a, n0b, hq, pm4, ntmp = [C("col", k) for k in range(10, 23)]
+    iota(C("ci", 0), [[0, 1]], 0, 1)
+    ts(C("ci", 1), C("ci", 0), 15, A.bitwise_and)
+    pi = C("ci", 1)
+    cp(pm, pi)
+    ts(mk0, pi, 0.0, A.is_equal)
+    ts(mk1, pi, 1.0, A.is_ge)
+    lin(c95, pm, 96.0, 95.0)
+    ts(mlo, pi, 8.0, A.is_lt)
+    ts(mhi, pi, 8.0, A.is_ge)
+    lin(pm4, pm, -4.0, None)
+    ms(R("ONE"), 1.0, "v")
+    ms(R("M3"), -3.0)
+    sel(R("WA", p=(0, 8)), R("ONE", p=(0, 8)), [[1, 144]], A.is_equal, -15, -16)
+    iota(R("t1"), [[-16, 8], [0, 16]], 0, 1)
+    ts(R("BO"), R("t1"), pm, A.is_equal)
+    sel(R("TRI"), R("BO"), [[1, 128]], A.is_gt, 0, -1)
+    sel(R("UPP"), R("BO"), [[-1, 128]], A.is_gt, 0, 1)
+    name("gupp")
+    iota(R("I144"), [[-1, 144]], 15, 1)
+    ts(R("WS2"), R("I144"), pm, A.is_equal, -128.0, A.mult)
+    ts(R("WS5"), R("I144"), pm, A.is_equal, -32768.0, A.mult)
+    iota(R("KV"), [[16, 80]], 2048, 0)
+    name("gkv")
+    lin(R("KV"), R("KV"), None, pm)
+    ph[0] = "c1"
+    iota(R("t2"), [[1, 16], [0, 8]], 0, 0)
+    iota(R("t3"), [[0, 16], [-16, 8]], 0, 1)
+    ts(R("t3"), R("t3"), pm, A.is_equal)
+    iota(R("t5", 0, 32), [[1, 32]], 0, 0)
+    ts(R("FW"), R("t5", 0, 32), pm, A.is_equal)
+    ts(R("t2"), R("t2"), pm, A.add, 16.0, A.min)
+    ts(R("t2"), R("t2"), -17.0, A.add, mk1, A.mult)
+    tt(R("t2"), R("t2"), R("t3"), A.mult)
+    ts(R("OS"), R("t2"), 16.0, A.add)
+    ms(R("ID7"), 1.0, "v")
+    sel(R("ID7"), R("ID7"), [[0, 7], [-1, 128]], A.is_equal, 0, 1)
+    name("gid")
+    em, at = {}, 0
+    for t in range(RO):
+        T = T0 + P * t
+        for s2 in range(PER[T][0]):
+            ph[0] = "em%d_%d" % (t, s2)
+            o0, o1 = 16 * s2 * T >> 12, (16 * s2 + 15) * T >> 12
+            n, v = o1 - o0 + 1, 16 * s2 * (T // 64) - 64 * o0
+            e = R("EM", at, at + 128 * n)
+            sel(e, R("ID7", 0, 128 * n), [[-64, n], [0, 8], [T // 64, 16]], A.is_ge, v, 0)
+            sel(e, e, [[64, n], [0, 8], [-(T // 64), 16]], A.is_ge, 63 - v, 0)
+            em[(T, s2)] = [(R("EM", at + 128 * k, at + 128 * k + 128), min(a for a in range(16) if (16 * s2 + a) * T >> 12 == o0 + k))
+                           for k in range(n)]
+            at += 128 * n
+    ph[0] = "sh"
+    for k in range(0, 128, 32):
+        act(R("SH", 16 * k, 16 * k + 512), IND(R("FW"), R("OS", k, k + 32)), F.Copy)
+    ph[0] = "c2"
+    iota(R("II"), [[0, 2], [16, 6]], 0, 0)
+    name("gii")
+    ts(R("II"), R("II"), pm, A.add)
+    ts(R("s1"), R("II"), 1.0 / 6, A.mult, -5.0 / 12, A.add)
+    cp(R("s2"), R("s1"))
+    ts(R("s1"), R("s2"), -6.0, A.mult)
+    tt(R("s1"), R("s1"), R("II"), A.add)
+    ts(R("EXO", 0, 6), R("s1", 0, 6), 0.0, A.add)
+    ts(R("EXO", 6, 12), R("s1", 6, 12), 6.0, A.add)
+    ts(R("s3"), R("s1"), 3.0, A.is_ge, -191.0, A.mult)
+    ts(R("k6"), R("s1"), 64.0, A.mult)
+    ts(R("k7"), R("s2"), 4.0, A.mult)
+    tt(R("s3"), R("s3"), R("k6"), A.add)
+    tt(R("s3"), R("s3"), R("k7"), A.add)
+    ts(R("LAN", 0, 6), R("s3", 0, 6), 0.0, A.add)
+    ts(R("LAN", 6, 12), R("s3", 6, 12), 2.0, A.add)
+    cp(R("LAU"), R("LAN"))
+    name("lau")
+    act(R("ZI"), IND(R("ZN"), R("LAU")), F.Copy)
+    for k in range(16):
+        copy(cfg["z16"][k], R("Z16", k, 3072, 16), R("ZI"))
+    ph[0] = "c3"
+    ms(R("DS"), 1.0)
+    ms(R("DS", 0, 96, 16), -1.0e6)
+    iota(R("t5"), [[0, 6], [1, 16]], 0, 0)
+    ts(R("t6"), R("t5"), pm, A.is_equal, -1.0e8, A.mult)
+    iota(R("t5"), [[0, 6], [1, 16]], -1, 0)
+    ts(R("t5"), R("t5"), pm, A.is_equal, 4194304.0, A.mult)
+    tt(R("DL"), R("t5"), R("t6"), A.add)
+    iota(R("C6"), [[0, 2], [-16, 6]], 80, 0)
+    iota(R("K4"), [[16, 12]], 4096, 0)
+    lin(R("K4"), R("K4"), None, pm)
+    ms(R("SG", 0, 9), 1.0)
+    ms(R("SG", 9, 12), -1.0)
+    iota(R("DK"), [[-64, 3], [-1, 4]], -1900, 0)
+    lin(R("DK"), R("DK"), None, pm4)
+    ms(R("ST"), 1.0)
+    ms(R("ST", 0, 12, 4), -3.0)
+    lin(C("CS", 0), pm, None, 1899.0)
+    lin(C("CS", 1), pm, 4.0, 1899.0 + 64 - 45)
+    lin(C("CS", 2), pm, 4.0, 1899.0 + 128 - 45)
+    for t in range(RO):
+        lin(C("col", 24 + t), mk0, float(NB + P * t - OFS), None)
+    iota(R("LJ"), [[1, 4], [4, 48]], 0, 0)
+    ms(R("JB", 0, 4), 0.0)
+    ms(R("UD"), 0)
+    ms(R("QD"), 0)
+    ms(R("KO"), 1032192.0)
+    ph[0] = "c4"
+    ts(C("ci", 2), C("WI", 0), 4032, A.bitwise_and)
+    ts(C("ci", 3), C("WI", 0), 63, A.bitwise_and)
+    cp(R("col", 10, 12), R("ci", 2, 4))
+    lin(R("WH"), R("BO"), whi, None)
+    lin(R("WL"), R("BO"), wlo, None)
+    ts(C("ci", 4), C("KI", 0), 127, A.bitwise_and)
+    ts(C("ci", 5), C("KI", 0), 1920, A.bitwise_and)
+    cp(R("col", 13, 15), R("ci", 4, 6))
+    lin(hq, pm, -2048.0, 30720.0)
+    lin(kva, hq, None, kvh)
+    iota(R("M96"), [[1, 16], [0, 6]], 0, 0)
+    ts(R("KA"), R("M96"), pm, A.is_equal, kva, A.mult)
+    ts(R("KB"), R("M96"), pm, A.is_equal, kvb, A.mult)
+    ts(R("KH"), R("M96"), pm, A.is_equal, kvh, A.mult)
+
+    ph[0] = "nl"
+    for k in range(2):
+        cp(R("LVB", 640 * k, 640 * k + 640, p=(0, 8)), R("LVI", 640 * k, 640 * k + 640, p=(0, 8)))
+        name("lvb%d" % k)
+    for a in range(16):
+        mm(R("PS7", 0, 80), R("WA", 15 - a, 143 - a, p=(0, 8)), R("LVB", a, 1280, 16, p=(0, 8)), a == 0, a == 15)
+    ts(R("NLD"), R("PS7", 0, 80), -1.0, A.mult)
+    scan(R("EI"), R("ONE", 0, 80), R("PS7", 0, 80), 0.0, A.mult, A.add)
+    mm(R("PS6", 0, 80), R("BO"), R("EI"), True, False)
+    mm(R("PS6", 0, 80), R("UPP"), R("NLD"), False, True)
+    mm(R("PS7", 128, 208), R("BO"), R("EI"))
+    ts(R("m1"), R("NLD"), 8192.0, A.mult)
+    tt(R("KV"), R("m1"), R("KV"), A.add)
+    tt(R("m1"), R("PS6", 0, 80), R("KV"), A.max)
+    ts(R("OSC"), R("m1"), -1.0, A.add)
+    for k in range(0, 80, cfg["nlp"]):
+        cp(R("NL", 0, 3328) | {"off": R("OSC", k, k + cfg["nlp"]), "k": 16 * cfg["nlp"]}, R("RI", 16 * k, 16 * (k + cfg["nlp"])))
+        name("nl%d" % k)
+    cp(nn, C("PS7", 128 + 79))
+    cp(n0b, C("PS7", 128 + 73))
+    ts(R("TO"), R("LAN"), C("PS7", 128 + 61), A.add)
+    for k in range(2):
+        ts(R("RG", 640 * k, 640 * k + 640), R("RI", 640 * k, 640 * k + 640), -float(OFS), A.add)
+    name("rg0")
+
+    def offsets():
+        ts(R("o1"), R("TO"), nn, A.is_ge, nn, A.mult)
+        tt(R("o2"), R("TO"), R("o1"), A.subtract)
+        cp(R("OFR"), R("o2"))
+    offsets()
+    ph[0] = "c5"
+    mm(R("PS7", 256, 352), R("BO"), R("KH"), True, False)
+    mm(R("PS7", 256, 352), R("BO"), R("KB"), False, True)
+    lin(R("KX"), R("PS7", 256, 352), None, None)
+    iota(R("REP", p=(0, 8)), [[1, 8], [0, 16]], 0, -1)
+    ts(R("REP", p=(0, 8)), R("REP", p=(0, 8)), 0.0, A.is_equal)
+    cp(R("TC", 0, 1, p=(0, 8)), R("TI", 0, 1, p=(0, 8)))
+    cp(R("TC", 1, 2, p=(0, 8)), R("CI", 0, 1, p=(0, 8)))
+    mm(R("PS7", 400, 402), R("REP", p=(0, 8)), R("TC", p=(0, 8)))
+    lin(thr, C("PS7", 400), -32768.0, 505.0 * 32768)
+    lin(cap, C("PS7", 401), None, None)
+
+    def cols(T, a, s2, s0, s1):
+        per, step = PER[T]
+        v0 = (16 * (s0 + s2) + a) * T >> 12
+        n = (s1 - s0) // per
+        return R("RG", v0, v0 + step * (n - 1) + 1, step)
+
+    def split(t):
+        T = T0 + P * t
+        per = max(2, PER[T][0])
+        s = 256
+        while ((16 * s - 1) * T >> 12) >= T - P:
+            s -= per
+        return s
+
+    def table(t, s0, s1, nb):
+        T = T0 + P * t
+        per = PER[T][0]
+        tb, xt = "TB%d" % (t % 2), "XT%d" % (t % 2)
+        ph[0] = "tb%d_%d" % (t, s0)
+        for s2 in range(per):
+            for k, (e, a) in enumerate(em[(T, s2)]):
+                mm(R("PS3", s0 + s2, s1, per), e, cols(T, a, s2, s0, s1), k == 0, k == len(em[(T, s2)]) - 1)
+        ts(R(tb, s0, s1), R("PS3", s0, s1), float(OFS), A.add)
+        name("tb%d%s" % (t, "n" if s1 == 256 else "o"))
+        for s in range(s0, s1, cfg["xp"]):
+            e = min(s1, s + cfg["xp"])
+            ph[0] = "xt%d_%d_%d" % (t, s0, s // 72)
+            act(R(xt, 16 * s, 16 * e), IND(R("XW", 0, nb), R(tb, s, e)), F.Copy)
+
+    def tails(t):
+        T = T0 + P * t
+        per = PER[T][0]
+        for a0 in range(0, 16, 2):
+            ps = "PS%d" % (4 + (a0 // 2) % 3)
+            ph[0] = "rt%d_%d" % (t, a0 // 4)
+            for a in (a0, a0 + 1):
+                o = 256 * (a % 2)
+                for s2 in range(per):
+                    mm(R(ps, o + s2, o + 256, per), R("SH", 128 * a, 128 * a + 128), cols(T, a, s2, 0, 256))
+            for a in (a0, a0 + 1):
+                o = 256 * (a % 2)
+                if a0 // 2 in cfg["rv"][t]:
+                    ts(R("RT", a, 4096, 16), R(ps, o, o + 256), float(OFS), A.add)
+                else:
+                    act(R("RT", a, 4096, 16), R(ps, o, o + 256), F.Identity, float(OFS))
+
+    for t in range(RO):
+        T, nb, xt, last = T0 + P * t, NB + P * t, "XT%d" % (t % 2), t == RO - 1
+        ph[0] = "rr%d" % t
+        cp(R("RR"), IND(R("NL", 0, 1856), R("OFR")))
+        table(t, split(t) if t else 0, 256, nb)
+        for h in range(2):
+            r0 = 0
+            for n in cfg["c2"][h]:
+                ph[0] = "g2_%d_%d_%d" % (t, h, r0 // 8)
+                a, b = 1536 * h + 96 * r0, 1536 * h + 96 * (r0 + n)
+                tt(R("D2", a, b), IND(R("XW", 0, nb), R("RR", a // 16, b // 16)), R("Z16", a, b), A.subtract)
+                name("d2_%d_%d_%d" % (t, h, r0))
+                if (h, r0) in cfg["a2v"][t]:
+                    ts(R("A2", a, b), R("D2", a, b), -1.0, A.mult, 0.0, A.max)
+                else:
+                    act(R("A2", a, b), R("D2", a, b), F.Relu, None, -1.0)
+                for r in range(r0, r0 + n):
+                    a = 1536 * h + 96 * r
+                    mm(R("PS%d" % h, 0, 96), R("WS2", 15 - r, 143 - r), R("A2", a, a + 96), r == 0, r == 15)
+                r0 += n
+            c0, c1 = 6 * h, 6 * h + 6
+            ph[0] = "p2_%d_%d" % (t, h)
+            scan(R("SC", 96 * h, 96 * h + 96), R("DS"), R("PS%d" % h, 0, 96), 0.0, A.add, A.max)
+            tt(R("e1", c0, c1), R("SC", 96 * h + 15, 96 * h + 96, 16), R("C6", c0, c1), A.add)
+            ts(R("e2", c0, c1), R("e1", c0, c1), 127, A.bitwise_and)
+            ts(R("OY", c0, c1), R("e2", c0, c1), -1.0, A.mult, c95, A.add)
+            name("oy%d_%d" % (t, h))
+            y0 = 192 * t + 96 * h
+            act(R("YS", y0, y0 + 96), IND(R("D2", 1536 * h, 1536 * h + 1536), R("OY", c0, c1)), F.Abs)
+            yr = 768 * t + 384 * h
+            cl = [0, 1] if h == 0 else [2]
+            tr = [(R("YS", y0 + 48 * k, y0 + 48 * k + 48), R("YR", yr + 48 * k, yr + 48 * k + 48),
+                   (rank + 1 + (t + c) % (N - 1)) % N) for k, c in enumerate(cl)]
+            add("g", "send", (tr, "arr%d" % (2 * t + h)), [x[0] for x in tr], [x[1] for x in tr], 0.3, lat=cfg["net"],
+                sem="arr%d" % (2 * t + h))
+            if h == 1:
+                copy(cfg["yo"], R("YR", yr + 48, yr + 96), R("YS", y0 + 48, y0 + 96))
+        ph[0] = "rh%d" % t
+        ts(R("RH"), R("RR"), -float(OFS), A.add)
+        for c in range(12):
+            i0 = 96 * (c // 6) + c % 6
+            mm(R("PS7", 16 * c, 16 * c + 16), R("SH", 0, 128), R("RH", i0, i0 + 91, 6))
+        act(R("RT", 4096, 4288), R("PS7", 0, 192), F.Identity, float(OFS))
+        lin(R("N0"), R("LJ"), mk0, C("col", 24 + t))
+        tails(t)
+        if not last:
+            table(t + 1, 0, split(t + 1), nb)
+            ph[0] = "nc%d" % t
+            lin(R("NC", 0, 3), R("CS", 0, 3), None, nn)
+            lin(R("TO"), R("LAN"), None, n0b)
+            lin(ntmp, nn, None, -48.0)
+        for h in range(2):
+            yr, c0, c1, w0 = 768 * t + 384 * h, 6 * h, 6 * h + 6, 96 * h
+            y = R("YR", yr, yr + 96)
+            ph[0] = "u%d_%d" % (t, h)
+            mm(R("PS2", w0, w0 + 96), R("WH"), y, True, False)
+            mm(R("PS2", w0, w0 + 96), R("WL"), y, False, True)
+            copy(cfg["yd"], R("YR", yr + 96, yr + 192), y)
+            copy(cfg["yd"], R("YR", yr + 192, yr + 384), R("YR", yr, yr + 192))
+            copy(cfg["yd"], R(xt, 4096 + w0, 4192 + w0), y)
+            scan(R("UL", w0, w0 + 96), R("DL"), R("PS2", w0, w0 + 96), 0.0, A.add, A.max)
+            cp(R("u0", c0, c1), R("UL", w0 + 15, w0 + 96, 16))
+            ts(R("UD", c0, c1), R("u0", c0, c1), 4095, A.bitwise_and)
+            tt(R("uu", c0, c1), R("UD", c0, c1), R("UD", c0, c1), A.mult)
+            tt(R("KU", w0, w0 + 96), IND(R("UD"), R("EXO", c0, c1)), R("KX"), A.mult)
+            ts(R("QD", c0, c1), R("uu", c0, c1), 5, A.logical_shift_right)
+            tt(R("HS", w0, w0 + 96), IND(R("QD"), R("EXO", c0, c1)), R("KU", w0, w0 + 96), A.add)
+            ts(R("HA", w0, w0 + 96), R("HS", w0, w0 + 96), 4095, A.bitwise_and)
+            cp(R("HX", w0, w0 + 96), R("HA", w0, w0 + 96))
+            m0 = 0
+            for n in cfg["c5"][h]:
+                ph[0] = "g5_%d_%d_%d" % (t, h, m0 // 8)
+                a, b = 1536 * h + 96 * m0, 1536 * h + 96 * (m0 + n)
+                tt(R("D5", a, b), IND(R(xt, 0, 4096), R("HX", a // 16, b // 16)), R("YR", yr, yr + 96 * n), A.subtract)
+                act(R("A5", a, b), R("D5", a, b), F.Abs)
+                m0 += n
+            m0 = 0
+            for n in cfg["p5"][h]:
+                ph[0] = "p5_%d_%d_%d" % (t, h, m0)
+                o = R("PS%d" % h, 6 * m0, 6 * (m0 + n))
+                for k, nm in enumerate(("KA", "KB", "KO")):
+                    mm(o, R("BO"), R(nm, 6 * m0, 6 * (m0 + n)), k == 0, False)
+                for r in range(16):
+                    a = 1536 * h + 96 * m0 + r
+                    mm(o, R("WS5", 15 - r, 143 - r), R("A5", a, a + 96 * n - 15, 16), False, r == 15)
+                m0 += n
+            for c in range(6):
+                red(C("KEY", c0 + c), R("PS%d" % h, c, 96, 6), A.max)
+        ph[0] = "k%d" % t
+        ts(R("FK"), R("KEY"), thr, A.is_ge)
+        cp(R("k1"), R("KEY"))
+        ts(R("k2"), R("k1"), 2047, A.bitwise_and)
+        tt(R("k3"), R("k2"), R("UD", 0, 12), A.mult)
+        tt(R("k4"), R("k3"), R("QD", 0, 12), A.add)
+        ts(R("k5"), R("k4"), 4095, A.bitwise_and)
+        ts(R("k6"), R("KEY"), thr, A.is_lt)
+        tt(R("k7"), R("k6"), R("K4"), A.mult)
+        tt(R("k8"), R("k5"), R("k7"), A.max)
+        cp(R("IDX"), R("k8"))
+        tt(R("NR"), IND(R("RT"), R("IDX")), R("N0"), A.add)
+        for h in range(2):
+            yr = 768 * t + 384 * h
+            tt(R("SX", 96 * h, 96 * h + 96), IND(R(xt), R("IDX", 6 * h, 6 * h + 6)), R("YR", yr, yr + 96), A.add)
+        act(R("SY"), R("SX"), F.Identity, 127.75, 0.5)
+        for c in range(4):
+            act(R("XW", nb + c, nb + 192, 4), R("SY", 48 * c, 48 * c + 48), F.Identity, -128.0)
+        for c in range(4):
+            copy(cfg["yt"][t][c], R("YT", 192 * t + c, 192 * t + 192, 4), R("NR", 48 * c, 48 * c + 48))
+        if not last:
+            ts(R("RG", T, T + 192), R("YT", 192 * t, 192 * t + 192), -float(OFS), A.add)
+            name("rg%d" % (t + 1))
+        ph[0] = "b%d" % t
+        mm(R("PS2", 256, 265), R("ONE", 0, 128), R("FK", 0, 9))
+        mm(R("PS2", 265, 268), R("M3"), R("FK", 9, 12))
+        scan(R("BB", 16 * t, 16 * t + 12), R("ONE", 0, 12), R("PS2", 256, 268), C("BB", 16 * t - 5) if t else 0.0, A.mult, A.add)
+        ts(R("OK"), R("SG"), C("BB", 16 * t + 11), A.mult, cap, A.is_le)
+        mk = 16 * t
+        for c in range(3):
+            tt(R("MK", mk + 4 * c, mk + 4 * c + 4), R("OK", c, 12, 3), R("FK", c, 12, 3), A.is_ge)
+        for c in range(3):
+            store("ysy"[c] if last else "y", "ya", 192 * t + 64 * c, 192 * t + 64 * c + 64, R("MK", mk + 4 * c, mk + 4 * c + 4))
+        store("s" if last else "y", "yx", 192 * t, 192 * t + 192, R("XW", nb, nb + 192))
+        store("y", "yt", 192 * t, 192 * t + 192, R("YT", 192 * t, 192 * t + 192))
+        if not last:
+            scan(R("JB", 4, 16), R("ST"), R("MK", mk, mk + 12), 3.0, A.add, A.add)
+            mm(R("PS2", 320, 323), R("TRI"), R("JB", 7, 16, 4), True, False)
+            mm(R("PS2", 320, 323), R("UPP"), R("JB", 3, 12, 4), False, True)
+            mm(R("PS2", 323, 324), R("BO"), C("JB", 15))
+            tt(R("EE"), R("MK", mk, mk + 12), R("DK"), A.mult)
+            tt(R("J2"), R("EE"), R("JB", 4, 16), A.add)
+            for c in range(3):
+                ts(R("OSC", c, 12, 3), R("J2", 4 * c, 4 * c + 4), C("PS2", 320 + c), A.add, C("NC", c), A.add)
+            ts(nn, C("PS2", 323), ntmp, A.add)
+            cp(R("NL") | {"off": R("OSC", 0, 12), "k": 192}, R("NR"))
+            offsets()
+            if t == 0:
+                ts(hq, C("JB", 11), mlo, A.mult)
+                ts(C("hb", 0), C("JB", 7), mhi, A.mult, hq, A.add)
+                mm(R("PS7", 300, 301), R("BO"), C("hb", 0))
+                lin(n0b, C("PS7", 300), None, ntmp)
+    for a, b in cfg["hints"]:
+        for t in range(RO):
+            if a.replace("#", str(t)) in lab and b.replace("#", str(t)) in lab:
+                hint(a.replace("#", str(t)), b.replace("#", str(t)))
+    return ops
+
+
+def depend(ops):
+    n = len(ops)
+    deps = [set() for _ in range(n)]
+    order = [set() for _ in range(n)]
+    hist, since = {}, {}
+    for i, o in enumerate(ops):
+        if o["fn"] == "load" and i and o["q"] == "y":
+            order[i].add(max(j for j in range(i) if ops[j]["q"] == "y"))
+        for kind, lst in (("r", o["r"]), ("w", o["w"])):
+            for x in lst:
+                nm = x["n"]
+                ps = nm[:2] == "PS"
+                for (j, k2, m) in hist.get(nm, ()):
+                    if j == i:
+                        continue
+                    same = ops[j]["q"] == o["q"]
+                    if ps and not same:
+                        deps[i].add(j)
+                    elif ps and o["q"] == "p":
+                        order[i].add(j)
+                        if m & x["m"] and not o["acc"]:
+                            deps[i].add(j)
+                    elif m & x["m"] and (kind == "w" or k2 == "w"):
+                        deps[i].add(j)
+        for kind, lst in (("r", o["r"]), ("w", o["w"])):
+            for x in lst:
+                h = hist.setdefault(x["n"], [])
+                if x["n"][:2] == "PS":
+                    if h and ops[h[-1][0]]["q"] != o["q"]:
+                        h[:] = [e for e in h if ops[e[0]]["q"] == ops[h[-1][0]]["q"] and e[0] > since.get(x["n"], -1)]
+                        since[x["n"]] = h[-1][0]
+                elif kind == "w":
+                    h[:] = [e for e in h if e[2] & ~x["m"] or e[0] == i]
+                h.append((i, kind, x["m"]))
+    return deps, order
+
+
+def edges(ops, deps, order, w):
+    return [[(j, ops[j]["lat"] + w) for j in deps[i]] + [(j, 0.0) for j in order[i] - deps[i]] for i in range(len(ops))]
+
+
+def place(cost, qs, pred, tail, rank):
+    n = len(cost)
+    start, line = [0.0] * n, {q: ([], []) for q in "vspgy"}
+    for i in rank:
+        t = tail[i]
+        for j, d in pred[i]:
+            x = start[j] + cost[j] + d
+            if x > t:
+                t = x
+        a, b = line[qs[i]]
+        k = len(b)
+        while k and b[k - 1] > t:
+            k -= 1
+        while k < len(a) and a[k] < t + cost[i]:
+            t = max(t, b[k])
+            k += 1
+        a.insert(k, t)
+        b.insert(k, t + cost[i])
+        start[i] = t
+    return start
+
+
+def replay(ops, pred, seq):
+    free, fin, end = {q: 0.0 for q in "vspgy"}, [0.0] * len(ops), 0.0
+    for i in seq:
+        o = ops[i]
+        t = free[o["q"]]
+        for j, d in pred[i]:
+            if fin[j] + d > t:
+                t = fin[j] + d
+        fin[i] = free[o["q"]] = t + o["c"]
+        end = max(end, fin[i] + o["lat"])
+    return end
+
+
+def schedule(cfg, rounds):
+    var = []
+    for ch in cfg["guess"]:
+        c = dict(cfg)
+        c.update(ch)
+        ops = build(0, c)
+        if not var:
+            deps, order = depend(ops)
+        var.append((ops, edges(ops, deps, order, c["wake"])))
+    ops, pred = var[0]
+    n = len(ops)
+    pred = [pred[i] + [(j, 0.0) for j in ops[i]["after"]] for i in range(n)]
+    topo, seen = [], [False] * n
+    for i in range(n):
+        stack = [i]
+        while stack:
+            k = stack[-1]
+            wait = [j for j, d in pred[k] if not seen[j]]
+            if wait:
+                stack.extend(wait)
+            else:
+                stack.pop()
+                if not seen[k]:
+                    seen[k] = True
+                    topo.append(k)
+    cost, qs = [o["c"] for o in ops], [o["q"] for o in ops]
+    succ = [[] for _ in range(n)]
+    for i in range(n):
+        for j, d in pred[i]:
+            succ[j].append((i, d))
+    lat, nil = [o["lat"] for o in ops], [0.0] * n
+    back = [0.0] * n
+    for i in topo[::-1]:
+        back[i] = max([back[k] + cost[k] + d for k, d in succ[i]] + [lat[i]])
+    rng = np.random.default_rng(cfg["seed"])
+    grp = {}
+    for i, o in enumerate(ops):
+        nm = o["w"][0]["n"] if o["w"] else "st"
+        grp.setdefault(o["ph"], []).append(i)
+        grp.setdefault((o["ph"], o["q"]), []).append(i)
+        grp.setdefault((o["ph"], nm), []).append(i)
+    grp = list(grp.values())
+    best, cur = None, None
+    for r in range(rounds):
+        if r == 0:
+            key = [-(back[i] + cost[i]) for i in range(n)]
+        elif r % 40 == 39:
+            fw = cur[3]
+            back = place(cost, qs, succ, lat, sorted(range(n), key=lambda i: (-(fw[i] + cost[i]), -i)))
+            key = [-(back[i] + cost[i]) for i in range(n)]
+        else:
+            key = list(cur[3])
+            sh = float(rng.choice([-1.0, 1.0])) * float(rng.choice([0.3, 1.0, 2.5, 6.0])) * (0.3 + float(rng.random()))
+            arcs = []
+            if r % 3:
+                fw, prev, lastq = cur[3], [-1] * n, {}
+                for i in cur[1]:
+                    prev[i] = lastq.get(qs[i], -1)
+                    lastq[qs[i]] = i
+                i = max(range(n), key=lambda k: fw[k] + cost[k] + lat[k])
+                while i >= 0:
+                    nx = -1
+                    for j, d in pred[i]:
+                        if fw[j] + cost[j] + d > fw[i] - 1e-9:
+                            nx = j
+                    if nx < 0 and prev[i] >= 0 and fw[prev[i]] + cost[prev[i]] > fw[i] - 1e-9:
+                        nx = prev[i]
+                        arcs.append((nx, i))
+                    i = nx
+            if arcs:
+                j, i = arcs[int(rng.integers(len(arcs)))]
+                far = float(rng.choice([0.0, 0.0, 0.3, 1.0]))
+                if sh < 0:
+                    key[i] = key[j] - 1e-4 - far
+                else:
+                    key[j] = key[i] + 1e-4 + far
+            else:
+                for i in grp[int(rng.integers(len(grp)))]:
+                    key[i] += sh
+            if sh > 0:
+                for i in topo:
+                    for j, d in pred[i]:
+                        if key[j] >= key[i]:
+                            key[i] = key[j] + 1e-6
+            else:
+                for i in topo[::-1]:
+                    for j, d in pred[i]:
+                        if key[j] >= key[i]:
+                            key[j] = key[i] - 1e-6
+        fw = place(cost, qs, pred, nil, sorted(range(n), key=lambda i: (key[i], i)))
+        seq = sorted(range(n), key=lambda i: (fw[i], i))
+        val = [replay(o, p, seq) for o, p in var]
+        score = sum(v / s for v, s in zip(val, cfg["norm"]))
+        if cur is None or score < cur[0] + 0.012 * (1 - r / rounds) * float(rng.random()):
+            cur = (score, seq, val, fw)
+        if best is None or score < best[0]:
+            best = (score, seq, val, fw)
+    return deps, best
+
+
+CFG = {"g": 1.5, "sc": 3.8, "pe": 0.5e-3, "wake": 0.08, "net": 2.5, "look": 0.15, "xp": 24, "z16": "s" * 16,
+       "nlp": 20, "hints": [("rg#", "d2_#_0_5"), ("rg0", "nl20"), ("gkv", "gid"), ("gii", "gid"), ("gupp", "gid"), ("lau", "lvb0"),
+                            ("tb0n", "nl60"), ("oy#_0", "d2_#_1_5"), ("tb#n", "d2_#_1_10")],
+       "a2v": [((0, 14), (0, 10), (1, 14), (1, 10))] * 3,
+       "yo": "s", "yd": "g", "yt": ["gggg", "gggg", "vvgg"],
+       "c2": [[5, 5, 4, 2], [5, 5, 4, 2]], "c5": [[4, 4, 4, 4], [4, 4, 2, 4, 2]], "p5": [[16], [10, 6]],
+       "rv": [(), (), ()], "seed": 1, "rounds": 5000, "norm": [70.0, 60.0, 85.0],
+       "guess": [{}, {"g": 1.1, "sc": 2.0, "pe": 0.9e-3, "wake": 0.15, "net": 3.5}, {"g": 2.0, "sc": 5.5, "wake": 0.05}]}
+PLAN = {}
+
+
+def rank_program(g, core, T, topo):
+    rank = T.rank_of(core)
+    if rank is None:
+        return
+    ops = build(rank, CFG)
+    if not PLAN:
+        PLAN["p"] = schedule(CFG, CFG["rounds"])
+    deps, seq = PLAN["p"][0], PLAN["p"][1][1]
+    Q = {"v": g.vector, "s": g.scalar, "p": g.tensor, "g": g, "y": g.sync}
+
+    def ap(x):
+        if not isinstance(x, dict):
+            return x
+        v = T[x["n"]][x["p"][0]:x["p"][1], x["a"]:x["b"]:x["st"]] if x["st"] != 1 else T[x["n"]][x["p"][0]:x["p"][1], x["a"]:x["b"]]
+        return v if x["off"] is None else v.indirect(ap(x["off"]))
+
+    mark, count, seen, total, sent = {}, {q: 0 for q in Q}, {}, {}, [0]
+    for i in seq:
+        o = ops[i]
+        q = o["q"]
+        need = {}
+        for j in deps[i]:
+            nm, v = mark[j]
+            need[nm] = max(need.get(nm, 0), v)
+        for nm in sorted(need):
+            if seen.get((q, nm), 0) < need[nm]:
+                Q[q].wait_ge(T.sem[nm], need[nm])
+                seen[(q, nm)] = need[nm]
+        fn, a = o["fn"], o["args"]
+        if fn == "load":
+            Q[q].dma_start(ap(a[0]), T[a[1]][:]).then_inc(T.sem[o["sem"]], 16)
+            mark[i] = (o["sem"], 16)
+        elif fn == "store":
+            Q[q].dma_start(T[a[0]][:, a[1]:a[2]], ap(a[3])).then_inc(T.sem[o["sem"]], 16)
+            mark[i] = (o["sem"], 16)
+        elif fn == "send":
+            trs, got = [], 0
+            for k, (src, dst, to) in enumerate(a[0]):
+                e = topo.engines(core, T.cores[to])
+                share = len(e) // len(a[0])
+                m = sum(1 << x for x in e[k * share:(k + 1) * share])
+                rid, pid, _se = topo.addr(T.cores[to])
+                trs.append(RemoteDMATransfer(dst_ids=[DstId(rid=rid, pnc=pid)], dma_engine_mask=m, remote_sem=T.sem[a[1]],
+                                             src=ap(src), dst=ap(dst)))
+                got += share
+            g.remote_dma_fused(trs, local_sem=T.sem.sent)
+            sent[0] += got
+            mark[i] = (a[1], got)
+        else:
+            if fn == "activation":
+                kw = {}
+                if a[3] is not None:
+                    kw["bias"] = ap(a[3])
+                if a[4] is not None:
+                    kw["scale"] = ap(a[4])
+                ins = g.scalar.activation(ap(a[0]), ap(a[1]), a[2], **kw)
+            elif fn == "iota":
+                if SCRATCH[a[0]["n"]][2] == i32:
+                    ins = g.iota(ap(a[0]), a[1], a[2], a[3])
+                else:
+                    ins = g.iota(ap(a[0]), a[1], a[2], a[3], allow_small_or_imprecise_dtypes=True)
+            else:
+                b = [ap(x) for x in a]
+                ins = (g.affine_select(*b) if fn == "affine_select" else g.tensor.matmul(*b) if fn == "matmul" else
+                       g.vector.tensor_copy(*b) if fn == "tensor_copy" else g.vector.tensor_tensor(*b) if fn == "tensor_tensor" else
+                       g.vector.tensor_scalar(*b) if fn == "tensor_scalar" else g.vector.memset(*b) if fn == "memset" else
+                       g.vector.tensor_tensor_scan(*b) if fn == "tensor_tensor_scan" else g.vector.tensor_reduce(*b))
+            count[q] += 1
+            ins.then_inc(T.sem["q" + q], 1)
+            mark[i] = ("q" + q, count[q])
+        total[mark[i][0]] = max(total.get(mark[i][0], 0), mark[i][1])
+    total["sent"] = sent[0]
+    for nm in sorted(total):
+        g.wait_ge(T.sem[nm], total[nm])

@@ -13,35 +13,41 @@ def _sb(n, d):
 
 f32, bf, i32, u16, f16 = "float32", "bfloat16", "int32", "uint16", "float16"
 SCRATCH = {
-    "XW": _sb(3648, bf), "RI": _sb(1280, i32), "RG": _sb(1664, f16), "NL": _sb(4096, f32), "RT": _sb(4288, f32),
+    "XW": _sb(3648, bf), "RI": _sb(1280, i32), "RG": _sb(1664, f16), "NL": _sb(3072, f32), "RT": _sb(4288, f32),
     "XT0": _sb(4288, bf), "XT1": _sb(4288, bf), "TB0": _sb(256, u16), "TB1": _sb(256, u16),
     "D2": _sb(3072, bf), "A2": _sb(3072, bf), "D5": _sb(3072, bf), "A5": _sb(3072, bf), "Z16": _sb(3072, bf),
-    "EM": _sb(6016, bf), "ID7": _sb(896, bf), "SH": _sb(2048, bf), "LVI": _sb(1280, i32), "LVB": _sb(1280, bf),
+    "EM": _sb(640, bf), "EA": _sb(2048, bf), "SH": _sb(2048, bf), "LVI": _sb(640, i32), "LVB": _sb(640, bf),
     "ZN": _sb(192, bf), "ZI": _sb(192, bf), "WI": _sb(4, i32), "KI": _sb(4, i32), "TI": _sb(4, i32), "CI": _sb(4, i32),
     "YR": _sb(2304, bf), "YS": _sb(576, bf), "YT": _sb(576, f32), "MK": _sb(48, f32),
     "RR": _sb(192, u16), "RH": _sb(192, f16), "OFR": _sb(12, u16), "OY": _sb(12, u16), "HX": _sb(192, u16),
-    "IDX": _sb(12, u16), "OSC": _sb(80, u16), "LAU": _sb(12, u16), "EXO": _sb(12, u16), "OS": _sb(128, u16),
-    "WS2": _sb(144, bf), "WS5": _sb(144, bf), "WA": _sb(144, bf), "BO": _sb(128, bf), "TRI": _sb(128, bf), "UPP": _sb(128, bf),
-    "ONE": _sb(144, bf), "M3": _sb(128, bf), "WH": _sb(128, bf), "WL": _sb(128, bf), "REP": _sb(128, f32), "FW": _sb(32, bf),
+    "IDX": _sb(12, u16), "OSC": _sb(12, u16), "LAU": _sb(12, u16), "EXO": _sb(12, u16), "VN": _sb(30, u16),
+    "WS1": _sb(144, bf), "WS2": _sb(144, bf), "WS5": _sb(144, bf), "WSV": _sb(144, bf), "WSU": _sb(144, f16),
+    "WA": _sb(272, bf), "ID": _sb(128, bf), "BO": _sb(128, bf), "TRI": _sb(128, bf), "UPP": _sb(128, bf), "INC": _sb(128, bf),
+    "ONE": _sb(480, bf), "M3": _sb(128, bf), "REP": _sb(128, f32), "TS": _sb(128, bf), "CE": _sb(32, f32),
     "KA": _sb(96, bf), "KB": _sb(96, bf), "KH": _sb(96, bf), "KO": _sb(96, bf), "KX": _sb(96, f32), "M96": _sb(96, f32),
-    "DS": _sb(96, f32), "DL": _sb(96, f32), "col": _sb(32, f32), "ci": _sb(16, i32), "I144": _sb(144, f32),
-    "t1": _sb(128, f32), "t2": _sb(128, f32), "t3": _sb(128, f32), "t5": _sb(96, f32), "t6": _sb(96, f32),
-    "II": _sb(12, f32), "s1": _sb(12, f32), "s2": _sb(12, i32), "s3": _sb(12, f32),
-    "LAN": _sb(12, f32), "C6": _sb(12, f32), "K4": _sb(12, f32), "SG": _sb(12, f32), "DK": _sb(12, f32), "ST": _sb(12, f32),
-    "CS": _sb(4, f32), "NC": _sb(4, f32), "LJ": _sb(192, f32), "N0": _sb(192, f32), "NR": _sb(192, f32),
-    "SC": _sb(192, f32), "e1": _sb(12, i32), "e2": _sb(12, i32), "UL": _sb(192, f32), "u0": _sb(12, i32), "UD": _sb(16, i32),
+    "KC": _sb(96, bf), "col": _sb(40, f32), "ci": _sb(16, i32), "I144": _sb(144, f32), "LT": _sb(192, bf),
+    "EB": _sb(176, bf), "BJ": _sb(11, f16), "BW": _sb(7, f32), "CW": _sb(80, f32), "WT": _sb(112, bf), "a2": _sb(7, f32),
+    "a3": _sb(7, f32), "FF": _sb(4272, bf), "FS": _sb(480, bf), "DEC": _sb(480, bf), "CL": _sb(480, bf),
+    "LAN": _sb(12, f32), "K4": _sb(12, f32), "DK": _sb(12, f32), "ST": _sb(12, f32),
+    "CS": _sb(4, f32), "NC": _sb(4, f32), "LJ": _sb(192, f32), "NR": _sb(192, f32),
+    "e1": _sb(12, i32), "e2": _sb(12, i32), "u0": _sb(12, i32), "UD": _sb(16, i32),
     "uu": _sb(12, i32), "QD": _sb(16, i32), "KU": _sb(192, f32), "HS": _sb(192, i32), "HA": _sb(192, i32),
-    "KEY": _sb(12, f32), "FK": _sb(12, bf), "k1": _sb(12, i32), "k2": _sb(12, i32), "k3": _sb(12, f32), "k4": _sb(12, i32),
-    "k5": _sb(12, i32), "k6": _sb(12, f32), "k7": _sb(12, f32), "k8": _sb(12, f32), "BB": _sb(48, f32), "OK": _sb(12, f32),
+    "KEY": _sb(12, i32), "FK": _sb(36, bf), "k2": _sb(12, i32), "k3": _sb(12, f32), "k4": _sb(12, i32),
+    "k5": _sb(12, i32), "k6": _sb(12, f32), "k7": _sb(12, f32), "k8": _sb(12, f32),
     "JB": _sb(16, bf), "EE": _sb(12, f32), "J2": _sb(12, f32), "TO": _sb(12, f32), "o1": _sb(12, f32), "o2": _sb(12, f32),
-    "SX": _sb(192, bf), "SY": _sb(192, bf), "NLD": _sb(80, bf), "EI": _sb(80, bf), "KV": _sb(80, f32), "m1": _sb(80, f32),
-    "hb": _sb(2, bf), "TC": _sb(2, f32),
+    "SX": _sb(192, bf), "SY": _sb(192, bf), "hb": _sb(2, bf), "TC": _sb(2, f32),
 }
-for _k in range(8):
-    SCRATCH["PS%d" % _k] = ("psum", [128, 512], f32)
-NDMA = 26
+for _k in ("PA", "PB"):
+    SCRATCH[_k] = ("psum", [128, 32, 16], f32)
+for _k in ("PC", "PD", "PU", "PT", "PX", "PY"):
+    SCRATCH[_k] = ("psum", [128, 512], f32)
+NDMA = 28
 SEMAPHORES = ["qv", "qs", "qp", "qg", "sent"] + ["d%d" % _k for _k in range(NDMA)] + ["arr%d" % _k for _k in range(6)]
 TWO = (bf, f16, u16)
+
+
+def psum(x):
+    return SCRATCH[x["n"]][0] == "psum"
 
 
 def R(name, a=0, b=None, st=1, p=(0, 128)):
@@ -68,7 +74,7 @@ def IND(win, off):
 
 
 def build(rank, cfg):
-    ops, ph = [], ["load"]
+    ops, ph, cy = [], ["load"], cfg["cy"]
 
     def add(q, fn, args, reads, writes, cost, lat=0.0, acc=False, sem=None):
         rd = []
@@ -82,33 +88,24 @@ def build(rank, cfg):
             wr.append(w)
             if w["off"] is not None:
                 rd.append(w["off"])
-        ops.append({"q": q, "fn": fn, "args": args, "r": rd, "w": wr, "c": cost, "lat": lat, "acc": acc, "sem": sem,
-                    "ph": ph[0], "after": []})
-
-    lab = {}
-
-    def name(k):
-        lab[k] = len(ops) - 1
-
-    def hint(a, b):
-        ops[lab[b]]["after"].append(lab[a])
+        ops.append({"q": q, "fn": fn, "args": args, "r": rd, "w": wr, "c": cost, "lat": lat, "acc": acc, "sem": sem, "ph": ph[0],
+                    "after": []})
 
     def two(*v):
         return all(SCRATCH[x["n"]][2] in TWO for x in v)
 
     def vc(out, in0, f):
         if in0 is not None and in0["off"] is not None:
-            return 0.05 + in0["k"] * cfg["g"] * 1e-3
+            return 0.05 + in0["k"] * cfg["g"] * cy
         if out["off"] is not None:
-            return 0.05 + out["k"] * cfg["sc"] * 1e-3
-        return max(64, out["k"] * f) * 1e-3
+            return 0.05 + out["k"] * cfg["sc"] * cy
+        return max(64, out["k"] * f) * cy
 
     def cp(out, a):
         add("v", "tensor_copy", (out, a), [a], [out], vc(out, a, 0.5 if two(out, a) else 1))
 
     def tt(out, a, b, op):
-        ps = a["n"][:2] == "PS" or b["n"][:2] == "PS"
-        add("v", "tensor_tensor", (out, a, b, op), [a, b], [out], vc(out, a, 1 if ps else 2))
+        add("v", "tensor_tensor", (out, a, b, op), [a, b], [out], vc(out, a, 1 if psum(a) or psum(b) else 2))
 
     def ts(out, a, s1, op0, s2=None, op1=None):
         args = (out, a, s1, s2, op0) if op1 is None else (out, a, s1, s2, op0, op1)
@@ -120,27 +117,46 @@ def build(rank, cfg):
         add("v", "memset", (out, v), [], [out], vc(out, None, 0.5 if two(out) else 1))
 
     def scan(out, d0, d1, init, op0, op1):
-        add("v", "tensor_tensor_scan", (out, d0, d1, init, op0, op1), [d0, d1, init], [out], vc(out, None, 1))
+        add("v", "tensor_tensor_scan", (out, d0, d1, init, op0, op1), [d0, d1, init], [out], vc(out, None, 0.5 if two(out, d0, d1) else 1))
 
     def red(out, a, op):
-        add("v", "tensor_reduce", (out, a, AxisListType.X, op), [a], [out], 0.064)
+        add("v", "tensor_reduce", (out, a, AxisListType.X, op), [a], [out], max(64, a["k"]) * cy)
 
     def act(out, a, func, bias=None, scale=None):
-        c = 0.065 + a["k"] * cfg["g"] * 1e-3 if a["off"] is not None else 0.03 + max(64, a["k"]) * 1e-3
+        c = 0.065 + a["k"] * cfg["g"] * cy if a["off"] is not None else 0.03 + max(64, a["k"]) * cy
         add("s", "activation", (out, a, func, bias, scale), [a, bias, scale], [out], c)
 
     def lin(out, a, scale, bias):
         act(out, a, F.Identity, bias, scale)
 
     def mm(out, l, r, start=True, stop=True):
-        c = max(64, r["k"]) * cfg["pe"] * (4 if SCRATCH[r["n"]][2] == f32 else 1) + 0.005
-        add("p", "matmul", (out, l, r, start, stop), [l, r], [out], c, acc=not start)
+        c = max(64, r["k"]) * cfg["pe"] * (4 if SCRATCH[r["n"]][2] == f32 else 1)
+        o = ops[-1]
+        if o["q"] == "p" and o["w"][0]["n"] == out["n"] and o["ph"] == ph[0] and len(o["args"]) < 17:
+            o["args"].append((out, l, r, start, stop))
+            o["r"] += [l, r]
+            o["w"].append(out)
+            o["c"] += c
+            o["acc"] = o["acc"] and not start
+        else:
+            add("p", "matmul", [(out, l, r, start, stop)], [l, r], [out], c, acc=not start)
+
+    tail = {}
+
+    def chain(k):
+        if k in tail:
+            ops[-1]["after"].append(tail[k])
+        tail[k] = len(ops) - 1
+
+    def put(out, ws, src, a, b, first=True):
+        for r in range(16):
+            mm(out, R(ws, 15 - r, 143 - r), R(src, a + r, b, 16), first and r == 0, r == 15)
 
     def iota(out, pat, base, cm):
-        add("g", "iota", (out, pat, base, cm), [], [out], 0.15 + out["k"] * 2e-3)
+        add("g", "iota", (out, pat, base, cm), [], [out], 0.15 + out["k"] * 2 * cy)
 
-    def sel(out, a, pat, op, base, cm):
-        add("g", "affine_select", (out, a, pat, op, 0.0, base, cm), [a], [out], 0.19 + out["k"] * 2e-3)
+    def sel(out, a, pat, op, base, cm, fill=0.0):
+        add("g", "affine_select", (out, a, pat, op, fill, base, cm), [a], [out], 0.19 + out["k"] * 2 * cy)
 
     def copy(q, out, a):
         if q == "v":
@@ -152,114 +168,143 @@ def build(rank, cfg):
 
     nd = [0]
 
-    def load(q, out, name, lat):
-        add(q, "load", (out, name), [], [out], 0.06, lat=lat, sem="d%d" % nd[0])
+    def load(q, out, name, a, b, lat):
+        add(q, "load", (out, name, a, b), [], [out], 0.06, lat=lat * cfg["ld"], sem="d%d" % nd[0])
         nd[0] += 1
 
     def store(q, name, a, b, src):
-        add(q, "store", (name, a, b, src), [src], [], 0.06 if q != "g" else 1.0, lat=2.0, sem="d%d" % nd[0])
+        add(q, "store", (name, a, b, src), [src], [], 0.06, lat=1.5, sem="d%d" % nd[0])
         nd[0] += 1
 
-    load("y", R("LVI", p=(0, 8)), "live", 2.0)
-    load("y", R("RI"), "rings", 4.0)
-    load("y", R("XW", 0, NB), "x0", 6.5)
-    load("s", R("ZN"), "z", 2.4)
-    load("y", C("WI", 0), "w", 7.0)
-    load("y", C("KI", 0), "kap", 7.0)
-    load("y", R("TI", 0, 1, p=(0, 8)), "th", 7.0)
-    load("y", R("CI", 0, 1, p=(0, 8)), "cap", 7.0)
+    load("y", R("LVI", p=(0, 8)), "live", 0, 640, 1.3)
+    load("y", R("LVI", p=(8, 16)), "live", 640, 1280, 1.3)
+    load("y", R("RI", 0, 640), "rings", 0, 640, 2.2)
+    load("y", R("RI", 640, 1280), "rings", 640, 1280, 3.0)
+    load("y", R("XW", 0, NB), "x0", 0, NB, 5.0)
+    load("s", R("ZN"), "z", 0, P, 1.5)
+    load("y", C("WI", 0), "w", 0, 1, 5.5)
+    load("y", C("KI", 0), "kap", 0, 1, 5.5)
+    load("y", R("TI", 0, 1, p=(0, 8)), "th", 0, 1, 5.5)
+    load("y", R("CI", 0, 1, p=(0, 8)), "cap", 0, 1, 5.5)
 
     ph[0] = "c0"
-    pm, npm, pm1, pmm, pm16, mk0, mk1, c95, mlo, mhi = [C("col", k) for k in range(10)]
-    whi, wlo, kva, kvb, kvh, thr, cap, nn, n0a, n0b, hq, pm4, ntmp = [C("col", k) for k in range(10, 23)]
-    iota(C("ci", 0), [[0, 1]], 0, 1)
-    ts(C("ci", 1), C("ci", 0), 15, A.bitwise_and)
+    (pm, mk0, c96, mlo, mhi, pm4, m15, dec, clo, chi, wv, fo, wsg, kva, kvb, kvh, thr, cap, nn, n0b, hq, ntmp, x0c, x1c,
+     c15, pm2) = [C("col", k) for k in range(26)]
     pi = C("ci", 1)
+    iota(C("ci", 0), [[0, 1]], 0, 1)
+    ts(pi, C("ci", 0), 15, A.bitwise_and)
     cp(pm, pi)
-    ts(mk0, pi, 0.0, A.is_equal)
-    ts(mk1, pi, 1.0, A.is_ge)
-    lin(c95, pm, 96.0, 95.0)
-    ts(mlo, pi, 8.0, A.is_lt)
-    ts(mhi, pi, 8.0, A.is_ge)
-    lin(pm4, pm, -4.0, None)
     ms(R("ONE"), 1.0, "v")
-    ms(R("M3"), -3.0)
-    sel(R("WA", p=(0, 8)), R("ONE", p=(0, 8)), [[1, 144]], A.is_equal, -15, -16)
-    iota(R("t1"), [[-16, 8], [0, 16]], 0, 1)
-    ts(R("BO"), R("t1"), pm, A.is_equal)
-    sel(R("TRI"), R("BO"), [[1, 128]], A.is_gt, 0, -1)
-    sel(R("UPP"), R("BO"), [[-1, 128]], A.is_gt, 0, 1)
-    name("gupp")
+    sel(R("WA", p=(0, 16)), R("ONE", 0, 272, p=(0, 16)), [[1, 272]], A.is_equal, -15, -16)
     iota(R("I144"), [[-1, 144]], 15, 1)
-    ts(R("WS2"), R("I144"), pm, A.is_equal, -128.0, A.mult)
-    ts(R("WS5"), R("I144"), pm, A.is_equal, -32768.0, A.mult)
-    iota(R("KV"), [[16, 80]], 2048, 0)
-    name("gkv")
-    lin(R("KV"), R("KV"), None, pm)
-    ph[0] = "c1"
-    iota(R("t2"), [[1, 16], [0, 8]], 0, 0)
-    iota(R("t3"), [[0, 16], [-16, 8]], 0, 1)
-    ts(R("t3"), R("t3"), pm, A.is_equal)
-    iota(R("t5", 0, 32), [[1, 32]], 0, 0)
-    ts(R("FW"), R("t5", 0, 32), pm, A.is_equal)
-    ts(R("t2"), R("t2"), pm, A.add, 16.0, A.min)
-    ts(R("t2"), R("t2"), -17.0, A.add, mk1, A.mult)
-    tt(R("t2"), R("t2"), R("t3"), A.mult)
-    ts(R("OS"), R("t2"), 16.0, A.add)
-    ms(R("ID7"), 1.0, "v")
-    sel(R("ID7"), R("ID7"), [[0, 7], [-1, 128]], A.is_equal, 0, 1)
-    name("gid")
-    em, at = {}, 0
-    for t in range(RO):
-        T = T0 + P * t
-        for s2 in range(PER[T][0]):
-            ph[0] = "em%d_%d" % (t, s2)
-            o0, o1 = 16 * s2 * T >> 12, (16 * s2 + 15) * T >> 12
-            n, v = o1 - o0 + 1, 16 * s2 * (T // 64) - 64 * o0
-            e = R("EM", at, at + 128 * n)
-            sel(e, R("ID7", 0, 128 * n), [[-64, n], [0, 8], [T // 64, 16]], A.is_ge, v, 0)
-            sel(e, e, [[64, n], [0, 8], [-(T // 64), 16]], A.is_ge, 63 - v, 0)
-            em[(T, s2)] = [(R("EM", at + 128 * k, at + 128 * k + 128), min(a for a in range(16) if (16 * s2 + a) * T >> 12 == o0 + k))
-                           for k in range(n)]
-            at += 128 * n
-    ph[0] = "sh"
-    for k in range(0, 128, 32):
-        act(R("SH", 16 * k, 16 * k + 512), IND(R("FW"), R("OS", k, k + 32)), F.Copy)
+    ts(R("WS1"), R("I144"), pm, A.is_equal)
+    sel(R("ID"), R("ONE", 0, 128), [[-1, 128]], A.is_equal, 0, 1)
+    sel(R("BO"), R("ONE", 0, 128), [[-16, 8], [0, 16]], A.is_ge, 0, 1)
+    sel(R("BO"), R("BO"), [[16, 8], [0, 16]], A.is_ge, 15, -1)
+    sel(R("INC"), R("BO"), [[1, 128]], A.is_ge, 0, -1)
+    sel(R("INC"), R("INC"), [[0, 8], [1, 16]], A.not_equal, -15, 0)
+    ts(m15, pi, 15.0, A.is_equal, 4096.0, A.mult)
+    lin(dec, m15, None, -4096.0)
+    lin(clo, m15, -256.0, -4096.0)
+    lin(chi, m15, 256.0, None)
+    lin(wv, m15, 17.0 / 2 ** 24, -1.0 / 4096)
+    lin(R("DEC"), R("ONE"), dec, None)
+    lin(R("WSV"), R("WS1"), wv, None)
+    iota(R("CW"), [[1, 80]], 0, 0)
+    act(R("CW"), R("CW"), F.Identity, dec, m15)
+    iota(R("BW", 0, 5), [[16, 5]], 1300, 0)
+    lin(R("BW", 0, 5), R("BW", 0, 5), None, pm)
+    ms(R("BJ", 5, 11), 0.0, "v")
+    cp(R("BJ", 0, 5), R("BW", 0, 5))
+    lin(R("BW", 5, 7), R("BW", 3, 5), None, 2600.0)
+    ts(C("BW", 5), pm, 14.0, A.is_ge, C("BW", 5), A.mult)
+    ms(R("EB", 0, 96), 0.0, "v")
+    ms(R("FF", 0, 480), -32768.0, "v")
     ph[0] = "c2"
-    iota(R("II"), [[0, 2], [16, 6]], 0, 0)
-    name("gii")
-    ts(R("II"), R("II"), pm, A.add)
-    ts(R("s1"), R("II"), 1.0 / 6, A.mult, -5.0 / 12, A.add)
-    cp(R("s2"), R("s1"))
-    ts(R("s1"), R("s2"), -6.0, A.mult)
-    tt(R("s1"), R("s1"), R("II"), A.add)
-    ts(R("EXO", 0, 6), R("s1", 0, 6), 0.0, A.add)
-    ts(R("EXO", 6, 12), R("s1", 6, 12), 6.0, A.add)
-    ts(R("s3"), R("s1"), 3.0, A.is_ge, -191.0, A.mult)
-    ts(R("k6"), R("s1"), 64.0, A.mult)
-    ts(R("k7"), R("s2"), 4.0, A.mult)
-    tt(R("s3"), R("s3"), R("k6"), A.add)
-    tt(R("s3"), R("s3"), R("k7"), A.add)
-    ts(R("LAN", 0, 6), R("s3", 0, 6), 0.0, A.add)
-    ts(R("LAN", 6, 12), R("s3", 6, 12), 2.0, A.add)
+    iota(R("LT", 0, 96), [[4, 16], [1, 2], [64, 3]], 0, 0)
+    iota(R("LT", 96, 192), [[0, 16], [1, 6]], 0, 0)
+    put(R("PX", 0, 12), "WS1", "LT", 0, 192)
+    ts(R("LAN", 0, 6), R("PX", 0, 6), 1.0 / 16, A.mult)
+    ts(R("LAN", 6, 12), R("PX", 0, 6), 1.0 / 16, A.mult, 2.0, A.add)
+    ts(R("EXO", 0, 6), R("PX", 6, 12), 1.0 / 16, A.mult)
+    ts(R("EXO", 6, 12), R("PX", 6, 12), 1.0 / 16, A.mult, 6.0, A.add)
     cp(R("LAU"), R("LAN"))
-    name("lau")
     act(R("ZI"), IND(R("ZN"), R("LAU")), F.Copy)
     for k in range(16):
         copy(cfg["z16"][k], R("Z16", k, 3072, 16), R("ZI"))
+
+    ph[0] = "nl"
+    cp(R("LVB", p=(0, 16)), R("LVI", p=(0, 16)))
+    for q in range(2):
+        for a in range(16):
+            mm(R("PC", 40 * q, 40 * q + 40), R("WA", 128 * q + 15 - a, 128 * q + 143 - a, p=(0, 16)), R("LVB", a, 640, 16, p=(0, 16)),
+               a == 0, a == 15)
+    scan(R("EB", 1, 81), R("ONE", 0, 80), R("PC", 0, 80), 0.0, A.mult, A.add)
+    ts(R("EB", 96, 176), R("PC", 0, 80), 4096.0, A.mult)
+    mm(R("PU", 0, 80), R("INC"), R("EB", 96, 176))
+    mm(R("PD", 16, 20), R("BO"), R("EB", 62, 81, 6))
+    mm(R("PD", 0, 11), R("ID"), R("BJ"), True, False)
+    put(R("PD", 0, 11), "WS1", "EB", 0, 176, False)
+    tt(R("WT", 0, 80), R("PU", 0, 80), R("CW"), A.add)
+    tt(R("WT", 80, 112), R("PU", 48, 80), R("CW", 48, 80), A.add)
+    tt(R("a2", 0, 5), R("PD", 6, 11), R("BW", 0, 5), A.min)
+    tt(R("a2", 5, 7), R("PD", 9, 11), R("BW", 5, 7), A.min)
+    tt(R("a3", 0, 5), R("PD", 0, 5), R("a2", 0, 5), A.subtract)
+    tt(R("a3", 5, 7), R("PD", 3, 5), R("a2", 5, 7), A.subtract)
+    ts(R("OSC", 0, 5), R("a3", 0, 5), 288.0, A.add)
+    ts(R("OSC", 5, 7), R("a3", 5, 7), C("PD", 19), A.subtract, 2888.0, A.add)
+    ts(R("col", 22, 24), R("PD", 16, 19, 2), C("PD", 19), A.subtract, 288.0, A.add)
+    cp(IND(R("FF"), R("OSC", 0, 7)), R("WT"))
+    for a, b in ((0, 288), (288, 480)):
+        scan(R("FS", a, b), R("DEC", a, b), R("FF", a, b), 0.0, A.add, A.max)
+    ts(R("OFR"), R("LAN"), x0c, A.add)
+    ts(R("CL", 0, 192), IND(R("FS"), R("OFR")), clo, A.max, chi, A.min)
+    put(R("PC", 96, 108), "WSV", "CL", 0, 192)
+    cp(R("VN", 0, 12), R("PC", 96, 108))
+    cp(R("RR"), IND(R("RI"), R("VN", 0, 12)))
+    ph[0] = "nl2"
+    ts(R("CL", 192, 480), R("FS", 192, 480), clo, A.max, chi, A.min)
+    put(R("PU", 96, 114), "WSV", "CL", 192, 480)
+    cp(R("VN", 12, 30), R("PU", 96, 114))
+    cp(R("NL", 192, 288), IND(R("RI"), R("VN", 12, 18)))
+    cp(R("NL", 0, 192), IND(R("RI"), R("VN", 18, 30)))
+    lin(R("TO"), R("LAN"), None, x1c)
+    ph[0] = "rg"
+    for k in range(2):
+        ts(R("RG", 640 * k, 640 * k + 640), R("RI", 640 * k, 640 * k + 640), -float(OFS), A.add)
+    ph[0] = "em"
+    ts(C("ci", 6), pi, 5.0, A.mult, 16.0, A.add)
+    ts(C("ci", 7), C("ci", 6), 4, A.logical_shift_right)
+    cp(fo, C("ci", 7))
+    for o in range(5):
+        ts(R("EM", 128 * o, 128 * o + 128), R("ID"), fo, A.mult, o + 1.0, A.is_equal)
+    for a in range(16):
+        ph[0] = "ea%d" % (a // 4)
+        sel(R("EA", 128 * a, 128 * a + 128), R("ID"), [[0, 8], [1, 16]], A.is_equal, -a, 0)
+    ph[0] = "sh"
+    iota(R("TS"), [[32, 8], [1, 16]], -1, 0)
+    sel(R("TS"), R("TS"), [[-16, 8], [0, 16]], A.is_ge, 0, 1, -100.0)
+    sel(R("TS"), R("TS"), [[0, 8], [1, 16]], A.is_gt, 0, 0, -100.0)
+    iota(R("CE"), [[15, 2], [-1, 16]], 0, 2)
+    lin(pm2, pm, -1.0, None)
+    lin(R("CE"), R("CE"), None, pm2)
+    lin(R("CE", 16, 32), R("CE", 16, 32), None, pm2)
+    for a in range(16):
+        ts(R("SH", 128 * a, 128 * a + 128), R("TS"), C("CE", 16 + a), A.min, C("CE", a), A.is_equal)
     ph[0] = "c3"
-    ms(R("DS"), 1.0)
-    ms(R("DS", 0, 96, 16), -1.0e6)
-    iota(R("t5"), [[0, 6], [1, 16]], 0, 0)
-    ts(R("t6"), R("t5"), pm, A.is_equal, -1.0e8, A.mult)
-    iota(R("t5"), [[0, 6], [1, 16]], -1, 0)
-    ts(R("t5"), R("t5"), pm, A.is_equal, 4194304.0, A.mult)
-    tt(R("DL"), R("t5"), R("t6"), A.add)
-    iota(R("C6"), [[0, 2], [-16, 6]], 80, 0)
+    ts(mk0, pi, 0.0, A.is_equal)
+    ts(mlo, pi, 8.0, A.is_lt)
+    ts(mhi, pi, 8.0, A.is_ge)
+    lin(c96, pm, 96.0, None)
+    lin(pm4, pm, -4.0, None)
+    lin(R("WS2"), R("WS1"), 128.0, None)
+    lin(R("WS5"), R("WS1"), -32768.0, None)
+    iota(R("KC"), [[1, 96]], 0, 0)
+    sel(R("TRI"), R("BO"), [[1, 128]], A.is_gt, 0, -1)
+    sel(R("UPP"), R("BO"), [[-1, 128]], A.is_gt, 0, 1)
+    ms(R("M3"), 3.0)
     iota(R("K4"), [[16, 12]], 4096, 0)
     lin(R("K4"), R("K4"), None, pm)
-    ms(R("SG", 0, 9), 1.0)
-    ms(R("SG", 9, 12), -1.0)
     iota(R("DK"), [[-64, 3], [-1, 4]], -1900, 0)
     lin(R("DK"), R("DK"), None, pm4)
     ms(R("ST"), 1.0)
@@ -268,69 +313,37 @@ def build(rank, cfg):
     lin(C("CS", 1), pm, 4.0, 1899.0 + 64 - 45)
     lin(C("CS", 2), pm, 4.0, 1899.0 + 128 - 45)
     for t in range(RO):
-        lin(C("col", 24 + t), mk0, float(NB + P * t - OFS), None)
+        lin(C("col", 30 + t), mk0, float(NB + P * t - OFS), float(OFS))
     iota(R("LJ"), [[1, 4], [4, 48]], 0, 0)
+    lin(R("LJ"), R("LJ"), mk0, None)
     ms(R("JB", 0, 4), 0.0)
     ms(R("UD"), 0)
     ms(R("QD"), 0)
     ms(R("KO"), 1032192.0)
+    ms(nn, 288.0)
     ph[0] = "c4"
-    ts(C("ci", 2), C("WI", 0), 4032, A.bitwise_and)
-    ts(C("ci", 3), C("WI", 0), 63, A.bitwise_and)
-    cp(R("col", 10, 12), R("ci", 2, 4))
-    lin(R("WH"), R("BO"), whi, None)
-    lin(R("WL"), R("BO"), wlo, None)
+    ts(C("ci", 2), C("WI", 0), 2048.0, A.is_ge, -4096.0, A.mult)
+    tt(wsg, C("ci", 2), C("WI", 0), A.add)
+    ts(R("WSU"), R("WS1"), wsg, A.mult)
     ts(C("ci", 4), C("KI", 0), 127, A.bitwise_and)
     ts(C("ci", 5), C("KI", 0), 1920, A.bitwise_and)
-    cp(R("col", 13, 15), R("ci", 4, 6))
-    lin(hq, pm, -2048.0, 30720.0)
-    lin(kva, hq, None, kvh)
+    cp(R("col", 14, 16), R("ci", 4, 6))
+    lin(c15, pm, -2048.0, 30720.0)
+    lin(kva, c15, None, kvh)
     iota(R("M96"), [[1, 16], [0, 6]], 0, 0)
     ts(R("KA"), R("M96"), pm, A.is_equal, kva, A.mult)
     ts(R("KB"), R("M96"), pm, A.is_equal, kvb, A.mult)
     ts(R("KH"), R("M96"), pm, A.is_equal, kvh, A.mult)
-
-    ph[0] = "nl"
-    for k in range(2):
-        cp(R("LVB", 640 * k, 640 * k + 640, p=(0, 8)), R("LVI", 640 * k, 640 * k + 640, p=(0, 8)))
-        name("lvb%d" % k)
-    for a in range(16):
-        mm(R("PS7", 0, 80), R("WA", 15 - a, 143 - a, p=(0, 8)), R("LVB", a, 1280, 16, p=(0, 8)), a == 0, a == 15)
-    ts(R("NLD"), R("PS7", 0, 80), -1.0, A.mult)
-    scan(R("EI"), R("ONE", 0, 80), R("PS7", 0, 80), 0.0, A.mult, A.add)
-    mm(R("PS6", 0, 80), R("BO"), R("EI"), True, False)
-    mm(R("PS6", 0, 80), R("UPP"), R("NLD"), False, True)
-    mm(R("PS7", 128, 208), R("BO"), R("EI"))
-    ts(R("m1"), R("NLD"), 8192.0, A.mult)
-    tt(R("KV"), R("m1"), R("KV"), A.add)
-    tt(R("m1"), R("PS6", 0, 80), R("KV"), A.max)
-    ts(R("OSC"), R("m1"), -1.0, A.add)
-    for k in range(0, 80, cfg["nlp"]):
-        cp(R("NL", 0, 3328) | {"off": R("OSC", k, k + cfg["nlp"]), "k": 16 * cfg["nlp"]}, R("RI", 16 * k, 16 * (k + cfg["nlp"])))
-        name("nl%d" % k)
-    cp(nn, C("PS7", 128 + 79))
-    cp(n0b, C("PS7", 128 + 73))
-    ts(R("TO"), R("LAN"), C("PS7", 128 + 61), A.add)
-    for k in range(2):
-        ts(R("RG", 640 * k, 640 * k + 640), R("RI", 640 * k, 640 * k + 640), -float(OFS), A.add)
-    name("rg0")
-
-    def offsets():
-        ts(R("o1"), R("TO"), nn, A.is_ge, nn, A.mult)
-        tt(R("o2"), R("TO"), R("o1"), A.subtract)
-        cp(R("OFR"), R("o2"))
-    offsets()
-    ph[0] = "c5"
-    mm(R("PS7", 256, 352), R("BO"), R("KH"), True, False)
-    mm(R("PS7", 256, 352), R("BO"), R("KB"), False, True)
-    lin(R("KX"), R("PS7", 256, 352), None, None)
+    mm(R("PY", 256, 352), R("BO"), R("KH"), True, False)
+    mm(R("PY", 256, 352), R("BO"), R("KB"), False, True)
+    lin(R("KX"), R("PY", 256, 352), None, None)
     iota(R("REP", p=(0, 8)), [[1, 8], [0, 16]], 0, -1)
     ts(R("REP", p=(0, 8)), R("REP", p=(0, 8)), 0.0, A.is_equal)
     cp(R("TC", 0, 1, p=(0, 8)), R("TI", 0, 1, p=(0, 8)))
     cp(R("TC", 1, 2, p=(0, 8)), R("CI", 0, 1, p=(0, 8)))
-    mm(R("PS7", 400, 402), R("REP", p=(0, 8)), R("TC", p=(0, 8)))
-    lin(thr, C("PS7", 400), -32768.0, 505.0 * 32768)
-    lin(cap, C("PS7", 401), None, None)
+    mm(R("PY", 400, 402), R("REP", p=(0, 8)), R("TC", p=(0, 8)))
+    lin(thr, C("PY", 400), -32768.0, 505.0 * 32768)
+    lin(cap, C("PY", 401), None, None)
 
     def cols(T, a, s2, s0, s1):
         per, step = PER[T]
@@ -351,21 +364,22 @@ def build(rank, cfg):
         per = PER[T][0]
         tb, xt = "TB%d" % (t % 2), "XT%d" % (t % 2)
         ph[0] = "tb%d_%d" % (t, s0)
+        ms_ = [("EM", o, (16 * o + 4) // 5) for o in range(5)] if t == 0 else [("EA", a, a) for a in range(16)]
         for s2 in range(per):
-            for k, (e, a) in enumerate(em[(T, s2)]):
-                mm(R("PS3", s0 + s2, s1, per), e, cols(T, a, s2, s0, s1), k == 0, k == len(em[(T, s2)]) - 1)
-        ts(R(tb, s0, s1), R("PS3", s0, s1), float(OFS), A.add)
-        name("tb%d%s" % (t, "n" if s1 == 256 else "o"))
+            for k, (e, o, a) in enumerate(ms_):
+                mm(R("PT", s0 + s2, s1, per), R(e, 128 * o, 128 * o + 128), cols(T, a, s2, s0, s1), k == 0, k == len(ms_) - 1)
+        ts(R(tb, s0, s1), R("PT", s0, s1), float(OFS), A.add)
         for s in range(s0, s1, cfg["xp"]):
             e = min(s1, s + cfg["xp"])
             ph[0] = "xt%d_%d_%d" % (t, s0, s // 72)
-            act(R(xt, 16 * s, 16 * e), IND(R("XW", 0, nb), R(tb, s, e)), F.Copy)
+            copy("v" if (t, s) in cfg["xv"] else "s", R(xt, 16 * s, 16 * e), IND(R("XW", 0, nb), R(tb, s, e)))
+            chain("x")
 
     def tails(t):
         T = T0 + P * t
         per = PER[T][0]
         for a0 in range(0, 16, 2):
-            ps = "PS%d" % (4 + (a0 // 2) % 3)
+            ps = ("PX", "PY")[(a0 // 2) % 2]
             ph[0] = "rt%d_%d" % (t, a0 // 4)
             for a in (a0, a0 + 1):
                 o = 256 * (a % 2)
@@ -374,37 +388,38 @@ def build(rank, cfg):
             for a in (a0, a0 + 1):
                 o = 256 * (a % 2)
                 if a0 // 2 in cfg["rv"][t]:
-                    ts(R("RT", a, 4096, 16), R(ps, o, o + 256), float(OFS), A.add)
+                    ts(R("RT", a, 4096, 16), R(ps, o, o + 256), C("col", 30 + t), A.add)
                 else:
-                    act(R("RT", a, 4096, 16), R(ps, o, o + 256), F.Identity, float(OFS))
+                    lin(R("RT", a, 4096, 16), R(ps, o, o + 256), None, C("col", 30 + t))
 
     for t in range(RO):
         T, nb, xt, last = T0 + P * t, NB + P * t, "XT%d" % (t % 2), t == RO - 1
         ph[0] = "rr%d" % t
-        cp(R("RR"), IND(R("NL", 0, 1856), R("OFR")))
+        if t:
+            cp(R("RR"), IND(R("NL", 0, 672), R("OFR")))
         table(t, split(t) if t else 0, 256, nb)
         for h in range(2):
-            r0 = 0
-            for n in cfg["c2"][h]:
+            r0, key = 0, R(("PA", "PB")[h], 0, 96)
+            ph[0] = "g2_%d_%d_0" % (t, h)
+            mm(key, R("ID"), R("KC"), True, False)
+            for n, q in zip(cfg["c2"][h], cfg["a2"][t][h]):
                 ph[0] = "g2_%d_%d_%d" % (t, h, r0 // 8)
                 a, b = 1536 * h + 96 * r0, 1536 * h + 96 * (r0 + n)
                 tt(R("D2", a, b), IND(R("XW", 0, nb), R("RR", a // 16, b // 16)), R("Z16", a, b), A.subtract)
-                name("d2_%d_%d_%d" % (t, h, r0))
-                if (h, r0) in cfg["a2v"][t]:
+                chain("d")
+                if q == "v":
                     ts(R("A2", a, b), R("D2", a, b), -1.0, A.mult, 0.0, A.max)
                 else:
                     act(R("A2", a, b), R("D2", a, b), F.Relu, None, -1.0)
                 for r in range(r0, r0 + n):
                     a = 1536 * h + 96 * r
-                    mm(R("PS%d" % h, 0, 96), R("WS2", 15 - r, 143 - r), R("A2", a, a + 96), r == 0, r == 15)
+                    mm(key, R("WS2", 15 - r, 143 - r), R("A2", a, a + 96), False, r == 15)
                 r0 += n
             c0, c1 = 6 * h, 6 * h + 6
             ph[0] = "p2_%d_%d" % (t, h)
-            scan(R("SC", 96 * h, 96 * h + 96), R("DS"), R("PS%d" % h, 0, 96), 0.0, A.add, A.max)
-            tt(R("e1", c0, c1), R("SC", 96 * h + 15, 96 * h + 96, 16), R("C6", c0, c1), A.add)
+            red(R("e1", c0, c1), key, A.min)
             ts(R("e2", c0, c1), R("e1", c0, c1), 127, A.bitwise_and)
-            ts(R("OY", c0, c1), R("e2", c0, c1), -1.0, A.mult, c95, A.add)
-            name("oy%d_%d" % (t, h))
+            ts(R("OY", c0, c1), R("e2", c0, c1), c96, A.add)
             y0 = 192 * t + 96 * h
             act(R("YS", y0, y0 + 96), IND(R("D2", 1536 * h, 1536 * h + 1536), R("OY", c0, c1)), F.Abs)
             yr = 768 * t + 384 * h
@@ -419,27 +434,25 @@ def build(rank, cfg):
         ts(R("RH"), R("RR"), -float(OFS), A.add)
         for c in range(12):
             i0 = 96 * (c // 6) + c % 6
-            mm(R("PS7", 16 * c, 16 * c + 16), R("SH", 0, 128), R("RH", i0, i0 + 91, 6))
-        act(R("RT", 4096, 4288), R("PS7", 0, 192), F.Identity, float(OFS))
-        lin(R("N0"), R("LJ"), mk0, C("col", 24 + t))
+            mm(R("PT", 256 + 16 * c, 272 + 16 * c), R("SH", 0, 128), R("RH", i0, i0 + 91, 6))
+        lin(R("RT", 4096, 4288), R("PT", 256, 448), None, C("col", 30 + t))
         tails(t)
         if not last:
             table(t + 1, 0, split(t + 1), nb)
             ph[0] = "nc%d" % t
             lin(R("NC", 0, 3), R("CS", 0, 3), None, nn)
-            lin(R("TO"), R("LAN"), None, n0b)
+            if t:
+                lin(R("TO"), R("LAN"), None, n0b)
             lin(ntmp, nn, None, -48.0)
         for h in range(2):
-            yr, c0, c1, w0 = 768 * t + 384 * h, 6 * h, 6 * h + 6, 96 * h
+            yr, c0, c1, w0, key = 768 * t + 384 * h, 6 * h, 6 * h + 6, 96 * h, ("PC", "PD")[h]
             y = R("YR", yr, yr + 96)
             ph[0] = "u%d_%d" % (t, h)
-            mm(R("PS2", w0, w0 + 96), R("WH"), y, True, False)
-            mm(R("PS2", w0, w0 + 96), R("WL"), y, False, True)
+            put(R("PU", c0, c1), "WSU", "YR", yr, yr + 96)
             copy(cfg["yd"], R("YR", yr + 96, yr + 192), y)
             copy(cfg["yd"], R("YR", yr + 192, yr + 384), R("YR", yr, yr + 192))
             copy(cfg["yd"], R(xt, 4096 + w0, 4192 + w0), y)
-            scan(R("UL", w0, w0 + 96), R("DL"), R("PS2", w0, w0 + 96), 0.0, A.add, A.max)
-            cp(R("u0", c0, c1), R("UL", w0 + 15, w0 + 96, 16))
+            cp(R("u0", c0, c1), R("PU", c0, c1))
             ts(R("UD", c0, c1), R("u0", c0, c1), 4095, A.bitwise_and)
             tt(R("uu", c0, c1), R("UD", c0, c1), R("UD", c0, c1), A.mult)
             tt(R("KU", w0, w0 + 96), IND(R("UD"), R("EXO", c0, c1)), R("KX"), A.mult)
@@ -452,24 +465,32 @@ def build(rank, cfg):
                 ph[0] = "g5_%d_%d_%d" % (t, h, m0 // 8)
                 a, b = 1536 * h + 96 * m0, 1536 * h + 96 * (m0 + n)
                 tt(R("D5", a, b), IND(R(xt, 0, 4096), R("HX", a // 16, b // 16)), R("YR", yr, yr + 96 * n), A.subtract)
+                chain("d")
                 act(R("A5", a, b), R("D5", a, b), F.Abs)
+                chain("a")
                 m0 += n
             m0 = 0
             for n in cfg["p5"][h]:
                 ph[0] = "p5_%d_%d_%d" % (t, h, m0)
-                o = R("PS%d" % h, 6 * m0, 6 * (m0 + n))
+                o = R(key, 6 * m0, 6 * (m0 + n))
                 for k, nm in enumerate(("KA", "KB", "KO")):
                     mm(o, R("BO"), R(nm, 6 * m0, 6 * (m0 + n)), k == 0, False)
-                for r in range(16):
-                    a = 1536 * h + 96 * m0 + r
-                    mm(o, R("WS5", 15 - r, 143 - r), R("A5", a, a + 96 * n - 15, 16), False, r == 15)
+                put(o, "WS5", "A5", 1536 * h + 96 * m0, 1536 * h + 96 * (m0 + n), False)
                 m0 += n
             for c in range(6):
-                red(C("KEY", c0 + c), R("PS%d" % h, c, 96, 6), A.max)
+                red(C("KEY", c0 + c), R(key, c, 96, 6), A.max)
+        ph[0] = "b%d" % t
+        mk = 16 * t
+        for c in range(4):
+            ts(R("FK", 12 * t + c, 12 * t + 12, 4), R("KEY", 3 * c, 3 * c + 3), thr, A.is_ge, 1.0 if c < 3 else -1.0, A.mult)
+        for c in range(12 * t + 12):
+            ph[0] = "b%d%s" % (t, "" if c >= 12 * t else "o")
+            mm(C("PU", 16), R("ONE", 0, 128) if c % 4 < 3 else R("M3"), C("FK", c), c == 0, c == 12 * t + 11)
+        ts(R("MK", mk, mk + 12), R("FK", 12 * t, 12 * t + 12), C("PU", 16), A.mult, cap, A.is_le)
+        for c in range(3):
+            store("ysy"[c] if last else "y", "ya", 192 * t + 64 * c, 192 * t + 64 * c + 64, R("MK", mk + 4 * c, mk + 4 * c + 4))
         ph[0] = "k%d" % t
-        ts(R("FK"), R("KEY"), thr, A.is_ge)
-        cp(R("k1"), R("KEY"))
-        ts(R("k2"), R("k1"), 2047, A.bitwise_and)
+        ts(R("k2"), R("KEY"), 2047, A.bitwise_and)
         tt(R("k3"), R("k2"), R("UD", 0, 12), A.mult)
         tt(R("k4"), R("k3"), R("QD", 0, 12), A.add)
         ts(R("k5"), R("k4"), 4095, A.bitwise_and)
@@ -477,51 +498,44 @@ def build(rank, cfg):
         tt(R("k7"), R("k6"), R("K4"), A.mult)
         tt(R("k8"), R("k5"), R("k7"), A.max)
         cp(R("IDX"), R("k8"))
-        tt(R("NR"), IND(R("RT"), R("IDX")), R("N0"), A.add)
-        for h in range(2):
-            yr = 768 * t + 384 * h
-            tt(R("SX", 96 * h, 96 * h + 96), IND(R(xt), R("IDX", 6 * h, 6 * h + 6)), R("YR", yr, yr + 96), A.add)
-        act(R("SY"), R("SX"), F.Identity, 127.75, 0.5)
+        tt(R("NR"), IND(R("RT"), R("IDX")), R("LJ"), A.add)
+        if cfg["sx"][t] == "v":
+            for h in range(2):
+                yr = 768 * t + 384 * h
+                tt(R("SX", 96 * h, 96 * h + 96), IND(R(xt), R("IDX", 6 * h, 6 * h + 6)), R("YR", yr, yr + 96), A.add)
+            lin(R("SY"), R("SX"), 0.5, 127.75)
+        else:
+            act(R("SX"), IND(R(xt), R("IDX")), F.Copy)
+            mm(R("PT", 256, 448), R("ID"), R(xt, 4096, 4288), True, False)
+            mm(R("PT", 256, 448), R("ID"), R("SX"), False, True)
+            lin(R("SY"), R("PT", 256, 448), 0.5, 127.75)
         for c in range(4):
-            act(R("XW", nb + c, nb + 192, 4), R("SY", 48 * c, 48 * c + 48), F.Identity, -128.0)
+            lin(R("XW", nb + c, nb + 192, 4), R("SY", 48 * c, 48 * c + 48), None, -128.0)
         for c in range(4):
             copy(cfg["yt"][t][c], R("YT", 192 * t + c, 192 * t + 192, 4), R("NR", 48 * c, 48 * c + 48))
-        if not last:
-            ts(R("RG", T, T + 192), R("YT", 192 * t, 192 * t + 192), -float(OFS), A.add)
-            name("rg%d" % (t + 1))
-        ph[0] = "b%d" % t
-        mm(R("PS2", 256, 265), R("ONE", 0, 128), R("FK", 0, 9))
-        mm(R("PS2", 265, 268), R("M3"), R("FK", 9, 12))
-        scan(R("BB", 16 * t, 16 * t + 12), R("ONE", 0, 12), R("PS2", 256, 268), C("BB", 16 * t - 5) if t else 0.0, A.mult, A.add)
-        ts(R("OK"), R("SG"), C("BB", 16 * t + 11), A.mult, cap, A.is_le)
-        mk = 16 * t
-        for c in range(3):
-            tt(R("MK", mk + 4 * c, mk + 4 * c + 4), R("OK", c, 12, 3), R("FK", c, 12, 3), A.is_ge)
-        for c in range(3):
-            store("ysy"[c] if last else "y", "ya", 192 * t + 64 * c, 192 * t + 64 * c + 64, R("MK", mk + 4 * c, mk + 4 * c + 4))
         store("s" if last else "y", "yx", 192 * t, 192 * t + 192, R("XW", nb, nb + 192))
         store("y", "yt", 192 * t, 192 * t + 192, R("YT", 192 * t, 192 * t + 192))
         if not last:
+            ts(R("RG", T, T + 192), R("YT", 192 * t, 192 * t + 192), -float(OFS), A.add)
+            ph[0] = "n%d" % t
             scan(R("JB", 4, 16), R("ST"), R("MK", mk, mk + 12), 3.0, A.add, A.add)
-            mm(R("PS2", 320, 323), R("TRI"), R("JB", 7, 16, 4), True, False)
-            mm(R("PS2", 320, 323), R("UPP"), R("JB", 3, 12, 4), False, True)
-            mm(R("PS2", 323, 324), R("BO"), C("JB", 15))
+            mm(R("PU", 32, 35), R("TRI"), R("JB", 7, 16, 4), True, False)
+            mm(R("PU", 32, 35), R("UPP"), R("JB", 3, 12, 4), False, True)
+            mm(R("PU", 35, 36), R("BO"), C("JB", 15))
             tt(R("EE"), R("MK", mk, mk + 12), R("DK"), A.mult)
             tt(R("J2"), R("EE"), R("JB", 4, 16), A.add)
             for c in range(3):
-                ts(R("OSC", c, 12, 3), R("J2", 4 * c, 4 * c + 4), C("PS2", 320 + c), A.add, C("NC", c), A.add)
-            ts(nn, C("PS2", 323), ntmp, A.add)
-            cp(R("NL") | {"off": R("OSC", 0, 12), "k": 192}, R("NR"))
-            offsets()
+                ts(R("OSC", c, 12, 3), R("J2", 4 * c, 4 * c + 4), C("PU", 32 + c), A.add, C("NC", c), A.add)
+            ts(nn, C("PU", 35), ntmp, A.add)
+            cp(IND(R("NL"), R("OSC")), R("NR"))
+            ts(R("o1"), R("TO"), nn, A.is_ge, nn, A.mult)
+            tt(R("o2"), R("TO"), R("o1"), A.subtract)
+            cp(R("OFR"), R("o2"))
             if t == 0:
                 ts(hq, C("JB", 11), mlo, A.mult)
                 ts(C("hb", 0), C("JB", 7), mhi, A.mult, hq, A.add)
-                mm(R("PS7", 300, 301), R("BO"), C("hb", 0))
-                lin(n0b, C("PS7", 300), None, ntmp)
-    for a, b in cfg["hints"]:
-        for t in range(RO):
-            if a.replace("#", str(t)) in lab and b.replace("#", str(t)) in lab:
-                hint(a.replace("#", str(t)), b.replace("#", str(t)))
+                mm(R("PU", 40, 41), R("BO"), C("hb", 0))
+                lin(n0b, C("PU", 40), None, ntmp)
     return ops
 
 
@@ -533,11 +547,11 @@ def depend(ops):
     for i, o in enumerate(ops):
         if o["fn"] == "load" and i and o["q"] == "y":
             order[i].add(max(j for j in range(i) if ops[j]["q"] == "y"))
+        order[i].update(o["after"])
         for kind, lst in (("r", o["r"]), ("w", o["w"])):
             for x in lst:
-                nm = x["n"]
-                ps = nm[:2] == "PS"
-                for (j, k2, m) in hist.get(nm, ()):
+                ps = psum(x)
+                for (j, k2, m, p) in hist.get(x["n"], ()):
                     if j == i:
                         continue
                     same = ops[j]["q"] == o["q"]
@@ -547,18 +561,18 @@ def depend(ops):
                         order[i].add(j)
                         if m & x["m"] and not o["acc"]:
                             deps[i].add(j)
-                    elif m & x["m"] and (kind == "w" or k2 == "w"):
+                    elif m & x["m"] and (kind == "w" or k2 == "w") and p[0] < x["p"][1] and x["p"][0] < p[1]:
                         deps[i].add(j)
         for kind, lst in (("r", o["r"]), ("w", o["w"])):
             for x in lst:
                 h = hist.setdefault(x["n"], [])
-                if x["n"][:2] == "PS":
+                if psum(x):
                     if h and ops[h[-1][0]]["q"] != o["q"]:
                         h[:] = [e for e in h if ops[e[0]]["q"] == ops[h[-1][0]]["q"] and e[0] > since.get(x["n"], -1)]
                         since[x["n"]] = h[-1][0]
-                elif kind == "w":
+                elif kind == "w" and x["p"] == (0, 128):
                     h[:] = [e for e in h if e[2] & ~x["m"] or e[0] == i]
-                h.append((i, kind, x["m"]))
+                h.append((i, kind, x["m"], x["p"]))
     return deps, order
 
 
@@ -612,20 +626,6 @@ def schedule(cfg, rounds):
         var.append((ops, edges(ops, deps, order, c["wake"])))
     ops, pred = var[0]
     n = len(ops)
-    pred = [pred[i] + [(j, 0.0) for j in ops[i]["after"]] for i in range(n)]
-    topo, seen = [], [False] * n
-    for i in range(n):
-        stack = [i]
-        while stack:
-            k = stack[-1]
-            wait = [j for j, d in pred[k] if not seen[j]]
-            if wait:
-                stack.extend(wait)
-            else:
-                stack.pop()
-                if not seen[k]:
-                    seen[k] = True
-                    topo.append(k)
     cost, qs = [o["c"] for o in ops], [o["q"] for o in ops]
     succ = [[] for _ in range(n)]
     for i in range(n):
@@ -633,7 +633,7 @@ def schedule(cfg, rounds):
             succ[j].append((i, d))
     lat, nil = [o["lat"] for o in ops], [0.0] * n
     back = [0.0] * n
-    for i in topo[::-1]:
+    for i in range(n - 1, -1, -1):
         back[i] = max([back[k] + cost[k] + d for k, d in succ[i]] + [lat[i]])
     rng = np.random.default_rng(cfg["seed"])
     grp = {}
@@ -647,7 +647,7 @@ def schedule(cfg, rounds):
     for r in range(rounds):
         if r == 0:
             key = [-(back[i] + cost[i]) for i in range(n)]
-        elif r % 40 == 39:
+        elif r % 40 == 39 or r < 6:
             fw = cur[3]
             back = place(cost, qs, succ, lat, sorted(range(n), key=lambda i: (-(fw[i] + cost[i]), -i)))
             key = [-(back[i] + cost[i]) for i in range(n)]
@@ -681,12 +681,12 @@ def schedule(cfg, rounds):
                 for i in grp[int(rng.integers(len(grp)))]:
                     key[i] += sh
             if sh > 0:
-                for i in topo:
+                for i in range(n):
                     for j, d in pred[i]:
                         if key[j] >= key[i]:
                             key[i] = key[j] + 1e-6
             else:
-                for i in topo[::-1]:
+                for i in range(n - 1, -1, -1):
                     for j, d in pred[i]:
                         if key[j] >= key[i]:
                             key[j] = key[i] - 1e-6
@@ -701,14 +701,12 @@ def schedule(cfg, rounds):
     return deps, best
 
 
-CFG = {"g": 1.5, "sc": 3.8, "pe": 0.5e-3, "wake": 0.08, "net": 2.5, "look": 0.15, "xp": 24, "z16": "s" * 16,
-       "nlp": 20, "hints": [("rg#", "d2_#_0_5"), ("rg0", "nl20"), ("gkv", "gid"), ("gii", "gid"), ("gupp", "gid"), ("lau", "lvb0"),
-                            ("tb0n", "nl60"), ("oy#_0", "d2_#_1_5"), ("tb#n", "d2_#_1_10")],
-       "a2v": [((0, 14), (0, 10), (1, 14), (1, 10))] * 3,
+CFG = {"cy": 1.04e-3, "g": 1.56, "sc": 3.8, "pe": 0.52e-3, "wake": 0.1, "net": 2.0, "ld": 1.0, "xp": 32, "z16": "sv" * 8,
+       "a2": [["ssvv", "ssvv"]] * 3, "xv": (), "sx": "ssv",
        "yo": "s", "yd": "g", "yt": ["gggg", "gggg", "vvgg"],
        "c2": [[5, 5, 4, 2], [5, 5, 4, 2]], "c5": [[4, 4, 4, 4], [4, 4, 2, 4, 2]], "p5": [[16], [10, 6]],
-       "rv": [(), (), ()], "seed": 1, "rounds": 5000, "norm": [70.0, 60.0, 85.0],
-       "guess": [{}, {"g": 1.1, "sc": 2.0, "pe": 0.9e-3, "wake": 0.15, "net": 3.5}, {"g": 2.0, "sc": 5.5, "wake": 0.05}]}
+       "rv": [(), (), ()], "seed": 1, "rounds": 8000, "norm": [70.0, 65.0, 85.0],
+       "guess": [{}, {"g": 1.15, "sc": 2.2, "wake": 0.15, "net": 3.0, "ld": 1.3}, {"g": 2.0, "sc": 5.5, "wake": 0.07, "ld": 0.8}]}
 PLAN = {}
 
 
@@ -725,6 +723,8 @@ def rank_program(g, core, T, topo):
     def ap(x):
         if not isinstance(x, dict):
             return x
+        if len(SCRATCH[x["n"]][1]) == 3:
+            return T[x["n"]][:, x["a"] // 16:x["b"] // 16, :]
         v = T[x["n"]][x["p"][0]:x["p"][1], x["a"]:x["b"]:x["st"]] if x["st"] != 1 else T[x["n"]][x["p"][0]:x["p"][1], x["a"]:x["b"]]
         return v if x["off"] is None else v.indirect(ap(x["off"]))
 
@@ -742,7 +742,8 @@ def rank_program(g, core, T, topo):
                 seen[(q, nm)] = need[nm]
         fn, a = o["fn"], o["args"]
         if fn == "load":
-            Q[q].dma_start(ap(a[0]), T[a[1]][:]).then_inc(T.sem[o["sem"]], 16)
+            src = T[a[1]][:] if a[3] - a[2] == T[a[1]].shape[1] else T[a[1]][:, a[2]:a[3]]
+            Q[q].dma_start(ap(a[0]), src).then_inc(T.sem[o["sem"]], 16)
             mark[i] = (o["sem"], 16)
         elif fn == "store":
             Q[q].dma_start(T[a[0]][:, a[1]:a[2]], ap(a[3])).then_inc(T.sem[o["sem"]], 16)
@@ -773,9 +774,12 @@ def rank_program(g, core, T, topo):
                     ins = g.iota(ap(a[0]), a[1], a[2], a[3])
                 else:
                     ins = g.iota(ap(a[0]), a[1], a[2], a[3], allow_small_or_imprecise_dtypes=True)
+            elif fn == "matmul":
+                for m in a:
+                    ins = g.tensor.matmul(*[ap(x) for x in m])
             else:
                 b = [ap(x) for x in a]
-                ins = (g.affine_select(*b) if fn == "affine_select" else g.tensor.matmul(*b) if fn == "matmul" else
+                ins = (g.affine_select(*b) if fn == "affine_select" else
                        g.vector.tensor_copy(*b) if fn == "tensor_copy" else g.vector.tensor_tensor(*b) if fn == "tensor_tensor" else
                        g.vector.tensor_scalar(*b) if fn == "tensor_scalar" else g.vector.memset(*b) if fn == "memset" else
                        g.vector.tensor_tensor_scan(*b) if fn == "tensor_tensor_scan" else g.vector.tensor_reduce(*b))

@@ -1,3 +1,4 @@
+import math
 import numpy as np
 from concourse.bass import DstId, RemoteDMATransfer
 from concourse.mybir import AluOpType as A, ActivationFunctionType as F, AxisListType
@@ -18,19 +19,19 @@ SCRATCH = {
     "D2": _sb(3072, bf), "A2": _sb(3072, bf), "D5": _sb(3072, bf), "A5": _sb(3072, bf), "Z16": _sb(3072, bf),
     "EM": _sb(640, bf), "EA": _sb(2048, bf), "SH": _sb(2048, bf), "LVI": _sb(640, i32), "LVB": _sb(640, bf),
     "ZN": _sb(192, bf), "ZI": _sb(192, bf), "WI": _sb(4, i32), "KI": _sb(4, i32), "TI": _sb(4, i32), "CI": _sb(4, i32),
-    "YR": _sb(2304, bf), "YS": _sb(576, bf), "YT": _sb(576, f32), "MK": _sb(48, f32),
-    "RR": _sb(192, u16), "RH": _sb(192, f16), "OFR": _sb(12, u16), "OY": _sb(12, u16), "HX": _sb(192, u16),
-    "IDX": _sb(12, u16), "OSC": _sb(12, u16), "LAU": _sb(12, u16), "EXO": _sb(12, u16), "VN": _sb(30, u16),
+    "YR": _sb(5040, bf), "YO": _sb(192, bf), "YT": _sb(576, f32), "MK": _sb(48, f32),
+    "RR": _sb(192, u16), "RH": _sb(192, f16), "OFR": _sb(12, u16), "OY": _sb(16, u16), "HX": _sb(192, u16), "NID": _sb(128, bf),
+    "IDX": _sb(12, u16), "OSC": _sb(12, u16), "LAU": _sb(12, u16), "EXO": _sb(16, u16), "VN": _sb(30, u16),
     "WS1": _sb(144, bf), "WS2": _sb(144, bf), "WS5": _sb(144, bf), "WSV": _sb(144, bf), "WSU": _sb(144, f16),
     "WA": _sb(272, bf), "ID": _sb(128, bf), "BO": _sb(128, bf), "TRI": _sb(128, bf), "UPP": _sb(128, bf), "INC": _sb(128, bf),
     "ONE": _sb(480, bf), "M3": _sb(128, bf), "REP": _sb(128, f32), "TS": _sb(128, bf), "CE": _sb(32, f32),
-    "KA": _sb(96, bf), "KB": _sb(96, bf), "KH": _sb(96, bf), "KO": _sb(96, bf), "KX": _sb(96, f32), "M96": _sb(96, f32),
-    "KC": _sb(96, bf), "col": _sb(40, f32), "ci": _sb(16, i32), "I144": _sb(144, f32), "LT": _sb(192, bf),
+    "KA": _sb(144, bf), "KB": _sb(144, bf), "KH": _sb(144, bf), "KO": _sb(144, bf), "KX": _sb(144, f32), "M96": _sb(144, f32),
+    "KC": _sb(96, bf), "col": _sb(40, f32), "ci": _sb(16, i32), "I144": _sb(144, f32), "LT": _sb(384, bf),
     "EB": _sb(176, bf), "BJ": _sb(11, f16), "BW": _sb(7, f32), "CW": _sb(80, f32), "WT": _sb(112, bf), "a2": _sb(7, f32),
     "a3": _sb(7, f32), "FF": _sb(4272, bf), "FS": _sb(480, bf), "DEC": _sb(480, bf), "CL": _sb(480, bf),
     "LAN": _sb(12, f32), "K4": _sb(12, f32), "DK": _sb(12, f32), "ST": _sb(12, f32),
     "CS": _sb(4, f32), "NC": _sb(4, f32), "LJ": _sb(192, f32), "NR": _sb(192, f32),
-    "e1": _sb(12, i32), "e2": _sb(12, i32), "u0": _sb(12, i32), "UD": _sb(16, i32),
+    "e1": _sb(16, i32), "e2": _sb(16, i32), "u0": _sb(12, i32), "UD": _sb(16, i32),
     "uu": _sb(12, i32), "QD": _sb(16, i32), "KU": _sb(192, f32), "HS": _sb(192, i32), "HA": _sb(192, i32),
     "KEY": _sb(12, i32), "FK": _sb(36, bf), "k2": _sb(12, i32), "k3": _sb(12, f32), "k4": _sb(12, i32),
     "k5": _sb(12, i32), "k6": _sb(12, f32), "k7": _sb(12, f32), "k8": _sb(12, f32),
@@ -42,7 +43,7 @@ for _k in ("PA", "PB"):
 for _k in ("PC", "PD", "PU", "PT", "PX", "PY"):
     SCRATCH[_k] = ("psum", [128, 512], f32)
 NDMA = 28
-SEMAPHORES = ["qv", "qs", "qp", "qg", "sent"] + ["d%d" % _k for _k in range(NDMA)] + ["arr%d" % _k for _k in range(6)]
+SEMAPHORES = ["qv", "qs", "qp", "qg", "sent"] + ["d%d" % _k for _k in range(NDMA)] + ["arr%d" % _k for _k in range(9)]
 TWO = (bf, f16, u16)
 
 
@@ -74,7 +75,7 @@ def IND(win, off):
 
 
 def build(rank, cfg):
-    ops, ph, cy = [], ["load"], cfg["cy"]
+    ops, ph, cy, lab, now = [], ["load"], cfg["cy"], {}, [-1]
 
     def add(q, fn, args, reads, writes, cost, lat=0.0, acc=False, sem=None):
         rd = []
@@ -90,6 +91,8 @@ def build(rank, cfg):
                 rd.append(w["off"])
         ops.append({"q": q, "fn": fn, "args": args, "r": rd, "w": wr, "c": cost, "lat": lat, "acc": acc, "sem": sem, "ph": ph[0],
                     "after": []})
+        if wr:
+            lab.setdefault((q, wr[0]["n"][:2], now[0]), []).append(len(ops) - 1)
 
     def two(*v):
         return all(SCRATCH[x["n"]][2] in TWO for x in v)
@@ -141,16 +144,16 @@ def build(rank, cfg):
         else:
             add("p", "matmul", [(out, l, r, start, stop)], [l, r], [out], c, acc=not start)
 
-    tail = {}
+    tail, nc = {}, [0]
 
     def chain(k):
         if k in tail:
             ops[-1]["after"].append(tail[k])
         tail[k] = len(ops) - 1
 
-    def put(out, ws, src, a, b, first=True):
+    def put(out, ws, src, a, b, first=True, stop=True):
         for r in range(16):
-            mm(out, R(ws, 15 - r, 143 - r), R(src, a + r, b, 16), first and r == 0, r == 15)
+            mm(out, R(ws, 15 - r, 143 - r), R(src, a + r, b, 16), first and r == 0, stop and r == 15)
 
     def iota(out, pat, base, cm):
         add("g", "iota", (out, pat, base, cm), [], [out], 0.15 + out["k"] * 2 * cy)
@@ -189,7 +192,7 @@ def build(rank, cfg):
 
     ph[0] = "c0"
     (pm, mk0, c96, mlo, mhi, pm4, m15, dec, clo, chi, wv, fo, wsg, kva, kvb, kvh, thr, cap, nn, n0b, hq, ntmp, x0c, x1c,
-     c15, pm2) = [C("col", k) for k in range(26)]
+     c15, pm2, c48) = [C("col", k) for k in range(27)]
     pi = C("ci", 1)
     iota(C("ci", 0), [[0, 1]], 0, 1)
     ts(pi, C("ci", 0), 15, A.bitwise_and)
@@ -199,10 +202,12 @@ def build(rank, cfg):
     iota(R("I144"), [[-1, 144]], 15, 1)
     ts(R("WS1"), R("I144"), pm, A.is_equal)
     sel(R("ID"), R("ONE", 0, 128), [[-1, 128]], A.is_equal, 0, 1)
-    sel(R("BO"), R("ONE", 0, 128), [[-16, 8], [0, 16]], A.is_ge, 0, 1)
-    sel(R("BO"), R("BO"), [[16, 8], [0, 16]], A.is_ge, 15, -1)
-    sel(R("INC"), R("BO"), [[1, 128]], A.is_ge, 0, -1)
-    sel(R("INC"), R("INC"), [[0, 8], [1, 16]], A.not_equal, -15, 0)
+    lin(hq, pm, -1.0, 7.5)
+    act(R("BO"), R("I144", 15, 143), F.Abs, hq)
+    ts(R("BO"), R("BO"), 8.0, A.is_lt)
+    lin(ntmp, pm, -0.5, 7.0)
+    act(R("INC"), R("I144", 15, 143), F.Abs, ntmp)
+    ts(R("INC"), R("INC"), ntmp, A.is_le)
     ts(m15, pi, 15.0, A.is_equal, 4096.0, A.mult)
     lin(dec, m15, None, -4096.0)
     lin(clo, m15, -256.0, -4096.0)
@@ -221,14 +226,20 @@ def build(rank, cfg):
     ms(R("EB", 0, 96), 0.0, "v")
     ms(R("FF", 0, 480), -32768.0, "v")
     ph[0] = "c2"
-    iota(R("LT", 0, 96), [[4, 16], [1, 2], [64, 3]], 0, 0)
-    iota(R("LT", 96, 192), [[0, 16], [1, 6]], 0, 0)
+    P2, P5, YW = cfg["P2"], cfg["P5"], 1680
+    KW = {n: 0 if n == len(P5[0]) else 48 * len(P5[0]) for n in set(len(cl) for cl in P5)}
+    iota(R("LT", 0, 96), [[4, 16], [1, 2], [64, 3]] if len(P2[0]) == 2 else [[1, 2], [4, 16], [64, 3]], 0, 0)
+    iota(R("LT", 96, 192), [[1, 2], [4, 16], [64, 3]], 2, 0)
+    for cl in P5:
+        iota(R("LT", 192 + 48 * cl[0], 240 + 48 * cl[-1]), [[0, 16], [1, 3 * len(cl)]], 3 * cl[0], 0)
     put(R("PX", 0, 12), "WS1", "LT", 0, 192)
-    ts(R("LAN", 0, 6), R("PX", 0, 6), 1.0 / 16, A.mult)
-    ts(R("LAN", 6, 12), R("PX", 0, 6), 1.0 / 16, A.mult, 2.0, A.add)
-    ts(R("EXO", 0, 6), R("PX", 6, 12), 1.0 / 16, A.mult)
-    ts(R("EXO", 6, 12), R("PX", 6, 12), 1.0 / 16, A.mult, 6.0, A.add)
-    cp(R("LAU"), R("LAN"))
+    ts(R("LAU"), R("PX", 0, 12), 1.0 / 16, A.mult)
+    ts(R("LAN"), R("PX", 0, 12), 1.0 / 16, A.mult)
+    ph[0] = "c2b"
+    put(R("PY", 0, 12), "WS1", "LT", 192, 384)
+    for cl in P5:
+        ts(R("EXO", 4 * cl[0], 4 * cl[0] + 3 * len(cl)), R("PY", 3 * cl[0], 3 * cl[-1] + 3), 1.0 / 16, A.mult)
+    ph[0] = "c2"
     act(R("ZI"), IND(R("ZN"), R("LAU")), F.Copy)
     for k in range(16):
         copy(cfg["z16"][k], R("Z16", k, 3072, 16), R("ZI"))
@@ -280,7 +291,10 @@ def build(rank, cfg):
         ts(R("EM", 128 * o, 128 * o + 128), R("ID"), fo, A.mult, o + 1.0, A.is_equal)
     for a in range(16):
         ph[0] = "ea%d" % (a // 4)
-        sel(R("EA", 128 * a, 128 * a + 128), R("ID"), [[0, 8], [1, 16]], A.is_equal, -a, 0)
+        if a < cfg["ea"]:
+            sel(R("EA", 128 * a, 128 * a + 128), R("ID"), [[0, 8], [1, 16]], A.is_equal, -a, 0)
+        else:
+            ts(R("EA", 128 * a, 128 * a + 128), R("ID"), pm, A.mult, float(a), A.is_equal)
     ph[0] = "sh"
     iota(R("TS"), [[32, 8], [1, 16]], -1, 0)
     sel(R("TS"), R("TS"), [[-16, 8], [0, 16]], A.is_ge, 0, 1, -100.0)
@@ -296,6 +310,8 @@ def build(rank, cfg):
     ts(mlo, pi, 8.0, A.is_lt)
     ts(mhi, pi, 8.0, A.is_ge)
     lin(c96, pm, 96.0, None)
+    lin(c48, pm, 48.0, None)
+    lin(R("NID"), R("ID"), -1.0, None)
     lin(pm4, pm, -4.0, None)
     lin(R("WS2"), R("WS1"), 128.0, None)
     lin(R("WS5"), R("WS1"), -32768.0, None)
@@ -330,17 +346,19 @@ def build(rank, cfg):
     cp(R("col", 14, 16), R("ci", 4, 6))
     lin(c15, pm, -2048.0, 30720.0)
     lin(kva, c15, None, kvh)
-    iota(R("M96"), [[1, 16], [0, 6]], 0, 0)
-    ts(R("KA"), R("M96"), pm, A.is_equal, kva, A.mult)
-    ts(R("KB"), R("M96"), pm, A.is_equal, kvb, A.mult)
-    ts(R("KH"), R("M96"), pm, A.is_equal, kvh, A.mult)
-    mm(R("PY", 256, 352), R("BO"), R("KH"), True, False)
-    mm(R("PY", 256, 352), R("BO"), R("KB"), False, True)
-    lin(R("KX"), R("PY", 256, 352), None, None)
-    iota(R("REP", p=(0, 8)), [[1, 8], [0, 16]], 0, -1)
-    ts(R("REP", p=(0, 8)), R("REP", p=(0, 8)), 0.0, A.is_equal)
-    cp(R("TC", 0, 1, p=(0, 8)), R("TI", 0, 1, p=(0, 8)))
-    cp(R("TC", 1, 2, p=(0, 8)), R("CI", 0, 1, p=(0, 8)))
+    for n, k0 in KW.items():
+        iota(R("M96", k0, k0 + 48 * n), [[1, 16], [0, 3 * n]], 0, 0)
+    kw = 48 * sum(KW)
+    ts(R("M96", 0, kw), R("M96", 0, kw), pm, A.is_equal)
+    lin(R("KA", 0, kw), R("M96", 0, kw), kva, None)
+    lin(R("KB", 0, kw), R("M96", 0, kw), kvb, None)
+    lin(R("KH", 0, kw), R("M96", 0, kw), kvh, None)
+    mm(R("PY", 256, 256 + kw), R("BO"), R("KH", 0, kw), True, False)
+    mm(R("PY", 256, 256 + kw), R("BO"), R("KB", 0, kw), False, True)
+    lin(R("KX", 0, kw), R("PY", 256, 256 + kw), None, None)
+    sel(R("REP", p=(0, 8)), R("ONE", 0, 128, p=(0, 8)), [[1, 8], [0, 16]], A.is_equal, 0, -1)
+    copy("g", R("TC", 0, 1, p=(0, 8)), R("TI", 0, 1, p=(0, 8)))
+    copy("g", R("TC", 1, 2, p=(0, 8)), R("CI", 0, 1, p=(0, 8)))
     mm(R("PY", 400, 402), R("REP", p=(0, 8)), R("TC", p=(0, 8)))
     lin(thr, C("PY", 400), -32768.0, 505.0 * 32768)
     lin(cap, C("PY", 401), None, None)
@@ -369,11 +387,14 @@ def build(rank, cfg):
             for k, (e, o, a) in enumerate(ms_):
                 mm(R("PT", s0 + s2, s1, per), R(e, 128 * o, 128 * o + 128), cols(T, a, s2, s0, s1), k == 0, k == len(ms_) - 1)
         ts(R(tb, s0, s1), R("PT", s0, s1), float(OFS), A.add)
-        for s in range(s0, s1, cfg["xp"]):
-            e = min(s1, s + cfg["xp"])
+        n = cfg["xp"][s0 > 0]
+        cut = [s0 + (s1 - s0) * k // (2 * n) * 2 for k in range(n + 1)]
+        for k in range(n):
+            s, e, q = cut[k], cut[k + 1], "v" if (t, s0 > 0, k) in cfg["xv"] else "s"
             ph[0] = "xt%d_%d_%d" % (t, s0, s // 72)
-            copy("v" if (t, s) in cfg["xv"] else "s", R(xt, 16 * s, 16 * e), IND(R("XW", 0, nb), R(tb, s, e)))
-            chain("x")
+            copy(q, R(xt, 16 * s, 16 * e), IND(R("XW", 0, nb), R(tb, s, e)))
+            lab.setdefault((q, "XN" if s0 else "XO", t), []).append(len(ops) - 1)
+            chain("x%d" % (s0 > 0))
 
     def tails(t):
         T = T0 + P * t
@@ -394,17 +415,19 @@ def build(rank, cfg):
 
     for t in range(RO):
         T, nb, xt, last = T0 + P * t, NB + P * t, "XT%d" % (t % 2), t == RO - 1
-        ph[0] = "rr%d" % t
+        ph[0], now[0] = "rr%d" % t, t
         if t:
             cp(R("RR"), IND(R("NL", 0, 672), R("OFR")))
         table(t, split(t) if t else 0, 256, nb)
-        for h in range(2):
-            r0, key = 0, R(("PA", "PB")[h], 0, 96)
+        home = {c: YW * t + 384 * h + 384 - 48 * (len(cl) - k) for h, cl in enumerate(P5) for k, c in enumerate(cl)}
+        for h, cl in enumerate(P2):
+            r0, w, d0 = 0, 48 * len(cl), 768 * cl[0]
+            key = R(("PA", "PB")[h % 2], 128 * (h // 2), 128 * (h // 2) + w)
             ph[0] = "g2_%d_%d_0" % (t, h)
-            mm(key, R("ID"), R("KC"), True, False)
+            mm(key, R("ID"), R("KC", 0, w), True, False)
             for n, q in zip(cfg["c2"][h], cfg["a2"][t][h]):
                 ph[0] = "g2_%d_%d_%d" % (t, h, r0 // 8)
-                a, b = 1536 * h + 96 * r0, 1536 * h + 96 * (r0 + n)
+                a, b = d0 + w * r0, d0 + w * (r0 + n)
                 tt(R("D2", a, b), IND(R("XW", 0, nb), R("RR", a // 16, b // 16)), R("Z16", a, b), A.subtract)
                 chain("d")
                 if q == "v":
@@ -412,30 +435,30 @@ def build(rank, cfg):
                 else:
                     act(R("A2", a, b), R("D2", a, b), F.Relu, None, -1.0)
                 for r in range(r0, r0 + n):
-                    a = 1536 * h + 96 * r
-                    mm(key, R("WS2", 15 - r, 143 - r), R("A2", a, a + 96), False, r == 15)
+                    mm(key, R("WS2", 15 - r, 143 - r), R("A2", d0 + w * r, d0 + w * r + w), False, r == 15)
                 r0 += n
-            c0, c1 = 6 * h, 6 * h + 6
+            c0 = 4 * cl[0]
+            c1 = c0 + w // 16
             ph[0] = "p2_%d_%d" % (t, h)
             red(R("e1", c0, c1), key, A.min)
             ts(R("e2", c0, c1), R("e1", c0, c1), 127, A.bitwise_and)
-            ts(R("OY", c0, c1), R("e2", c0, c1), c96, A.add)
-            y0 = 192 * t + 96 * h
-            act(R("YS", y0, y0 + 96), IND(R("D2", 1536 * h, 1536 * h + 1536), R("OY", c0, c1)), F.Abs)
-            yr = 768 * t + 384 * h
-            cl = [0, 1] if h == 0 else [2]
-            tr = [(R("YS", y0 + 48 * k, y0 + 48 * k + 48), R("YR", yr + 48 * k, yr + 48 * k + 48),
-                   (rank + 1 + (t + c) % (N - 1)) % N) for k, c in enumerate(cl)]
-            add("g", "send", (tr, "arr%d" % (2 * t + h)), [x[0] for x in tr], [x[1] for x in tr], 0.3, lat=cfg["net"],
-                sem="arr%d" % (2 * t + h))
-            if h == 1:
-                copy(cfg["yo"], R("YR", yr + 48, yr + 96), R("YS", y0 + 48, y0 + 96))
+            ts(R("OY", c0, c1), R("e2", c0, c1), c48 if w == 48 else c96, A.add)
+            y0 = home[3] if cl == (3,) else YW * t + 1536 + 48 * cl[0]
+            act(R("YR", y0, y0 + w), IND(R("D2", d0, d0 + 16 * w), R("OY", c0, c1)), F.Abs)
+            if cl != (3,):
+                tr = [(R("YR", y0 + 48 * k, y0 + 48 + 48 * k), R("YR", home[c], home[c] + 48),
+                       (rank + 1 + (t + c) % (N - 1)) % N) for k, c in enumerate(cl)]
+                add("g", "send", (tr, "arr%d" % (3 * t + h)), [x[0] for x in tr], [x[1] for x in tr], 0.3,
+                    lat=cfg["net"] + cfg["net2"] * (len(cl) - 1), sem="arr%d" % (3 * t + h))
+                chain("y")
         ph[0] = "rh%d" % t
         ts(R("RH"), R("RR"), -float(OFS), A.add)
-        for c in range(12):
-            i0 = 96 * (c // 6) + c % 6
-            mm(R("PT", 256 + 16 * c, 272 + 16 * c), R("SH", 0, 128), R("RH", i0, i0 + 91, 6))
-        lin(R("RT", 4096, 4288), R("PT", 256, 448), None, C("col", 30 + t))
+        for cl in P2:
+            st = 3 * len(cl)
+            for c in range(3 * cl[0], 3 * cl[0] + st):
+                i0 = 48 * cl[0] + c - 3 * cl[0]
+                mm(R("PD", 256 + 16 * c, 272 + 16 * c), R("SH", 0, 128), R("RH", i0, i0 + 15 * st + 1, st))
+        lin(R("RT", 4096, 4288), R("PD", 256, 448), None, C("col", 30 + t))
         tails(t)
         if not last:
             table(t + 1, 0, split(t + 1), nb)
@@ -444,73 +467,106 @@ def build(rank, cfg):
             if t:
                 lin(R("TO"), R("LAN"), None, n0b)
             lin(ntmp, nn, None, -48.0)
-        for h in range(2):
-            yr, c0, c1, w0, key = 768 * t + 384 * h, 6 * h, 6 * h + 6, 96 * h, ("PC", "PD")[h]
-            y = R("YR", yr, yr + 96)
+        for h, cl in enumerate(P5):
+            w, nw, yr, key = 48 * len(cl), 3 * len(cl), YW * t + 384 * h, ("PC", "PD")[h % 2]
+            c0, w0, d0, k0, e0, s0 = 3 * cl[0], 48 * cl[0], 768 * cl[0], KW[len(cl)], 4 * cl[0], 96 * (h // 2)
+            c1, y = c0 + nw, R("YR", yr + 384 - w, yr + 384)
             ph[0] = "u%d_%d" % (t, h)
-            put(R("PU", c0, c1), "WSU", "YR", yr, yr + 96)
-            copy(cfg["yd"], R("YR", yr + 96, yr + 192), y)
-            copy(cfg["yd"], R("YR", yr + 192, yr + 384), R("YR", yr, yr + 192))
-            copy(cfg["yd"], R(xt, 4096 + w0, 4192 + w0), y)
+            put(R("PU", c0, c1), "WSU", "YR", yr + 384 - w, yr + 384)
+            n = w
+            while n < 384:
+                copy(cfg["yd"], R("YR", yr + 384 - 2 * n, yr + 384 - n), R("YR", yr + 384 - n, yr + 384))
+                n *= 2
+            copy(cfg["yd"], R(xt, 4096 + w0, 4096 + w0 + w), y)
+            if cfg["sx"][t] == "v":
+                copy(cfg["yd"], R("YO", w0, w0 + w), y)
             cp(R("u0", c0, c1), R("PU", c0, c1))
             ts(R("UD", c0, c1), R("u0", c0, c1), 4095, A.bitwise_and)
             tt(R("uu", c0, c1), R("UD", c0, c1), R("UD", c0, c1), A.mult)
-            tt(R("KU", w0, w0 + 96), IND(R("UD"), R("EXO", c0, c1)), R("KX"), A.mult)
+            tt(R("KU", w0, w0 + w), IND(R("UD"), R("EXO", e0, e0 + nw)), R("KX", k0, k0 + w), A.mult)
             ts(R("QD", c0, c1), R("uu", c0, c1), 5, A.logical_shift_right)
-            tt(R("HS", w0, w0 + 96), IND(R("QD"), R("EXO", c0, c1)), R("KU", w0, w0 + 96), A.add)
-            ts(R("HA", w0, w0 + 96), R("HS", w0, w0 + 96), 4095, A.bitwise_and)
-            cp(R("HX", w0, w0 + 96), R("HA", w0, w0 + 96))
+            tt(R("HS", w0, w0 + w), IND(R("QD"), R("EXO", e0, e0 + nw)), R("KU", w0, w0 + w), A.add)
+            ts(R("HA", w0, w0 + w), R("HS", w0, w0 + w), 4095, A.bitwise_and)
+            cp(R("HX", w0, w0 + w), R("HA", w0, w0 + w))
             m0 = 0
-            for n in cfg["c5"][h]:
-                ph[0] = "g5_%d_%d_%d" % (t, h, m0 // 8)
-                a, b = 1536 * h + 96 * m0, 1536 * h + 96 * (m0 + n)
-                tt(R("D5", a, b), IND(R(xt, 0, 4096), R("HX", a // 16, b // 16)), R("YR", yr, yr + 96 * n), A.subtract)
-                chain("d")
-                act(R("A5", a, b), R("D5", a, b), F.Abs)
-                chain("a")
+            for n, q in zip(cfg["c5"][h], cfg["a5"][t][h]):
+                ph[0] = "g5_%d_%d_%d" % (t, h, m0)
+                a, b = d0 + w * m0, d0 + w * (m0 + n)
+                src, ys = IND(R(xt, 0, 4096), R("HX", a // 16, b // 16)), R("YR", yr + 384 - w * n, yr + 384)
+                if q == "c":
+                    act(R("D5", a, b), src, F.Copy)
+                    chain("c")
+                    o = R(("PA", "PB")[nc[0] % 2], 0, w * n)
+                    nc[0] += 1
+                    mm(o, R("NID"), ys, True, False)
+                    mm(o, R("ID"), R("D5", a, b), False, True)
+                    act(R("A5", a, b), o, F.Abs)
+                else:
+                    tt(R("D5", a, b), src, ys, A.subtract)
+                    chain("d")
+                    act(R("A5", a, b), R("D5", a, b), F.Abs)
+                    chain("a")
                 m0 += n
             m0 = 0
             for n in cfg["p5"][h]:
                 ph[0] = "p5_%d_%d_%d" % (t, h, m0)
-                o = R(key, 6 * m0, 6 * (m0 + n))
+                o = R(key, s0 + nw * m0, s0 + nw * (m0 + n))
                 for k, nm in enumerate(("KA", "KB", "KO")):
-                    mm(o, R("BO"), R(nm, 6 * m0, 6 * (m0 + n)), k == 0, False)
-                put(o, "WS5", "A5", 1536 * h + 96 * m0, 1536 * h + 96 * (m0 + n), False)
+                    mm(o, R("BO"), R(nm, k0 + nw * m0, k0 + nw * (m0 + n)), k == 0, False)
+                ph[0] += "a"
+                put(o, "WS5", "A5", d0 + w * m0, d0 + w * (m0 + n), False)
                 m0 += n
-            for c in range(6):
-                red(C("KEY", c0 + c), R(key, c, 96, 6), A.max)
+            for c in range(nw):
+                red(C("KEY", c0 + c), R(key, s0 + c, s0 + w, nw), A.max)
         ph[0] = "b%d" % t
         mk = 16 * t
         for c in range(4):
             ts(R("FK", 12 * t + c, 12 * t + 12, 4), R("KEY", 3 * c, 3 * c + 3), thr, A.is_ge, 1.0 if c < 3 else -1.0, A.mult)
-        for c in range(12 * t + 12):
-            ph[0] = "b%d%s" % (t, "" if c >= 12 * t else "o")
+        for c in sorted(range(12 * t + 12), key=lambda c: (c // 12, c % 4 in P5[-1])):
+            ph[0] = "b%d%s" % (t, "o" if c < 12 * t else "" if c % 4 in P5[-1] else "h")
             mm(C("PU", 16), R("ONE", 0, 128) if c % 4 < 3 else R("M3"), C("FK", c), c == 0, c == 12 * t + 11)
         ts(R("MK", mk, mk + 12), R("FK", 12 * t, 12 * t + 12), C("PU", 16), A.mult, cap, A.is_le)
         for c in range(3):
             store("ysy"[c] if last else "y", "ya", 192 * t + 64 * c, 192 * t + 64 * c + 64, R("MK", mk + 4 * c, mk + 4 * c + 4))
         ph[0] = "k%d" % t
-        ts(R("k2"), R("KEY"), 2047, A.bitwise_and)
-        tt(R("k3"), R("k2"), R("UD", 0, 12), A.mult)
-        tt(R("k4"), R("k3"), R("QD", 0, 12), A.add)
-        ts(R("k5"), R("k4"), 4095, A.bitwise_and)
-        ts(R("k6"), R("KEY"), thr, A.is_lt)
-        tt(R("k7"), R("k6"), R("K4"), A.mult)
-        tt(R("k8"), R("k5"), R("k7"), A.max)
-        cp(R("IDX"), R("k8"))
+        for a, b, thin in cfg["kk"]:
+            ts(R("k2", a, b), R("KEY", a, b), 2047, A.bitwise_and)
+            ts(R("k6", a, b), R("KEY", a, b), thr, A.is_lt)
+            tt(R("k7", a, b), R("k6", a, b), R("K4", a, b), A.mult)
+            if thin:
+                cp(R("k3", a, b), R("UD", a, b))
+                cp(R("k8", a, b), R("QD", a, b))
+                for c in range(a, b):
+                    ts(C("k4", c), C("k2", c), C("k3", c), A.mult, C("k8", c), A.add)
+                ts(R("k5", a, b), R("k4", a, b), 4095, A.bitwise_and)
+                for c in range(a, b):
+                    ts(C("IDX", c), C("k5", c), C("k7", c), A.max)
+            else:
+                tt(R("k3", a, b), R("k2", a, b), R("UD", a, b), A.mult)
+                tt(R("k4", a, b), R("k3", a, b), R("QD", a, b), A.add)
+                ts(R("k5", a, b), R("k4", a, b), 4095, A.bitwise_and)
+                tt(R("k8", a, b), R("k5", a, b), R("k7", a, b), A.max)
+                cp(R("IDX", a, b), R("k8", a, b))
         tt(R("NR"), IND(R("RT"), R("IDX")), R("LJ"), A.add)
         if cfg["sx"][t] == "v":
-            for h in range(2):
-                yr = 768 * t + 384 * h
-                tt(R("SX", 96 * h, 96 * h + 96), IND(R(xt), R("IDX", 6 * h, 6 * h + 6)), R("YR", yr, yr + 96), A.add)
-            lin(R("SY"), R("SX"), 0.5, 127.75)
+            tt(R("SX"), IND(R(xt), R("IDX")), R("YO"), A.add)
+            sx = R("SX")
         else:
             act(R("SX"), IND(R(xt), R("IDX")), F.Copy)
-            mm(R("PT", 256, 448), R("ID"), R(xt, 4096, 4288), True, False)
-            mm(R("PT", 256, 448), R("ID"), R("SX"), False, True)
-            lin(R("SY"), R("PT", 256, 448), 0.5, 127.75)
-        for c in range(4):
-            lin(R("XW", nb + c, nb + 192, 4), R("SY", 48 * c, 48 * c + 48), None, -128.0)
+            sx = R("PC", 256, 448)
+            mm(sx, R("ID"), R(xt, 4096, 4288), True, False)
+            mm(sx, R("ID"), R("SX"), False, True)
+        if cfg["sy"][t] == "s":
+            lin(R("SY"), sx, 0.5, 127.75)
+            for c in range(4):
+                if last and c % 2:
+                    ts(R("XW", nb + c, nb + 192, 4), R("SY", 48 * c, 48 * c + 48), -128.0, A.add)
+                else:
+                    lin(R("XW", nb + c, nb + 192, 4), R("SY", 48 * c, 48 * c + 48), None, -128.0)
+        else:
+            ts(R("HA"), sx, 0.5, A.mult, -0.25, A.add)
+            for c in range(4):
+                copy("g", R("XW", nb + c, nb + 192, 4), R("HA", 48 * c, 48 * c + 48))
         for c in range(4):
             copy(cfg["yt"][t][c], R("YT", 192 * t + c, 192 * t + 192, 4), R("NR", 48 * c, 48 * c + 48))
         store("s" if last else "y", "yx", 192 * t, 192 * t + 192, R("XW", nb, nb + 192))
@@ -536,6 +592,16 @@ def build(rank, cfg):
                 ts(C("hb", 0), C("JB", 7), mhi, A.mult, hq, A.add)
                 mm(R("PU", 40, 41), R("BO"), C("hb", 0))
                 lin(n0b, C("PU", 40), None, ntmp)
+    for q, lines in cfg["order"]:
+        prev = None
+        for t in range(RO):
+            for w in lines[min(t, len(lines) - 1)].split():
+                nm, k = w.rstrip("-+").split(".")
+                ids = lab.get((q, nm, t - w.count("-") + w.count("+")), [])
+                if int(k) < len(ids):
+                    if prev is not None:
+                        ops[ids[int(k)]]["after"].append(prev)
+                    prev = ids[int(k)]
     return ops
 
 
@@ -602,17 +668,20 @@ def place(cost, qs, pred, tail, rank):
     return start
 
 
-def replay(ops, pred, seq):
-    free, fin, end = {q: 0.0 for q in "vspgy"}, [0.0] * len(ops), 0.0
-    for i in seq:
-        o = ops[i]
-        t = free[o["q"]]
+def replay(ops, pred, seq, a, fin):
+    cost, qs, stores = ops
+    free, k = {}, a - 1
+    while k >= 0 and len(free) < 5:
+        free.setdefault(qs[seq[k]], fin[seq[k]])
+        k -= 1
+    for i in seq[a:]:
+        t = free.get(qs[i], 0.0)
         for j, d in pred[i]:
             if fin[j] + d > t:
                 t = fin[j] + d
-        fin[i] = free[o["q"]] = t + o["c"]
-        end = max(end, fin[i] + o["lat"])
-    return end
+        fin[i] = free[qs[i]] = t + cost[i]
+    end, last = max((fin[i] + d, i) for i, d in stores)
+    return end, fin, last
 
 
 def schedule(cfg, rounds):
@@ -623,90 +692,116 @@ def schedule(cfg, rounds):
         ops = build(0, c)
         if not var:
             deps, order = depend(ops)
-        var.append((ops, edges(ops, deps, order, c["wake"])))
-    ops, pred = var[0]
+        var.append((([o["c"] for o in ops], [o["q"] for o in ops], [(i, o["lat"]) for i, o in enumerate(ops) if o["fn"] == "store"]),
+                    edges(ops, deps, order, c["wake"])))
+    ops = build(0, cfg)
+    (cost, qs, stores), pred = var[0]
     n = len(ops)
-    cost, qs = [o["c"] for o in ops], [o["q"] for o in ops]
     succ = [[] for _ in range(n)]
     for i in range(n):
         for j, d in pred[i]:
             succ[j].append((i, d))
+    left, topo = [len(p) for p in pred], [i for i in range(n) if not pred[i]]
+    for j in topo:
+        for i, d in succ[j]:
+            left[i] -= 1
+            if not left[i]:
+                topo.append(i)
+    assert len(topo) == n
     lat, nil = [o["lat"] for o in ops], [0.0] * n
     back = [0.0] * n
-    for i in range(n - 1, -1, -1):
+    for i in topo[::-1]:
         back[i] = max([back[k] + cost[k] + d for k, d in succ[i]] + [lat[i]])
-    rng = np.random.default_rng(cfg["seed"])
-    grp = {}
-    for i, o in enumerate(ops):
-        nm = o["w"][0]["n"] if o["w"] else "st"
-        grp.setdefault(o["ph"], []).append(i)
-        grp.setdefault((o["ph"], o["q"]), []).append(i)
-        grp.setdefault((o["ph"], nm), []).append(i)
-    grp = list(grp.values())
-    best, cur = None, None
+    rank = {i: k for k, i in enumerate(topo)}
+    best, floor = None, list(nil)
+    fill = [o["ph"][:2] in cfg["fill"] for o in ops]
+    core = [i for i in range(n) if not fill[i]]
+
+    def worth(fins):
+        fin = fins[0][1]
+        return sum(f[0] / s for f, s in zip(fins, cfg["norm"])) + cfg["early"] * sum([fin[i] for i in core]) / len(core)
+
+    lean = [p if fill[i] else [(j, d) for j, d in p if not fill[j]] for i, p in enumerate(pred)]
+    for r in range(cfg["passes"]):
+        fw = place(cost, qs, lean, floor, sorted(range(n), key=lambda i: (fill[i], -(back[i] + cost[i]), rank[i])))
+        key = list(fw)
+        for i in topo:
+            key[i] = max([key[i]] + [key[j] + 1e-6 for j, d in pred[i]])
+        seq = sorted(range(n), key=lambda i: (key[i], rank[i]))
+        fins = [replay(o, p, seq, 0, [0.0] * n) for o, p in var]
+        val = worth(fins)
+        if best is None or val < best[0]:
+            best = (val, seq, fins)
+        for i in range(n):
+            late = max([fw[j] + cost[j] + d for j, d in pred[i] if fill[j]] + [0.0])
+            if not fill[i] and late > fw[i]:
+                floor[i] = fw[i] + cfg["step"] * (late - fw[i])
+    cur, arcs = best, None
+    before, after = [set(j for j, d in p) for p in pred], [set(i for i, d in s) for s in succ]
+    rnd = np.random.default_rng(cfg["seed"]).random((rounds, 6)).tolist()
     for r in range(rounds):
-        if r == 0:
-            key = [-(back[i] + cost[i]) for i in range(n)]
-        elif r % 40 == 39 or r < 6:
-            fw = cur[3]
-            back = place(cost, qs, succ, lat, sorted(range(n), key=lambda i: (-(fw[i] + cost[i]), -i)))
-            key = [-(back[i] + cost[i]) for i in range(n)]
-        else:
-            key = list(cur[3])
-            sh = float(rng.choice([-1.0, 1.0])) * float(rng.choice([0.3, 1.0, 2.5, 6.0])) * (0.3 + float(rng.random()))
-            arcs = []
-            if r % 3:
-                fw, prev, lastq = cur[3], [-1] * n, {}
-                for i in cur[1]:
-                    prev[i] = lastq.get(qs[i], -1)
-                    lastq[qs[i]] = i
-                i = max(range(n), key=lambda k: fw[k] + cost[k] + lat[k])
+        val, seq, fins = cur
+        if arcs is None:
+            arcs, pos, prev, lastq = [], [0] * n, [-1] * n, {}
+            for k, i in enumerate(seq):
+                pos[i], prev[i], lastq[qs[i]] = k, lastq.get(qs[i], -1), i
+            for (o, p), (end, fin, i) in zip(var, fins):
                 while i >= 0:
-                    nx = -1
-                    for j, d in pred[i]:
-                        if fw[j] + cost[j] + d > fw[i] - 1e-9:
+                    t, nx = fin[i] - o[0][i] - 1e-9, -1
+                    for j, d in p[i]:
+                        if fin[j] + d > t:
                             nx = j
-                    if nx < 0 and prev[i] >= 0 and fw[prev[i]] + cost[prev[i]] > fw[i] - 1e-9:
+                    if nx < 0 and prev[i] >= 0 and fin[prev[i]] > t:
                         nx = prev[i]
                         arcs.append((nx, i))
                     i = nx
-            if arcs:
-                j, i = arcs[int(rng.integers(len(arcs)))]
-                far = float(rng.choice([0.0, 0.0, 0.3, 1.0]))
-                if sh < 0:
-                    key[i] = key[j] - 1e-4 - far
-                else:
-                    key[j] = key[i] + 1e-4 + far
+        x = rnd[r]
+        j, i = arcs[int(x[0] * len(arcs))]
+        if x[5] < cfg["any"]:
+            i = int(x[0] * n)
+            j = prev[i]
+            if j < 0:
+                continue
+        far = int(x[1] * (1, 1, 1, 4, 11, 31, 81)[int(x[2] * 7)])
+        if x[3] < 0.5:
+            a, b, lead, links, step = max(0, pos[j] - far), pos[i], i, before, -1
+        else:
+            a, b, lead, links, step = pos[j], min(n - 1, pos[i] + far), j, after, 1
+        tied, move, rest = set(links[lead]), [lead], []
+        for k in seq[a:b + 1][::step][1:]:
+            if k in tied:
+                move.append(k)
+                tied |= links[k]
             else:
-                for i in grp[int(rng.integers(len(grp)))]:
-                    key[i] += sh
-            if sh > 0:
-                for i in range(n):
-                    for j, d in pred[i]:
-                        if key[j] >= key[i]:
-                            key[i] = key[j] + 1e-6
-            else:
-                for i in range(n - 1, -1, -1):
-                    for j, d in pred[i]:
-                        if key[j] >= key[i]:
-                            key[j] = key[i] - 1e-6
-        fw = place(cost, qs, pred, nil, sorted(range(n), key=lambda i: (key[i], i)))
-        seq = sorted(range(n), key=lambda i: (fw[i], i))
-        val = [replay(o, p, seq) for o, p in var]
-        score = sum(v / s for v, s in zip(val, cfg["norm"]))
-        if cur is None or score < cur[0] + 0.012 * (1 - r / rounds) * float(rng.random()):
-            cur = (score, seq, val, fw)
-        if best is None or score < best[0]:
-            best = (score, seq, val, fw)
+                rest.append(k)
+        if not rest:
+            continue
+        new = seq[:a] + (rest + move if step == 1 else move[::-1] + rest[::-1]) + seq[b + 1:]
+        got = [replay(o, p, new, a, list(f[1])) for (o, p), f in zip(var, fins)]
+        v = worth(got)
+        if v <= val - cfg["heat"] * 0.1 ** (r / rounds) * math.log(1 - x[4]):
+            cur, arcs = (v, new, got), None
+            if v < best[0]:
+                best = cur
     return deps, best
 
 
-CFG = {"cy": 1.04e-3, "g": 1.56, "sc": 3.8, "pe": 0.52e-3, "wake": 0.1, "net": 2.0, "ld": 1.0, "xp": 32, "z16": "sv" * 8,
-       "a2": [["ssvv", "ssvv"]] * 3, "xv": (), "sx": "ssv",
-       "yo": "s", "yd": "g", "yt": ["gggg", "gggg", "vvgg"],
-       "c2": [[5, 5, 4, 2], [5, 5, 4, 2]], "c5": [[4, 4, 4, 4], [4, 4, 2, 4, 2]], "p5": [[16], [10, 6]],
-       "rv": [(), (), ()], "seed": 1, "rounds": 8000, "norm": [70.0, 65.0, 85.0],
-       "guess": [{}, {"g": 1.15, "sc": 2.2, "wake": 0.15, "net": 3.0, "ld": 1.3}, {"g": 2.0, "sc": 5.5, "wake": 0.07, "ld": 0.8}]}
+CFG = {"cy": 0.85e-3, "g": 1.56, "sc": 3.8, "pe": 0.43e-3, "wake": 0.2, "net": 1.6, "net2": 0.3, "ld": 1.0, "xp": (7, 1),
+       "z16": "gsvs" * 4, "P2": [(0, 1), (2,), (3,)], "P5": [(0, 1), (2,), (3,)], "kk": [(0, 9, 0), (9, 12, 1)],
+       "a2": [["svvv", "vvvv", "vvvv"]] * 3, "xv": (), "sx": "ssv", "ea": 16,
+       "sy": "sss", "yd": "g", "yt": ["gggg", "gggg", "vvgg"],
+       "c2": [[6, 4, 4, 2], [4, 4, 4, 4], [4, 4, 4, 4]], "c5": [[4, 4, 4, 4], [8, 8], [8, 4, 4]], "p5": [[16], [16], [16]],
+       "a5": [["bcbb", "cb", "bbb"]] * 3,
+       "order": [("v", ["ON.0- WS.0- LV.0- LA.0- RG.0- EB.1- EB.2- RG.1- a2.0- a2.1- a3.0- a3.1- OS.0- OS.1- FF.1- TB.0 FS.0- FS.1- "
+                        "CL.0- VN.0- RR.0- D2.0", ""]),
+                 ("g", ["ci.0- I1.0- LT.0- LT.1- WA.0- ID.0- BW.0- CW.0- Z1.0- Z1.1- Z1.2- Z1.3- KC.0- LT.2- TS.0- TS.1- TS.2- CE.0- "
+                        "EA.0-", ""]),
+                 ("p", ["PX.0- PC.0- PC.1- PD.0- PD.1- PT.0 PC.2-", ""]),
+                 ("s", ["ZI.0- Z1.0- Z1.1- Z1.2- Z1.3- Z1.4- Z1.5- Z1.6- Z1.7- XO.0", ""])],
+       "rv": [(), (), ()], "seed": 1, "rounds": 50000, "passes": 60, "step": 0.3, "any": 0.3, "early": 0.03,
+       "fill": ("tb", "xt", "rt", "ea", "sh", "c3", "c4", "rh", "nc"), "heat": 0.004, "norm": [70.0, 72.0, 88.0],
+       "guess": [{}, {"cy": 1.0e-3, "pe": 0.5e-3, "g": 1.2, "sc": 2.4, "wake": 0.22, "net": 2.4, "ld": 1.3},
+                 {"cy": 1.15e-3, "pe": 0.58e-3, "g": 1.9, "sc": 5.0, "wake": 0.16, "ld": 0.85}]}
 PLAN = {}
 
 

import math
import numpy as np
from concourse.bass import DstId, RemoteDMATransfer
from concourse.mybir import AluOpType as A, ActivationFunctionType as F, AxisListType

N, NB, T0, P, RO = 8, 3072, 1280, 192, 3
OFS = 1824
PER = {1280: (1, 5), 1472: (4, 23), 1664: (2, 13)}


def _sb(n, d):
    return ("sbuf", [128, n], d)


f32, bf, i32, u16, f16 = "float32", "bfloat16", "int32", "uint16", "float16"
SCRATCH = {
    "XW": _sb(3648, bf), "RI": _sb(1280, i32), "RG": _sb(1664, f16), "NL": _sb(3072, f32), "RT": _sb(4288, f32),
    "XT0": _sb(4288, bf), "XT1": _sb(4288, bf), "TB0": _sb(256, u16), "TB1": _sb(256, u16),
    "D2": _sb(3072, bf), "A2": _sb(3072, bf), "D5": _sb(3072, bf), "A5": _sb(3072, bf), "Z16": _sb(3072, bf),
    "EM": _sb(640, bf), "EA": _sb(2048, bf), "SH": _sb(2048, bf), "LVI": _sb(640, i32), "LVB": _sb(640, bf),
    "ZN": _sb(192, bf), "ZI": _sb(192, bf), "WI": _sb(4, i32), "KI": _sb(4, i32), "TI": _sb(4, i32), "CI": _sb(4, i32),
    "YR": _sb(5040, bf), "YO": _sb(192, bf), "YT": _sb(576, f32), "MK": _sb(48, f32),
    "RR": _sb(192, u16), "RH": _sb(192, f16), "OFR": _sb(12, u16), "OY": _sb(16, u16), "HX": _sb(192, u16), "NID": _sb(128, bf),
    "IDX": _sb(12, u16), "OSC": _sb(12, u16), "LAU": _sb(12, u16), "EXO": _sb(16, u16), "VN": _sb(30, u16),
    "WS1": _sb(144, bf), "WS2": _sb(144, bf), "WS5": _sb(144, bf), "WSV": _sb(144, bf), "WSU": _sb(144, f16),
    "WA": _sb(272, bf), "ID": _sb(128, bf), "BO": _sb(128, bf), "TRI": _sb(128, bf), "UPP": _sb(128, bf), "INC": _sb(128, bf),
    "ONE": _sb(480, bf), "M3": _sb(128, bf), "REP": _sb(128, f32), "TS": _sb(128, bf), "CE": _sb(32, f32),
    "KA": _sb(144, bf), "KB": _sb(144, bf), "KH": _sb(144, bf), "KO": _sb(144, bf), "KX": _sb(144, f32), "M96": _sb(144, f32),
    "KC": _sb(96, bf), "col": _sb(40, f32), "ci": _sb(16, i32), "I144": _sb(144, f32), "LT": _sb(384, bf),
    "EB": _sb(176, bf), "BJ": _sb(11, f16), "BW": _sb(7, f32), "CW": _sb(80, f32), "WT": _sb(112, bf), "a2": _sb(7, f32),
    "a3": _sb(7, f32), "FF": _sb(4272, bf), "FS": _sb(480, bf), "DEC": _sb(480, bf), "CL": _sb(480, bf),
    "LAN": _sb(12, f32), "K4": _sb(12, f32), "DK": _sb(12, f32), "ST": _sb(12, f32),
    "CS": _sb(4, f32), "NC": _sb(4, f32), "LJ": _sb(192, f32), "NR": _sb(192, f32),
    "e1": _sb(16, i32), "e2": _sb(16, i32), "u0": _sb(12, i32), "UD": _sb(16, i32),
    "uu": _sb(12, i32), "QD": _sb(16, i32), "KU": _sb(192, f32), "HS": _sb(192, i32), "HA": _sb(192, i32),
    "KEY": _sb(12, i32), "FK": _sb(36, bf), "k2": _sb(12, i32), "k3": _sb(12, f32), "k4": _sb(12, i32),
    "k5": _sb(12, i32), "k6": _sb(12, f32), "k7": _sb(12, f32), "k8": _sb(12, f32),
    "JB": _sb(16, bf), "EE": _sb(12, f32), "J2": _sb(12, f32), "TO": _sb(12, f32), "o1": _sb(12, f32), "o2": _sb(12, f32),
    "SX": _sb(192, bf), "SY": _sb(192, bf), "hb": _sb(2, bf), "TC": _sb(2, f32),
}
for _k in ("PA", "PB"):
    SCRATCH[_k] = ("psum", [128, 32, 16], f32)
for _k in ("PC", "PD", "PU", "PT", "PX", "PY"):
    SCRATCH[_k] = ("psum", [128, 512], f32)
NDMA = 28
SEMAPHORES = ["qv", "qs", "qp", "qg", "sent"] + ["d%d" % _k for _k in range(NDMA)] + ["arr%d" % _k for _k in range(9)]
TWO = (bf, f16, u16)


def psum(x):
    return SCRATCH[x["n"]][0] == "psum"


def R(name, a=0, b=None, st=1, p=(0, 128)):
    if b is None:
        b = SCRATCH[name][1][1]
    m = 0
    if st == 1:
        m = ((1 << (b - a)) - 1) << a
    else:
        for c in range(a, b, st):
            m |= 1 << c
    return {"n": name, "a": a, "b": b, "st": st, "p": p, "m": m, "k": len(range(a, b, st)), "off": None}


def C(name, c):
    return R(name, c, c + 1)


def IND(win, off):
    d = dict(win)
    d["off"] = off
    d["k"] = 16 * off["k"]
    return d


def build(rank, cfg):
    ops, ph, cy, lab, now = [], ["load"], cfg["cy"], {}, [-1]

    def add(q, fn, args, reads, writes, cost, lat=0.0, acc=False, sem=None):
        rd = []
        for r in reads:
            if isinstance(r, dict):
                rd.append(r)
                if r["off"] is not None:
                    rd.append(r["off"])
        wr = []
        for w in writes:
            wr.append(w)
            if w["off"] is not None:
                rd.append(w["off"])
        ops.append({"q": q, "fn": fn, "args": args, "r": rd, "w": wr, "c": cost, "lat": lat, "acc": acc, "sem": sem, "ph": ph[0],
                    "after": []})
        if wr:
            lab.setdefault((q, wr[0]["n"][:2], now[0]), []).append(len(ops) - 1)

    def two(*v):
        return all(SCRATCH[x["n"]][2] in TWO for x in v)

    def vc(out, in0, f):
        if in0 is not None and in0["off"] is not None:
            return 0.05 + in0["k"] * cfg["g"] * cy
        if out["off"] is not None:
            return 0.05 + out["k"] * cfg["sc"] * cy
        return max(64, out["k"] * f) * cy

    def cp(out, a):
        add("v", "tensor_copy", (out, a), [a], [out], vc(out, a, 0.5 if two(out, a) else 1))

    def tt(out, a, b, op):
        add("v", "tensor_tensor", (out, a, b, op), [a, b], [out], vc(out, a, 1 if psum(a) or psum(b) else 2))

    def ts(out, a, s1, op0, s2=None, op1=None):
        args = (out, a, s1, s2, op0) if op1 is None else (out, a, s1, s2, op0, op1)
        add("v", "tensor_scalar", args, [a, s1, s2], [out], vc(out, a, 0.5 if two(out, a) else 1))

    def ms(out, v, q="g"):
        if q == "g":
            return iota(out, [[0, out["k"]]], int(v), 0)
        add("v", "memset", (out, v), [], [out], vc(out, None, 0.5 if two(out) else 1))

    def scan(out, d0, d1, init, op0, op1):
        add("v", "tensor_tensor_scan", (out, d0, d1, init, op0, op1), [d0, d1, init], [out], vc(out, None, 0.5 if two(out, d0, d1) else 1))

    def red(out, a, op):
        add("v", "tensor_reduce", (out, a, AxisListType.X, op), [a], [out], max(64, a["k"]) * cy)

    def act(out, a, func, bias=None, scale=None):
        c = 0.065 + a["k"] * cfg["g"] * cy if a["off"] is not None else 0.03 + max(64, a["k"]) * cy
        add("s", "activation", (out, a, func, bias, scale), [a, bias, scale], [out], c)

    def lin(out, a, scale, bias):
        act(out, a, F.Identity, bias, scale)

    def mm(out, l, r, start=True, stop=True):
        c = max(64, r["k"]) * cfg["pe"] * (4 if SCRATCH[r["n"]][2] == f32 else 1)
        o = ops[-1]
        if o["q"] == "p" and o["w"][0]["n"] == out["n"] and o["ph"] == ph[0] and len(o["args"]) < 17:
            o["args"].append((out, l, r, start, stop))
            o["r"] += [l, r]
            o["w"].append(out)
            o["c"] += c
            o["acc"] = o["acc"] and not start
        else:
            add("p", "matmul", [(out, l, r, start, stop)], [l, r], [out], c, acc=not start)

    tail, nc = {}, [0]

    def chain(k):
        if k in tail:
            ops[-1]["after"].append(tail[k])
        tail[k] = len(ops) - 1

    def put(out, ws, src, a, b, first=True, stop=True):
        for r in range(16):
            mm(out, R(ws, 15 - r, 143 - r), R(src, a + r, b, 16), first and r == 0, stop and r == 15)

    def iota(out, pat, base, cm):
        add("g", "iota", (out, pat, base, cm), [], [out], 0.15 + out["k"] * 2 * cy)

    def sel(out, a, pat, op, base, cm, fill=0.0):
        add("g", "affine_select", (out, a, pat, op, fill, base, cm), [a], [out], 0.19 + out["k"] * 2 * cy)

    def copy(q, out, a):
        if q == "v":
            cp(out, a)
        elif q == "s":
            act(out, a, F.Copy)
        else:
            sel(out, a, [[0, a["k"]]], A.is_ge, 0, 0)

    nd = [0]

    def load(q, out, name, a, b, lat):
        add(q, "load", (out, name, a, b), [], [out], 0.06, lat=lat * cfg["ld"], sem="d%d" % nd[0])
        nd[0] += 1

    def store(q, name, a, b, src):
        add(q, "store", (name, a, b, src), [src], [], 0.06, lat=1.5, sem="d%d" % nd[0])
        nd[0] += 1

    load("y", R("LVI", p=(0, 8)), "live", 0, 640, 1.3)
    load("y", R("LVI", p=(8, 16)), "live", 640, 1280, 1.3)
    load("y", R("RI", 0, 640), "rings", 0, 640, 2.2)
    load("y", R("RI", 640, 1280), "rings", 640, 1280, 3.0)
    load("y", R("XW", 0, NB), "x0", 0, NB, 5.0)
    load("s", R("ZN"), "z", 0, P, 1.5)
    load("y", C("WI", 0), "w", 0, 1, 5.5)
    load("y", C("KI", 0), "kap", 0, 1, 5.5)
    load("y", R("TI", 0, 1, p=(0, 8)), "th", 0, 1, 5.5)
    load("y", R("CI", 0, 1, p=(0, 8)), "cap", 0, 1, 5.5)

    ph[0] = "c0"
    (pm, mk0, c96, mlo, mhi, pm4, m15, dec, clo, chi, wv, fo, wsg, kva, kvb, kvh, thr, cap, nn, n0b, hq, ntmp, x0c, x1c,
     c15, pm2, c48) = [C("col", k) for k in range(27)]
    pi = C("ci", 1)
    iota(C("ci", 0), [[0, 1]], 0, 1)
    ts(pi, C("ci", 0), 15, A.bitwise_and)
    cp(pm, pi)
    ms(R("ONE"), 1.0, "v")
    sel(R("WA", p=(0, 16)), R("ONE", 0, 272, p=(0, 16)), [[1, 272]], A.is_equal, -15, -16)
    iota(R("I144"), [[-1, 144]], 15, 1)
    ts(R("WS1"), R("I144"), pm, A.is_equal)
    sel(R("ID"), R("ONE", 0, 128), [[-1, 128]], A.is_equal, 0, 1)
    lin(hq, pm, -1.0, 7.5)
    act(R("BO"), R("I144", 15, 143), F.Abs, hq)
    ts(R("BO"), R("BO"), 8.0, A.is_lt)
    lin(ntmp, pm, -0.5, 7.0)
    act(R("INC"), R("I144", 15, 143), F.Abs, ntmp)
    ts(R("INC"), R("INC"), ntmp, A.is_le)
    ts(m15, pi, 15.0, A.is_equal, 4096.0, A.mult)
    lin(dec, m15, None, -4096.0)
    lin(clo, m15, -256.0, -4096.0)
    lin(chi, m15, 256.0, None)
    lin(wv, m15, 17.0 / 2 ** 24, -1.0 / 4096)
    lin(R("DEC"), R("ONE"), dec, None)
    lin(R("WSV"), R("WS1"), wv, None)
    iota(R("CW"), [[1, 80]], 0, 0)
    act(R("CW"), R("CW"), F.Identity, dec, m15)
    iota(R("BW", 0, 5), [[16, 5]], 1300, 0)
    lin(R("BW", 0, 5), R("BW", 0, 5), None, pm)
    ms(R("BJ", 5, 11), 0.0, "v")
    cp(R("BJ", 0, 5), R("BW", 0, 5))
    lin(R("BW", 5, 7), R("BW", 3, 5), None, 2600.0)
    ts(C("BW", 5), pm, 14.0, A.is_ge, C("BW", 5), A.mult)
    ms(R("EB", 0, 96), 0.0, "v")
    ms(R("FF", 0, 480), -32768.0, "v")
    ph[0] = "c2"
    P2, P5, YW = cfg["P2"], cfg["P5"], 1680
    KW = {n: 0 if n == len(P5[0]) else 48 * len(P5[0]) for n in set(len(cl) for cl in P5)}
    iota(R("LT", 0, 96), [[4, 16], [1, 2], [64, 3]] if len(P2[0]) == 2 else [[1, 2], [4, 16], [64, 3]], 0, 0)
    iota(R("LT", 96, 192), [[1, 2], [4, 16], [64, 3]], 2, 0)
    for cl in P5:
        iota(R("LT", 192 + 48 * cl[0], 240 + 48 * cl[-1]), [[0, 16], [1, 3 * len(cl)]], 3 * cl[0], 0)
    put(R("PX", 0, 12), "WS1", "LT", 0, 192)
    ts(R("LAU"), R("PX", 0, 12), 1.0 / 16, A.mult)
    ts(R("LAN"), R("PX", 0, 12), 1.0 / 16, A.mult)
    ph[0] = "c2b"
    put(R("PY", 0, 12), "WS1", "LT", 192, 384)
    for cl in P5:
        ts(R("EXO", 4 * cl[0], 4 * cl[0] + 3 * len(cl)), R("PY", 3 * cl[0], 3 * cl[-1] + 3), 1.0 / 16, A.mult)
    ph[0] = "c2"
    act(R("ZI"), IND(R("ZN"), R("LAU")), F.Copy)
    for k in range(16):
        copy(cfg["z16"][k], R("Z16", k, 3072, 16), R("ZI"))

    ph[0] = "nl"
    cp(R("LVB", p=(0, 16)), R("LVI", p=(0, 16)))
    for q in range(2):
        for a in range(16):
            mm(R("PC", 40 * q, 40 * q + 40), R("WA", 128 * q + 15 - a, 128 * q + 143 - a, p=(0, 16)), R("LVB", a, 640, 16, p=(0, 16)),
               a == 0, a == 15)
    scan(R("EB", 1, 81), R("ONE", 0, 80), R("PC", 0, 80), 0.0, A.mult, A.add)
    ts(R("EB", 96, 176), R("PC", 0, 80), 4096.0, A.mult)
    mm(R("PU", 0, 80), R("INC"), R("EB", 96, 176))
    mm(R("PD", 16, 20), R("BO"), R("EB", 62, 81, 6))
    mm(R("PD", 0, 11), R("ID"), R("BJ"), True, False)
    put(R("PD", 0, 11), "WS1", "EB", 0, 176, False)
    tt(R("WT", 0, 80), R("PU", 0, 80), R("CW"), A.add)
    tt(R("WT", 80, 112), R("PU", 48, 80), R("CW", 48, 80), A.add)
    tt(R("a2", 0, 5), R("PD", 6, 11), R("BW", 0, 5), A.min)
    tt(R("a2", 5, 7), R("PD", 9, 11), R("BW", 5, 7), A.min)
    tt(R("a3", 0, 5), R("PD", 0, 5), R("a2", 0, 5), A.subtract)
    tt(R("a3", 5, 7), R("PD", 3, 5), R("a2", 5, 7), A.subtract)
    ts(R("OSC", 0, 5), R("a3", 0, 5), 288.0, A.add)
    ts(R("OSC", 5, 7), R("a3", 5, 7), C("PD", 19), A.subtract, 2888.0, A.add)
    ts(R("col", 22, 24), R("PD", 16, 19, 2), C("PD", 19), A.subtract, 288.0, A.add)
    cp(IND(R("FF"), R("OSC", 0, 7)), R("WT"))
    for a, b in ((0, 288), (288, 480)):
        scan(R("FS", a, b), R("DEC", a, b), R("FF", a, b), 0.0, A.add, A.max)
    ts(R("OFR"), R("LAN"), x0c, A.add)
    ts(R("CL", 0, 192), IND(R("FS"), R("OFR")), clo, A.max, chi, A.min)
    put(R("PC", 96, 108), "WSV", "CL", 0, 192)
    cp(R("VN", 0, 12), R("PC", 96, 108))
    cp(R("RR"), IND(R("RI"), R("VN", 0, 12)))
    ph[0] = "nl2"
    ts(R("CL", 192, 480), R("FS", 192, 480), clo, A.max, chi, A.min)
    put(R("PU", 96, 114), "WSV", "CL", 192, 480)
    cp(R("VN", 12, 30), R("PU", 96, 114))
    cp(R("NL", 192, 288), IND(R("RI"), R("VN", 12, 18)))
    cp(R("NL", 0, 192), IND(R("RI"), R("VN", 18, 30)))
    lin(R("TO"), R("LAN"), None, x1c)
    ph[0] = "rg"
    for k in range(2):
        ts(R("RG", 640 * k, 640 * k + 640), R("RI", 640 * k, 640 * k + 640), -float(OFS), A.add)
    ph[0] = "em"
    ts(C("ci", 6), pi, 5.0, A.mult, 16.0, A.add)
    ts(C("ci", 7), C("ci", 6), 4, A.logical_shift_right)
    cp(fo, C("ci", 7))
    for o in range(5):
        ts(R("EM", 128 * o, 128 * o + 128), R("ID"), fo, A.mult, o + 1.0, A.is_equal)
    for a in range(16):
        ph[0] = "ea%d" % (a // 4)
        if a < cfg["ea"]:
            sel(R("EA", 128 * a, 128 * a + 128), R("ID"), [[0, 8], [1, 16]], A.is_equal, -a, 0)
        else:
            ts(R("EA", 128 * a, 128 * a + 128), R("ID"), pm, A.mult, float(a), A.is_equal)
    ph[0] = "sh"
    iota(R("TS"), [[32, 8], [1, 16]], -1, 0)
    sel(R("TS"), R("TS"), [[-16, 8], [0, 16]], A.is_ge, 0, 1, -100.0)
    sel(R("TS"), R("TS"), [[0, 8], [1, 16]], A.is_gt, 0, 0, -100.0)
    iota(R("CE"), [[15, 2], [-1, 16]], 0, 2)
    lin(pm2, pm, -1.0, None)
    lin(R("CE"), R("CE"), None, pm2)
    lin(R("CE", 16, 32), R("CE", 16, 32), None, pm2)
    for a in range(16):
        ts(R("SH", 128 * a, 128 * a + 128), R("TS"), C("CE", 16 + a), A.min, C("CE", a), A.is_equal)
    ph[0] = "c3"
    ts(mk0, pi, 0.0, A.is_equal)
    ts(mlo, pi, 8.0, A.is_lt)
    ts(mhi, pi, 8.0, A.is_ge)
    lin(c96, pm, 96.0, None)
    lin(c48, pm, 48.0, None)
    lin(R("NID"), R("ID"), -1.0, None)
    lin(pm4, pm, -4.0, None)
    lin(R("WS2"), R("WS1"), 128.0, None)
    lin(R("WS5"), R("WS1"), -32768.0, None)
    iota(R("KC"), [[1, 96]], 0, 0)
    sel(R("TRI"), R("BO"), [[1, 128]], A.is_gt, 0, -1)
    sel(R("UPP"), R("BO"), [[-1, 128]], A.is_gt, 0, 1)
    ms(R("M3"), 3.0)
    iota(R("K4"), [[16, 12]], 4096, 0)
    lin(R("K4"), R("K4"), None, pm)
    iota(R("DK"), [[-64, 3], [-1, 4]], -1900, 0)
    lin(R("DK"), R("DK"), None, pm4)
    ms(R("ST"), 1.0)
    ms(R("ST", 0, 12, 4), -3.0)
    lin(C("CS", 0), pm, None, 1899.0)
    lin(C("CS", 1), pm, 4.0, 1899.0 + 64 - 45)
    lin(C("CS", 2), pm, 4.0, 1899.0 + 128 - 45)
    for t in range(RO):
        lin(C("col", 30 + t), mk0, float(NB + P * t - OFS), float(OFS))
    iota(R("LJ"), [[1, 4], [4, 48]], 0, 0)
    lin(R("LJ"), R("LJ"), mk0, None)
    ms(R("JB", 0, 4), 0.0)
    ms(R("UD"), 0)
    ms(R("QD"), 0)
    ms(R("KO"), 1032192.0)
    ms(nn, 288.0)
    ph[0] = "c4"
    ts(C("ci", 2), C("WI", 0), 2048.0, A.is_ge, -4096.0, A.mult)
    tt(wsg, C("ci", 2), C("WI", 0), A.add)
    ts(R("WSU"), R("WS1"), wsg, A.mult)
    ts(C("ci", 4), C("KI", 0), 127, A.bitwise_and)
    ts(C("ci", 5), C("KI", 0), 1920, A.bitwise_and)
    cp(R("col", 14, 16), R("ci", 4, 6))
    lin(c15, pm, -2048.0, 30720.0)
    lin(kva, c15, None, kvh)
    for n, k0 in KW.items():
        iota(R("M96", k0, k0 + 48 * n), [[1, 16], [0, 3 * n]], 0, 0)
    kw = 48 * sum(KW)
    ts(R("M96", 0, kw), R("M96", 0, kw), pm, A.is_equal)
    lin(R("KA", 0, kw), R("M96", 0, kw), kva, None)
    lin(R("KB", 0, kw), R("M96", 0, kw), kvb, None)
    lin(R("KH", 0, kw), R("M96", 0, kw), kvh, None)
    mm(R("PY", 256, 256 + kw), R("BO"), R("KH", 0, kw), True, False)
    mm(R("PY", 256, 256 + kw), R("BO"), R("KB", 0, kw), False, True)
    lin(R("KX", 0, kw), R("PY", 256, 256 + kw), None, None)
    sel(R("REP", p=(0, 8)), R("ONE", 0, 128, p=(0, 8)), [[1, 8], [0, 16]], A.is_equal, 0, -1)
    copy("g", R("TC", 0, 1, p=(0, 8)), R("TI", 0, 1, p=(0, 8)))
    copy("g", R("TC", 1, 2, p=(0, 8)), R("CI", 0, 1, p=(0, 8)))
    mm(R("PY", 400, 402), R("REP", p=(0, 8)), R("TC", p=(0, 8)))
    lin(thr, C("PY", 400), -32768.0, 505.0 * 32768)
    lin(cap, C("PY", 401), None, None)

    def cols(T, a, s2, s0, s1):
        per, step = PER[T]
        v0 = (16 * (s0 + s2) + a) * T >> 12
        n = (s1 - s0) // per
        return R("RG", v0, v0 + step * (n - 1) + 1, step)

    def split(t):
        T = T0 + P * t
        per = max(2, PER[T][0])
        s = 256
        while ((16 * s - 1) * T >> 12) >= T - P:
            s -= per
        return s

    def table(t, s0, s1, nb):
        T = T0 + P * t
        per = PER[T][0]
        tb, xt = "TB%d" % (t % 2), "XT%d" % (t % 2)
        ph[0] = "tb%d_%d" % (t, s0)
        ms_ = [("EM", o, (16 * o + 4) // 5) for o in range(5)] if t == 0 else [("EA", a, a) for a in range(16)]
        for s2 in range(per):
            for k, (e, o, a) in enumerate(ms_):
                mm(R("PT", s0 + s2, s1, per), R(e, 128 * o, 128 * o + 128), cols(T, a, s2, s0, s1), k == 0, k == len(ms_) - 1)
        ts(R(tb, s0, s1), R("PT", s0, s1), float(OFS), A.add)
        n = cfg["xp"][s0 > 0]
        cut = [s0 + (s1 - s0) * k // (2 * n) * 2 for k in range(n + 1)]
        for k in range(n):
            s, e, q = cut[k], cut[k + 1], "v" if (t, s0 > 0, k) in cfg["xv"] else "s"
            ph[0] = "xt%d_%d_%d" % (t, s0, s // 72)
            copy(q, R(xt, 16 * s, 16 * e), IND(R("XW", 0, nb), R(tb, s, e)))
            lab.setdefault((q, "XN" if s0 else "XO", t), []).append(len(ops) - 1)
            chain("x%d" % (s0 > 0))

    def tails(t):
        T = T0 + P * t
        per = PER[T][0]
        for a0 in range(0, 16, 2):
            ps = ("PX", "PY")[(a0 // 2) % 2]
            ph[0] = "rt%d_%d" % (t, a0 // 4)
            for a in (a0, a0 + 1):
                o = 256 * (a % 2)
                for s2 in range(per):
                    mm(R(ps, o + s2, o + 256, per), R("SH", 128 * a, 128 * a + 128), cols(T, a, s2, 0, 256))
            for a in (a0, a0 + 1):
                o = 256 * (a % 2)
                if a0 // 2 in cfg["rv"][t]:
                    ts(R("RT", a, 4096, 16), R(ps, o, o + 256), C("col", 30 + t), A.add)
                else:
                    lin(R("RT", a, 4096, 16), R(ps, o, o + 256), None, C("col", 30 + t))

    for t in range(RO):
        T, nb, xt, last = T0 + P * t, NB + P * t, "XT%d" % (t % 2), t == RO - 1
        ph[0], now[0] = "rr%d" % t, t
        if t:
            cp(R("RR"), IND(R("NL", 0, 672), R("OFR")))
        table(t, split(t) if t else 0, 256, nb)
        home = {c: YW * t + 384 * h + 384 - 48 * (len(cl) - k) for h, cl in enumerate(P5) for k, c in enumerate(cl)}
        for h, cl in enumerate(P2):
            r0, w, d0 = 0, 48 * len(cl), 768 * cl[0]
            key = R(("PA", "PB")[h % 2], 128 * (h // 2), 128 * (h // 2) + w)
            ph[0] = "g2_%d_%d_0" % (t, h)
            mm(key, R("ID"), R("KC", 0, w), True, False)
            for n, q in zip(cfg["c2"][h], cfg["a2"][t][h]):
                ph[0] = "g2_%d_%d_%d" % (t, h, r0 // 8)
                a, b = d0 + w * r0, d0 + w * (r0 + n)
                tt(R("D2", a, b), IND(R("XW", 0, nb), R("RR", a // 16, b // 16)), R("Z16", a, b), A.subtract)
                chain("d")
                if q == "v":
                    ts(R("A2", a, b), R("D2", a, b), -1.0, A.mult, 0.0, A.max)
                else:
                    act(R("A2", a, b), R("D2", a, b), F.Relu, None, -1.0)
                for r in range(r0, r0 + n):
                    mm(key, R("WS2", 15 - r, 143 - r), R("A2", d0 + w * r, d0 + w * r + w), False, r == 15)
                r0 += n
            c0 = 4 * cl[0]
            c1 = c0 + w // 16
            ph[0] = "p2_%d_%d" % (t, h)
            red(R("e1", c0, c1), key, A.min)
            ts(R("e2", c0, c1), R("e1", c0, c1), 127, A.bitwise_and)
            ts(R("OY", c0, c1), R("e2", c0, c1), c48 if w == 48 else c96, A.add)
            y0 = home[3] if cl == (3,) else YW * t + 1536 + 48 * cl[0]
            act(R("YR", y0, y0 + w), IND(R("D2", d0, d0 + 16 * w), R("OY", c0, c1)), F.Abs)
            if cl != (3,):
                tr = [(R("YR", y0 + 48 * k, y0 + 48 + 48 * k), R("YR", home[c], home[c] + 48),
                       (rank + 1 + (t + c) % (N - 1)) % N) for k, c in enumerate(cl)]
                add("g", "send", (tr, "arr%d" % (3 * t + h)), [x[0] for x in tr], [x[1] for x in tr], 0.3,
                    lat=cfg["net"] + cfg["net2"] * (len(cl) - 1), sem="arr%d" % (3 * t + h))
                chain("y")
        ph[0] = "rh%d" % t
        ts(R("RH"), R("RR"), -float(OFS), A.add)
        for cl in P2:
            st = 3 * len(cl)
            for c in range(3 * cl[0], 3 * cl[0] + st):
                i0 = 48 * cl[0] + c - 3 * cl[0]
                mm(R("PD", 256 + 16 * c, 272 + 16 * c), R("SH", 0, 128), R("RH", i0, i0 + 15 * st + 1, st))
        lin(R("RT", 4096, 4288), R("PD", 256, 448), None, C("col", 30 + t))
        tails(t)
        if not last:
            table(t + 1, 0, split(t + 1), nb)
            ph[0] = "nc%d" % t
            lin(R("NC", 0, 3), R("CS", 0, 3), None, nn)
            if t:
                lin(R("TO"), R("LAN"), None, n0b)
            lin(ntmp, nn, None, -48.0)
        for h, cl in enumerate(P5):
            w, nw, yr, key = 48 * len(cl), 3 * len(cl), YW * t + 384 * h, ("PC", "PD")[h % 2]
            c0, w0, d0, k0, e0, s0 = 3 * cl[0], 48 * cl[0], 768 * cl[0], KW[len(cl)], 4 * cl[0], 96 * (h // 2)
            c1, y = c0 + nw, R("YR", yr + 384 - w, yr + 384)
            ph[0] = "u%d_%d" % (t, h)
            put(R("PU", c0, c1), "WSU", "YR", yr + 384 - w, yr + 384)
            n = w
            while n < 384:
                copy(cfg["yd"], R("YR", yr + 384 - 2 * n, yr + 384 - n), R("YR", yr + 384 - n, yr + 384))
                n *= 2
            copy(cfg["yd"], R(xt, 4096 + w0, 4096 + w0 + w), y)
            if cfg["sx"][t] == "v":
                copy(cfg["yd"], R("YO", w0, w0 + w), y)
            cp(R("u0", c0, c1), R("PU", c0, c1))
            ts(R("UD", c0, c1), R("u0", c0, c1), 4095, A.bitwise_and)
            tt(R("uu", c0, c1), R("UD", c0, c1), R("UD", c0, c1), A.mult)
            tt(R("KU", w0, w0 + w), IND(R("UD"), R("EXO", e0, e0 + nw)), R("KX", k0, k0 + w), A.mult)
            ts(R("QD", c0, c1), R("uu", c0, c1), 5, A.logical_shift_right)
            tt(R("HS", w0, w0 + w), IND(R("QD"), R("EXO", e0, e0 + nw)), R("KU", w0, w0 + w), A.add)
            ts(R("HA", w0, w0 + w), R("HS", w0, w0 + w), 4095, A.bitwise_and)
            cp(R("HX", w0, w0 + w), R("HA", w0, w0 + w))
            m0 = 0
            for n, q in zip(cfg["c5"][h], cfg["a5"][t][h]):
                ph[0] = "g5_%d_%d_%d" % (t, h, m0)
                a, b = d0 + w * m0, d0 + w * (m0 + n)
                src, ys = IND(R(xt, 0, 4096), R("HX", a // 16, b // 16)), R("YR", yr + 384 - w * n, yr + 384)
                if q == "c":
                    act(R("D5", a, b), src, F.Copy)
                    chain("c")
                    o = R(("PA", "PB")[nc[0] % 2], 0, w * n)
                    nc[0] += 1
                    mm(o, R("NID"), ys, True, False)
                    mm(o, R("ID"), R("D5", a, b), False, True)
                    act(R("A5", a, b), o, F.Abs)
                else:
                    tt(R("D5", a, b), src, ys, A.subtract)
                    chain("d")
                    act(R("A5", a, b), R("D5", a, b), F.Abs)
                    chain("a")
                m0 += n
            m0 = 0
            for n in cfg["p5"][h]:
                ph[0] = "p5_%d_%d_%d" % (t, h, m0)
                o = R(key, s0 + nw * m0, s0 + nw * (m0 + n))
                for k, nm in enumerate(("KA", "KB", "KO")):
                    mm(o, R("BO"), R(nm, k0 + nw * m0, k0 + nw * (m0 + n)), k == 0, False)
                ph[0] += "a"
                put(o, "WS5", "A5", d0 + w * m0, d0 + w * (m0 + n), False)
                m0 += n
            for c in range(nw):
                red(C("KEY", c0 + c), R(key, s0 + c, s0 + w, nw), A.max)
        ph[0] = "b%d" % t
        mk = 16 * t
        for c in range(4):
            ts(R("FK", 12 * t + c, 12 * t + 12, 4), R("KEY", 3 * c, 3 * c + 3), thr, A.is_ge, 1.0 if c < 3 else -1.0, A.mult)
        for c in sorted(range(12 * t + 12), key=lambda c: (c // 12, c % 4 in P5[-1])):
            ph[0] = "b%d%s" % (t, "o" if c < 12 * t else "" if c % 4 in P5[-1] else "h")
            mm(C("PU", 16), R("ONE", 0, 128) if c % 4 < 3 else R("M3"), C("FK", c), c == 0, c == 12 * t + 11)
        ts(R("MK", mk, mk + 12), R("FK", 12 * t, 12 * t + 12), C("PU", 16), A.mult, cap, A.is_le)
        for c in range(3):
            store("ysy"[c] if last else "y", "ya", 192 * t + 64 * c, 192 * t + 64 * c + 64, R("MK", mk + 4 * c, mk + 4 * c + 4))
        ph[0] = "k%d" % t
        for a, b, thin in cfg["kk"]:
            ts(R("k2", a, b), R("KEY", a, b), 2047, A.bitwise_and)
            ts(R("k6", a, b), R("KEY", a, b), thr, A.is_lt)
            tt(R("k7", a, b), R("k6", a, b), R("K4", a, b), A.mult)
            if thin:
                cp(R("k3", a, b), R("UD", a, b))
                cp(R("k8", a, b), R("QD", a, b))
                for c in range(a, b):
                    ts(C("k4", c), C("k2", c), C("k3", c), A.mult, C("k8", c), A.add)
                ts(R("k5", a, b), R("k4", a, b), 4095, A.bitwise_and)
                for c in range(a, b):
                    ts(C("IDX", c), C("k5", c), C("k7", c), A.max)
            else:
                tt(R("k3", a, b), R("k2", a, b), R("UD", a, b), A.mult)
                tt(R("k4", a, b), R("k3", a, b), R("QD", a, b), A.add)
                ts(R("k5", a, b), R("k4", a, b), 4095, A.bitwise_and)
                tt(R("k8", a, b), R("k5", a, b), R("k7", a, b), A.max)
                cp(R("IDX", a, b), R("k8", a, b))
        tt(R("NR"), IND(R("RT"), R("IDX")), R("LJ"), A.add)
        if cfg["sx"][t] == "v":
            tt(R("SX"), IND(R(xt), R("IDX")), R("YO"), A.add)
            sx = R("SX")
        else:
            act(R("SX"), IND(R(xt), R("IDX")), F.Copy)
            sx = R("PC", 256, 448)
            mm(sx, R("ID"), R(xt, 4096, 4288), True, False)
            mm(sx, R("ID"), R("SX"), False, True)
        if cfg["sy"][t] == "s":
            lin(R("SY"), sx, 0.5, 127.75)
            for c in range(4):
                if last and c % 2:
                    ts(R("XW", nb + c, nb + 192, 4), R("SY", 48 * c, 48 * c + 48), -128.0, A.add)
                else:
                    lin(R("XW", nb + c, nb + 192, 4), R("SY", 48 * c, 48 * c + 48), None, -128.0)
        else:
            ts(R("HA"), sx, 0.5, A.mult, -0.25, A.add)
            for c in range(4):
                copy("g", R("XW", nb + c, nb + 192, 4), R("HA", 48 * c, 48 * c + 48))
        for c in range(4):
            copy(cfg["yt"][t][c], R("YT", 192 * t + c, 192 * t + 192, 4), R("NR", 48 * c, 48 * c + 48))
        store("s" if last else "y", "yx", 192 * t, 192 * t + 192, R("XW", nb, nb + 192))
        store("y", "yt", 192 * t, 192 * t + 192, R("YT", 192 * t, 192 * t + 192))
        if not last:
            ts(R("RG", T, T + 192), R("YT", 192 * t, 192 * t + 192), -float(OFS), A.add)
            ph[0] = "n%d" % t
            scan(R("JB", 4, 16), R("ST"), R("MK", mk, mk + 12), 3.0, A.add, A.add)
            mm(R("PU", 32, 35), R("TRI"), R("JB", 7, 16, 4), True, False)
            mm(R("PU", 32, 35), R("UPP"), R("JB", 3, 12, 4), False, True)
            mm(R("PU", 35, 36), R("BO"), C("JB", 15))
            tt(R("EE"), R("MK", mk, mk + 12), R("DK"), A.mult)
            tt(R("J2"), R("EE"), R("JB", 4, 16), A.add)
            for c in range(3):
                ts(R("OSC", c, 12, 3), R("J2", 4 * c, 4 * c + 4), C("PU", 32 + c), A.add, C("NC", c), A.add)
            ts(nn, C("PU", 35), ntmp, A.add)
            cp(IND(R("NL"), R("OSC")), R("NR"))
            ts(R("o1"), R("TO"), nn, A.is_ge, nn, A.mult)
            tt(R("o2"), R("TO"), R("o1"), A.subtract)
            cp(R("OFR"), R("o2"))
            if t == 0:
                ts(hq, C("JB", 11), mlo, A.mult)
                ts(C("hb", 0), C("JB", 7), mhi, A.mult, hq, A.add)
                mm(R("PU", 40, 41), R("BO"), C("hb", 0))
                lin(n0b, C("PU", 40), None, ntmp)
    for q, lines in cfg["order"]:
        prev = None
        for t in range(RO):
            for w in lines[min(t, len(lines) - 1)].split():
                nm, k = w.rstrip("-+").split(".")
                ids = lab.get((q, nm, t - w.count("-") + w.count("+")), [])
                if int(k) < len(ids):
                    if prev is not None:
                        ops[ids[int(k)]]["after"].append(prev)
                    prev = ids[int(k)]
    return ops


def depend(ops):
    n = len(ops)
    deps = [set() for _ in range(n)]
    order = [set() for _ in range(n)]
    hist, since = {}, {}
    for i, o in enumerate(ops):
        if o["fn"] == "load" and i and o["q"] == "y":
            order[i].add(max(j for j in range(i) if ops[j]["q"] == "y"))
        order[i].update(o["after"])
        for kind, lst in (("r", o["r"]), ("w", o["w"])):
            for x in lst:
                ps = psum(x)
                for (j, k2, m, p) in hist.get(x["n"], ()):
                    if j == i:
                        continue
                    same = ops[j]["q"] == o["q"]
                    if ps and not same:
                        deps[i].add(j)
                    elif ps and o["q"] == "p":
                        order[i].add(j)
                        if m & x["m"] and not o["acc"]:
                            deps[i].add(j)
                    elif m & x["m"] and (kind == "w" or k2 == "w") and p[0] < x["p"][1] and x["p"][0] < p[1]:
                        deps[i].add(j)
        for kind, lst in (("r", o["r"]), ("w", o["w"])):
            for x in lst:
                h = hist.setdefault(x["n"], [])
                if psum(x):
                    if h and ops[h[-1][0]]["q"] != o["q"]:
                        h[:] = [e for e in h if ops[e[0]]["q"] == ops[h[-1][0]]["q"] and e[0] > since.get(x["n"], -1)]
                        since[x["n"]] = h[-1][0]
                elif kind == "w" and x["p"] == (0, 128):
                    h[:] = [e for e in h if e[2] & ~x["m"] or e[0] == i]
                h.append((i, kind, x["m"], x["p"]))
    return deps, order


def edges(ops, deps, order, w):
    return [[(j, ops[j]["lat"] + w) for j in deps[i]] + [(j, 0.0) for j in order[i] - deps[i]] for i in range(len(ops))]


def place(cost, qs, pred, tail, rank):
    n = len(cost)
    start, line = [0.0] * n, {q: ([], []) for q in "vspgy"}
    for i in rank:
        t = tail[i]
        for j, d in pred[i]:
            x = start[j] + cost[j] + d
            if x > t:
                t = x
        a, b = line[qs[i]]
        k = len(b)
        while k and b[k - 1] > t:
            k -= 1
        while k < len(a) and a[k] < t + cost[i]:
            t = max(t, b[k])
            k += 1
        a.insert(k, t)
        b.insert(k, t + cost[i])
        start[i] = t
    return start


def replay(ops, pred, seq, a, fin):
    cost, qs, stores = ops
    free, k = {}, a - 1
    while k >= 0 and len(free) < 5:
        free.setdefault(qs[seq[k]], fin[seq[k]])
        k -= 1
    for i in seq[a:]:
        t = free.get(qs[i], 0.0)
        for j, d in pred[i]:
            if fin[j] + d > t:
                t = fin[j] + d
        fin[i] = free[qs[i]] = t + cost[i]
    end, last = max((fin[i] + d, i) for i, d in stores)
    return end, fin, last


def schedule(cfg, rounds):
    var = []
    for ch in cfg["guess"]:
        c = dict(cfg)
        c.update(ch)
        ops = build(0, c)
        if not var:
            deps, order = depend(ops)
        var.append((([o["c"] for o in ops], [o["q"] for o in ops], [(i, o["lat"]) for i, o in enumerate(ops) if o["fn"] == "store"]),
                    edges(ops, deps, order, c["wake"])))
    ops = build(0, cfg)
    (cost, qs, stores), pred = var[0]
    n = len(ops)
    succ = [[] for _ in range(n)]
    for i in range(n):
        for j, d in pred[i]:
            succ[j].append((i, d))
    left, topo = [len(p) for p in pred], [i for i in range(n) if not pred[i]]
    for j in topo:
        for i, d in succ[j]:
            left[i] -= 1
            if not left[i]:
                topo.append(i)
    assert len(topo) == n
    lat, nil = [o["lat"] for o in ops], [0.0] * n
    back = [0.0] * n
    for i in topo[::-1]:
        back[i] = max([back[k] + cost[k] + d for k, d in succ[i]] + [lat[i]])
    rank = {i: k for k, i in enumerate(topo)}
    best, floor = None, list(nil)
    fill = [o["ph"][:2] in cfg["fill"] for o in ops]
    core = [i for i in range(n) if not fill[i]]

    def worth(fins):
        fin = fins[0][1]
        return sum(f[0] / s for f, s in zip(fins, cfg["norm"])) + cfg["early"] * sum([fin[i] for i in core]) / len(core)

    lean = [p if fill[i] else [(j, d) for j, d in p if not fill[j]] for i, p in enumerate(pred)]
    for r in range(cfg["passes"]):
        fw = place(cost, qs, lean, floor, sorted(range(n), key=lambda i: (fill[i], -(back[i] + cost[i]), rank[i])))
        key = list(fw)
        for i in topo:
            key[i] = max([key[i]] + [key[j] + 1e-6 for j, d in pred[i]])
        seq = sorted(range(n), key=lambda i: (key[i], rank[i]))
        fins = [replay(o, p, seq, 0, [0.0] * n) for o, p in var]
        val = worth(fins)
        if best is None or val < best[0]:
            best = (val, seq, fins)
        for i in range(n):
            late = max([fw[j] + cost[j] + d for j, d in pred[i] if fill[j]] + [0.0])
            if not fill[i] and late > fw[i]:
                floor[i] = fw[i] + cfg["step"] * (late - fw[i])
    cur, arcs = best, None
    before, after = [set(j for j, d in p) for p in pred], [set(i for i, d in s) for s in succ]
    rnd = np.random.default_rng(cfg["seed"]).random((rounds, 6)).tolist()
    for r in range(rounds):
        val, seq, fins = cur
        if arcs is None:
            arcs, pos, prev, lastq = [], [0] * n, [-1] * n, {}
            for k, i in enumerate(seq):
                pos[i], prev[i], lastq[qs[i]] = k, lastq.get(qs[i], -1), i
            for (o, p), (end, fin, i) in zip(var, fins):
                while i >= 0:
                    t, nx = fin[i] - o[0][i] - 1e-9, -1
                    for j, d in p[i]:
                        if fin[j] + d > t:
                            nx = j
                    if nx < 0 and prev[i] >= 0 and fin[prev[i]] > t:
                        nx = prev[i]
                        arcs.append((nx, i))
                    i = nx
        x = rnd[r]
        j, i = arcs[int(x[0] * len(arcs))]
        if x[5] < cfg["any"]:
            i = int(x[0] * n)
            j = prev[i]
            if j < 0:
                continue
        far = int(x[1] * (1, 1, 1, 4, 11, 31, 81)[int(x[2] * 7)])
        if x[3] < 0.5:
            a, b, lead, links, step = max(0, pos[j] - far), pos[i], i, before, -1
        else:
            a, b, lead, links, step = pos[j], min(n - 1, pos[i] + far), j, after, 1
        tied, move, rest = set(links[lead]), [lead], []
        for k in seq[a:b + 1][::step][1:]:
            if k in tied:
                move.append(k)
                tied |= links[k]
            else:
                rest.append(k)
        if not rest:
            continue
        new = seq[:a] + (rest + move if step == 1 else move[::-1] + rest[::-1]) + seq[b + 1:]
        got = [replay(o, p, new, a, list(f[1])) for (o, p), f in zip(var, fins)]
        v = worth(got)
        if v <= val - cfg["heat"] * 0.1 ** (r / rounds) * math.log(1 - x[4]):
            cur, arcs = (v, new, got), None
            if v < best[0]:
                best = cur
    return deps, best


CFG = {"cy": 0.85e-3, "g": 1.56, "sc": 3.8, "pe": 0.43e-3, "wake": 0.2, "net": 1.6, "net2": 0.3, "ld": 1.0, "xp": (7, 1),
       "z16": "gsvs" * 4, "P2": [(0, 1), (2,), (3,)], "P5": [(0, 1), (2,), (3,)], "kk": [(0, 9, 0), (9, 12, 1)],
       "a2": [["svvv", "vvvv", "vvvv"]] * 3, "xv": (), "sx": "ssv", "ea": 16,
       "sy": "sss", "yd": "g", "yt": ["gggg", "gggg", "vvgg"],
       "c2": [[6, 4, 4, 2], [4, 4, 4, 4], [4, 4, 4, 4]], "c5": [[4, 4, 4, 4], [8, 8], [8, 4, 4]], "p5": [[16], [16], [16]],
       "a5": [["bcbb", "cb", "bbb"]] * 3,
       "order": [("v", ["ON.0- WS.0- LV.0- LA.0- RG.0- EB.1- EB.2- RG.1- a2.0- a2.1- a3.0- a3.1- OS.0- OS.1- FF.1- TB.0 FS.0- FS.1- "
                        "CL.0- VN.0- RR.0- D2.0", ""]),
                 ("g", ["ci.0- I1.0- LT.0- LT.1- WA.0- ID.0- BW.0- CW.0- Z1.0- Z1.1- Z1.2- Z1.3- KC.0- LT.2- TS.0- TS.1- TS.2- CE.0- "
                        "EA.0-", ""]),
                 ("p", ["PX.0- PC.0- PC.1- PD.0- PD.1- PT.0 PC.2-", ""]),
                 ("s", ["ZI.0- Z1.0- Z1.1- Z1.2- Z1.3- Z1.4- Z1.5- Z1.6- Z1.7- XO.0", ""])],
       "rv": [(), (), ()], "seed": 1, "rounds": 50000, "passes": 60, "step": 0.3, "any": 0.3, "early": 0.03,
       "fill": ("tb", "xt", "rt", "ea", "sh", "c3", "c4", "rh", "nc"), "heat": 0.004, "norm": [70.0, 72.0, 88.0],
       "guess": [{}, {"cy": 1.0e-3, "pe": 0.5e-3, "g": 1.2, "sc": 2.4, "wake": 0.22, "net": 2.4, "ld": 1.3},
                 {"cy": 1.15e-3, "pe": 0.58e-3, "g": 1.9, "sc": 5.0, "wake": 0.16, "ld": 0.85}]}
PLAN = {}


def rank_program(g, core, T, topo):
    rank = T.rank_of(core)
    if rank is None:
        return
    ops = build(rank, CFG)
    if not PLAN:
        PLAN["p"] = schedule(CFG, CFG["rounds"])
    deps, seq = PLAN["p"][0], PLAN["p"][1][1]
    Q = {"v": g.vector, "s": g.scalar, "p": g.tensor, "g": g, "y": g.sync}

    def ap(x):
        if not isinstance(x, dict):
            return x
        if len(SCRATCH[x["n"]][1]) == 3:
            return T[x["n"]][:, x["a"] // 16:x["b"] // 16, :]
        v = T[x["n"]][x["p"][0]:x["p"][1], x["a"]:x["b"]:x["st"]] if x["st"] != 1 else T[x["n"]][x["p"][0]:x["p"][1], x["a"]:x["b"]]
        return v if x["off"] is None else v.indirect(ap(x["off"]))

    mark, count, seen, total, sent = {}, {q: 0 for q in Q}, {}, {}, [0]
    for i in seq:
        o = ops[i]
        q = o["q"]
        need = {}
        for j in deps[i]:
            nm, v = mark[j]
            need[nm] = max(need.get(nm, 0), v)
        for nm in sorted(need):
            if seen.get((q, nm), 0) < need[nm]:
                Q[q].wait_ge(T.sem[nm], need[nm])
                seen[(q, nm)] = need[nm]
        fn, a = o["fn"], o["args"]
        if fn == "load":
            src = T[a[1]][:] if a[3] - a[2] == T[a[1]].shape[1] else T[a[1]][:, a[2]:a[3]]
            Q[q].dma_start(ap(a[0]), src).then_inc(T.sem[o["sem"]], 16)
            mark[i] = (o["sem"], 16)
        elif fn == "store":
            Q[q].dma_start(T[a[0]][:, a[1]:a[2]], ap(a[3])).then_inc(T.sem[o["sem"]], 16)
            mark[i] = (o["sem"], 16)
        elif fn == "send":
            trs, got = [], 0
            for k, (src, dst, to) in enumerate(a[0]):
                e = topo.engines(core, T.cores[to])
                share = len(e) // len(a[0])
                m = sum(1 << x for x in e[k * share:(k + 1) * share])
                rid, pid, _se = topo.addr(T.cores[to])
                trs.append(RemoteDMATransfer(dst_ids=[DstId(rid=rid, pnc=pid)], dma_engine_mask=m, remote_sem=T.sem[a[1]],
                                             src=ap(src), dst=ap(dst)))
                got += share
            g.remote_dma_fused(trs, local_sem=T.sem.sent)
            sent[0] += got
            mark[i] = (a[1], got)
        else:
            if fn == "activation":
                kw = {}
                if a[3] is not None:
                    kw["bias"] = ap(a[3])
                if a[4] is not None:
                    kw["scale"] = ap(a[4])
                ins = g.scalar.activation(ap(a[0]), ap(a[1]), a[2], **kw)
            elif fn == "iota":
                if SCRATCH[a[0]["n"]][2] == i32:
                    ins = g.iota(ap(a[0]), a[1], a[2], a[3])
                else:
                    ins = g.iota(ap(a[0]), a[1], a[2], a[3], allow_small_or_imprecise_dtypes=True)
            elif fn == "matmul":
                for m in a:
                    ins = g.tensor.matmul(*[ap(x) for x in m])
            else:
                b = [ap(x) for x in a]
                ins = (g.affine_select(*b) if fn == "affine_select" else
                       g.vector.tensor_copy(*b) if fn == "tensor_copy" else g.vector.tensor_tensor(*b) if fn == "tensor_tensor" else
                       g.vector.tensor_scalar(*b) if fn == "tensor_scalar" else g.vector.memset(*b) if fn == "memset" else
                       g.vector.tensor_tensor_scan(*b) if fn == "tensor_tensor_scan" else g.vector.tensor_reduce(*b))
            count[q] += 1
            ins.then_inc(T.sem["q" + q], 1)
            mark[i] = ("q" + q, count[q])
        total[mark[i][0]] = max(total.get(mark[i][0], 0), mark[i][1])
    total["sent"] = sent[0]
    for nm in sorted(total):
        g.wait_ge(T.sem[nm], total[nm])
